import numpy as np
import ml_dtypes


def mxq(x, axis, fmt="e4m3"):
    dtype, down = {"e4m3": (ml_dtypes.float8_e4m3fn, 7), "e5m2": (ml_dtypes.float8_e5m2, 14)}[fmt]
    v = np.moveaxis(np.asarray(x, np.float32).astype(ml_dtypes.bfloat16).astype(np.float64), axis, -1)
    blocks = v.reshape(v.shape[:-1] + (-1, 32))
    amax = np.abs(blocks).max(-1, keepdims=True)
    byte = np.maximum(np.where(amax > 0, np.frexp(amax)[1] - 1 + 127, 0) - down, 1)
    scale = np.exp2(byte - 127.0)
    codes = (blocks / scale).astype(np.float32).astype(dtype).astype(np.float64)
    return np.moveaxis((codes * scale).reshape(v.shape), -1, axis)


WIDE = False


def mx_kscale(k):
    if not WIDE:
        return np.ones(k)
    levels = np.array([10, -10, 5, -5, 0])
    if k % 512:
        return np.exp2(np.random.permutation(np.resize(levels, k // 32))).repeat(32)
    a = np.empty((k // 512, 16))
    for p in range(k // 512):
        a[p, :8] = np.random.permutation(np.resize(levels, 8))
        for g in range(8):
            far = levels[np.abs(levels - a[p, g]) >= 10]
            a[p, g + 8] = far[np.random.randint(len(far))]
    return np.exp2(a.ravel()).repeat(32)


def f64(x):
    return np.asarray(x).astype(np.float64)


def striped(idx):
    return np.tile(idx.reshape(-1, 16).T, (8, 1)).astype(np.uint16)


def unstriped(offs):
    return offs[:16].T.reshape(-1).astype(np.int64)


E2M1 = np.array([0.0, 0.5, 1.0, 1.5, 2.0, 3.0, 4.0, 6.0, -0.0, -0.5, -1.0, -1.5, -2.0, -3.0, -4.0, -6.0])


def pack_weight(w, fmt):
    k, n = w.shape
    w = f64(np.asarray(w, np.float32).astype(ml_dtypes.bfloat16)).reshape(k // 32, 32, n)
    amax = np.abs(w).max(1)
    if fmt == "e4m3":
        byte = np.frexp(amax)[1] - 1 + 127 - 7
    else:
        mant, ex = np.frexp(amax / 6.0)
        byte = np.where(mant > 0.5, ex, ex - 1) + 127
    byte = np.clip(np.where(amax > 0, byte, 1), 1, 254)
    scaled = (w * np.exp2(127.0 - byte)[:, None, :]).reshape(k, n).astype(np.float32)
    by_word = np.ascontiguousarray(scaled.reshape(k // 512, 128, 4, n).transpose(0, 1, 3, 2))
    if fmt == "e4m3":
        words = by_word.astype(ml_dtypes.float8_e4m3fn).view(np.uint8)
    else:
        c = by_word.astype(ml_dtypes.float4_e2m1fn).view(np.uint8) & 0xF
        words = (c[..., 0::2] | (c[..., 1::2] << 4)).reshape(k // 512, 128, 2 * n)
    return np.ascontiguousarray(words), np.ascontiguousarray(byte.astype(np.uint8).reshape(k // 512, 16, n))


def unpack_weight(words, scales, fmt):
    g, _, n = scales.shape
    words = np.ascontiguousarray(words).reshape(g, 128, n, -1)
    if fmt == "e4m3":
        vals = words.view(ml_dtypes.float8_e4m3fn).astype(np.float64)
    else:
        nib = np.empty((g, 128, n, 4), np.uint8)
        nib[..., 0::2] = words & 0xF
        nib[..., 1::2] = words >> 4
        vals = E2M1[nib]
    vals = vals * np.repeat(np.exp2(scales.astype(np.float64) - 127.0), 8, axis=1)[..., None]
    return vals.transpose(0, 1, 3, 2).reshape(g * 512, n)


def gelu(v):
    return 0.5 * v * (1.0 + np.tanh(np.sqrt(2.0 / np.pi) * (v + 0.044715 * v**3)))


K, T, S, H, T2, N = 1024, 4096, 1024, 512, 2048, 384

def setup_inputs():
    n = np.random.standard_normal
    s = mx_kscale(K)[:, None]
    u = mx_kscale(H)[:, None]
    tab_words, tab_scales = pack_weight(n((K, T)) * s, "e4m3")
    w4_words, w4_scales = pack_weight(n((K, H)) / np.sqrt(K) / s * u.T, "e2m1")
    w1 = (n((K, H)) / np.sqrt(K) / s * u.T).astype(np.float32)
    wo = (n((H, N)) / np.sqrt(H) / u).astype(np.float32)
    rough = (np.random.uniform(0.3, 1.5, (H, T2)) * u * u).astype(np.float32)
    wg1 = np.exp(0.3 * n((128, S))).astype(np.float32)
    wg2 = np.exp(0.3 * n((128, S))).astype(np.float32)
    offs = striped(np.random.permutation(T)[:S])
    offs2 = striped(np.random.permutation(T2)[:S])
    offs3 = striped(np.random.permutation(T2)[:S])
    return {"tab_words": tab_words, "tab_scales": tab_scales, "w1": w1,
            "w4_words": w4_words, "w4_scales": w4_scales, "wo": wo, "rough": rough,
            "wg1": wg1, "wg2": wg2, "offs": offs, "offs2": offs2, "offs3": offs3}

def reference(tab_words, tab_scales, w1, w4_words, w4_scales, wo, rough, wg1, wg2, offs, offs2, offs3):
    v = unpack_weight(tab_words, tab_scales, "e4m3")[:, unstriped(offs)]
    w4 = unpack_weight(w4_words, w4_scales, "e2m1")
    h1 = np.square(mxq(f64(w1), 0, "e4m3").T @ v)
    h2 = np.square(w4.T @ v)
    pageA = np.zeros((H, T2))
    pageA[:, unstriped(offs2)] = np.tile(f64(wg1), (H // 128, 1)) * h1
    pageB = np.zeros((H, T2))
    pageB[:, unstriped(offs3)] = np.tile(f64(wg2), (H // 128, 1)) * h2
    z = np.sqrt(pageA + pageB + f64(rough))
    return mxq(f64(wo), 0, "e4m3").T @ mxq(z, 0, "e4m3")

@@ -1,0 +1,254 @@
+from contextlib import ExitStack
+
+import concourse.mybir as mybir
+from concourse.masks import make_identity
+
+K, T, S, H, T2, N = 1024, 4096, 1024, 512, 2048, 384
+FLOPS = 2 * (2 * K * H * S + H * N * T2)
+
+F32 = mybir.dt.float32
+BF16 = mybir.dt.bfloat16
+I32 = mybir.dt.int32
+U32 = mybir.dt.uint32
+U16 = mybir.dt.uint16
+U8 = mybir.dt.uint8
+FP8X4 = mybir.dt.float8_e4m3fn_x4
+FP4X4 = mybir.dt.float4_e2m1fn_x4
+ACT = mybir.ActivationFunctionType
+MULT = mybir.AluOpType.mult
+
+P = 128
+PACK = 4
+PASSES = K // (P * PACK)
+SLICES = H // P
+BANK = 512
+HALVES = S // BANK
+CHUNKS = T2 // BANK
+GROUPS = N // P
+COLS = BANK // 16
+
+
+def tile_list_inlet_speed_map_kernel(
+    tc, tab_words, tab_scales, w1, w4_words, w4_scales, wo, rough, wg1, wg2, offs, offs2, offs3, out
+):
+    nc = tc.nc
+    with ExitStack() as ctx:
+        keep = ctx.enter_context(tc.tile_pool(name="keep", bufs=1))
+        psum = ctx.enter_context(tc.psum_pool(name="psum", bufs=4))
+
+        idx = keep.tile([P, S // 16], U16, name="idx")
+        idx2 = keep.tile([P, S // 16], U16, name="idx2")
+        idx3 = keep.tile([P, S // 16], U16, name="idx3")
+        tscale = keep.tile([P, T], U8, name="tscale", align_bytes=64)
+        w4s = keep.tile([P, PASSES, H], U8, name="w4s", align_bytes=64)
+        nc.vector.memset(tscale[:].bitcast(I32), 0)
+        nc.vector.memset(w4s[:].rearrange("p a t -> p (a t)").bitcast(I32), 0)
+
+        nc.sync.dma_start(idx[:], offs)
+        twords = []
+        for a in range(PASSES):
+            tw = keep.tile([P, T], I32, name=f"twords{a}", tag=f"twords{a}", align_bytes=64)
+            nc.sync.dma_start(tw[:], tab_words[a].rearrange("p t i -> p (t i)").bitcast(I32))
+            twords.append(tw)
+            if a == 0:
+                for r in range(4):
+                    nc.sync.dma_start(
+                        tscale[r:P:16, :].bitcast(I32),
+                        tab_scales.bitcast(I32).rearrange("a (q r) t -> r q a t", r=4)[r],
+                    )
+        w4w = keep.tile([P, PASSES, 2 * H], U8, name="w4w", align_bytes=64)
+        nc.sync.dma_start(w4w[:].bitcast(I32), w4_words.bitcast(I32).rearrange("a p c -> p a c"))
+        for r in range(4):
+            nc.sync.dma_start(
+                w4s[r:P:32, :, :].bitcast(I32),
+                w4_scales.bitcast(I32).rearrange("a (q r) t -> r q a t", r=4)[r],
+            )
+        nc.sync.dma_start(idx3[:], offs3)
+        gain2 = keep.tile([P, S], F32, name="gain2")
+        nc.sync.dma_start(gain2[:], wg2)
+        w1raw = []
+        for a in range(PASSES):
+            wr = keep.tile([P, PACK, H], F32, name=f"w1raw{a}", tag=f"w1raw{a}", align_bytes=64)
+            nc.sync.dma_start(wr[:], w1[a * 512 : (a + 1) * 512, :].rearrange("(p j) c -> p j c", j=PACK))
+            w1raw.append(wr)
+        woraw = keep.tile([P, PACK, N], F32, name="woraw")
+        nc.sync.dma_start(woraw[:], wo.rearrange("(p j) n -> p j n", j=PACK))
+        nc.sync.dma_start(idx2[:], offs2)
+        gain1 = keep.tile([P, S], F32, name="gain1")
+        nc.sync.dma_start(gain1[:], wg1)
+        roughs = []
+        for t in range(SLICES):
+            rt = keep.tile([P, T2], F32, name=f"rough{t}")
+            nc.sync.dma_start(rt[:], rough[t * P : (t + 1) * P, :])
+            roughs.append(rt)
+
+        ident = keep.tile([P, P], F32, name="ident")
+        make_identity(nc, ident[:])
+        warm = keep.tile([P, 1], F32, name="warm")
+        nc.scalar.activation(warm[:], ident[:, 0:1], ACT.Sqrt)
+
+        pages_b = []
+        for b in range(2):
+            pg = keep.tile([P, T2], F32, name=f"pageb{b}")
+            nc.vector.memset(pg[:, : T2 // 2 - 1], 0.0)
+            nc.vector.memset(pg[:, T2 // 2 - 1 :], 0.0)
+            pages_b.append(pg)
+
+        gwords = []
+        gscale = [keep.tile([P, S], U8, name=f"gscale{a}", align_bytes=64) for a in range(PASSES)]
+        nc.vector.memset(gscale[1][:].bitcast(I32), 0)
+        nc.vector.tensor_copy(gscale[0][:], tscale[:].indirect(idx[:]))
+        nc.scalar.dma_start(gscale[1][0 : P - 16, :].bitcast(I32), gscale[0][16:P, :].bitcast(I32))
+        for a in range(PASSES):
+            gw = keep.tile([P, S], U32, name=f"gwords{a}", align_bytes=64)
+            window = twords[a][:].bitcast(U32)
+            if a < PASSES - 1:
+                nc.vector.tensor_copy(gw[:], window.indirect(idx[:]))
+            else:
+                for h in range(HALVES):
+                    nc.vector.tensor_copy(
+                        gw[:, h * BANK : (h + 1) * BANK], window.indirect(idx[:, h * COLS : (h + 1) * COLS])
+                    )
+            gwords.append(gw)
+
+        w1bf = keep.tile([P, SLICES, PASSES, P, PACK], BF16, name="w1bf", align_bytes=64)
+        w1c = keep.tile([P, SLICES, PASSES, P], U32, name="w1c", align_bytes=64)
+        w1s = keep.tile([P, SLICES, PASSES, P], U8, name="w1s", align_bytes=64)
+        wobf = keep.tile([P, N, PACK], BF16, name="wobf", align_bytes=64)
+        woc = keep.tile([P, N], U32, name="woc", align_bytes=64)
+        wos = keep.tile([P, N], U8, name="wos", align_bytes=64)
+
+        def prepare_w1():
+            for a in range(PASSES):
+                nc.scalar.copy(w1bf[:, :, a, :, :], w1raw[a][:].rearrange("p j (t c) -> p t c j", t=SLICES))
+            for lo, hi in ((0, 1), (1, 2), (2, 4)):
+                nc.vector.quantize_mx(
+                    out=w1c[:, lo:hi].rearrange("p t a c -> p (t a c)").bitcast(FP8X4),
+                    scales=w1s[:, lo:hi].rearrange("p t a c -> p (t a c)"),
+                    in_=w1bf[:, lo:hi].rearrange("p t a c j -> p (t a c j)"),
+                )
+
+        def prepare_wo():
+            nc.scalar.copy(wobf[:], woraw[:].rearrange("p j n -> p n j"))
+            for lo, hi in ((0, 256), (256, N)):
+                nc.vector.quantize_mx(
+                    out=woc[:, lo:hi].bitcast(FP8X4),
+                    scales=wos[:, lo:hi],
+                    in_=wobf[:, lo:hi, :].rearrange("p n j -> p (n j)"),
+                )
+
+        def produce(kind, t):
+            sq = keep.tile([P, S], F32, name="sq", tag="sq", bufs=2)
+            for h in range(HALVES):
+                cols = slice(h * BANK, (h + 1) * BANK)
+                acc = psum.tile([P, BANK], F32, name="acc", tag="acc")
+                for a in range(PASSES):
+                    if kind == "a":
+                        lhs, lhs_s = w1c[:, t, a, :].bitcast(FP8X4), w1s[:, t, a, :]
+                    else:
+                        lhs = w4w[:, a, 2 * P * t : 2 * P * (t + 1)].bitcast(FP4X4)
+                        lhs_s = w4s[:, a, P * t : P * (t + 1)]
+                    nc.tensor.matmul_mx(
+                        out=acc[:], lhsT=lhs, lhsT_scale=lhs_s,
+                        rhs=gwords[a][:, cols].bitcast(FP8X4), rhs_scale=gscale[a][:, cols],
+                        start=(a == 0), stop=(a == PASSES - 1),
+                    )
+                nc.scalar.activation(sq[:, cols], acc[:], ACT.Square)
+            return sq
+
+        def scatter(page, offsets, sq, gain, pieces):
+            width = S // pieces
+            for h in range(pieces):
+                cols = slice(h * width, (h + 1) * width)
+                nc.vector.tensor_tensor(
+                    page[:].indirect(offsets[:, h * width // 16 : (h + 1) * width // 16]),
+                    sq[:, cols], gain[:, cols], MULT,
+                )
+
+        def add_transposed(bank, c, src, first, last):
+            for mt in range(4):
+                nc.tensor.matmul(
+                    bank[:, mt * P : (mt + 1) * P], src[:, c * BANK + mt * P : c * BANK + (mt + 1) * P], ident[:],
+                    is_transpose=True, start=(first and mt == 0), stop=(last and mt == 3),
+                )
+
+        zts = [keep.tile([P, 2, 4, 2 * P], BF16, name=f"zt{c}", align_bytes=64) for c in range(CHUNKS)]
+
+        def open_sum(t, page):
+            banks = [psum.tile([P, BANK], F32, name="total", tag="total") for c in range(CHUNKS)]
+            for c in range(CHUNKS):
+                add_transposed(banks[c], c, roughs[t], True, False)
+            for c in range(CHUNKS):
+                add_transposed(banks[c], c, page, False, False)
+            return banks
+
+        def close_chunk(t, c, bank, page):
+            add_transposed(bank, c, page, False, True)
+            nc.scalar.activation(
+                zts[c][:, :, :, 64 * t : 64 * (t + 1)].rearrange("m u mt (p e) -> m u mt p e", e=2),
+                bank[:].rearrange("m (mt p u e) -> m u mt p e", mt=4, u=2, e=2),
+                ACT.Sqrt,
+            )
+
+        def finish_chunk(c):
+            zq = keep.tile([P, BANK * PACK], BF16, name=f"zq{c}", align_bytes=64)
+            words = zts[c][:].bitcast(F32)
+            for hh in range(2):
+                back = psum.tile([P, 2, 2 * P], F32, name="acc", tag="acc")
+                for u in range(2):
+                    for ml in range(2):
+                        nc.tensor.transpose(back[:, u, ml * P : (ml + 1) * P], words[:, u, 2 * hh + ml, :], ident[:])
+                dst = zq[:, hh * 1024 : (hh + 1) * 1024].bitcast(F32).rearrange("p (m u) -> p m u", u=2)
+                src = back[:].rearrange("p u m -> p m u")
+                if hh == 0:
+                    nc.vector.tensor_copy(dst, src)
+                else:
+                    nc.scalar.copy(dst, src)
+            zc = keep.tile([P, BANK], U32, name=f"zc{c}", align_bytes=64)
+            zs = keep.tile([P, BANK], U8, name=f"zs{c}", align_bytes=64)
+            nc.vector.quantize_mx(out=zc[:].bitcast(FP8X4), scales=zs[:], in_=zq[:])
+            for g in range(GROUPS):
+                res = psum.tile([P, BANK], F32, name="total", tag="total")
+                nc.tensor.matmul_mx(
+                    out=res[:], lhsT=woc[:, g * P : (g + 1) * P].bitcast(FP8X4), lhsT_scale=wos[:, g * P : (g + 1) * P],
+                    rhs=zc[:].bitcast(FP8X4), rhs_scale=zs[:], start=True, stop=True,
+                )
+                staged = keep.tile([P, BANK], F32, name=f"staged{c}_{g}")
+                if (c * GROUPS + g) % 2 == 0:
+                    nc.scalar.copy(staged[:], res[:])
+                else:
+                    nc.vector.tensor_copy(staged[:], res[:])
+                nc.sync.dma_start(out[g * P : (g + 1) * P, c * BANK : (c + 1) * BANK], staged[:])
+
+        sq_b0 = produce("b", 0)
+        sq_b1 = produce("b", 1)
+        scatter(pages_b[0], idx3, sq_b0, gain2, 2)
+        prepare_w1()
+        prepare_wo()
+        pages_a = []
+        for b, tag in enumerate(("twords1", "w1raw0")):
+            pg = keep.tile([P, T2], F32, name=f"pagea{b}", tag=tag, align_bytes=64)
+            nc.gpsimd.memset(pg[:], 0.0)
+            pages_a.append(pg)
+        scatter(pages_b[1], idx3, sq_b1, gain2, 1)
+        sq_a0 = produce("a", 0)
+        sq_a1 = produce("a", 1)
+        banks = open_sum(0, pages_b[0])
+        scatter(pages_a[0], idx2, sq_a0, gain1, 2)
+        sq_b = produce("b", 2)
+        for c in range(CHUNKS):
+            close_chunk(0, c, banks[c], pages_a[0])
+        banks = open_sum(1, pages_b[1])
+        scatter(pages_a[1], idx2, sq_a1, gain1, 1)
+        for t in range(2, SLICES):
+            sq_a = produce("a", t)
+            for c in range(CHUNKS):
+                close_chunk(t - 1, c, banks[c], pages_a[(t - 1) % 2])
+            scatter(pages_b[t % 2], idx3, sq_b, gain2, 1)
+            if t + 1 < SLICES:
+                sq_b = produce("b", t + 1)
+            banks = open_sum(t, pages_b[t % 2])
+            scatter(pages_a[t % 2], idx2, sq_a, gain1, 1)
+        for c in range(CHUNKS):
+            close_chunk(SLICES - 1, c, banks[c], pages_a[(SLICES - 1) % 2])
+            finish_chunk(c)

@@ -25,6 +25,7 @@ BANK = 512
 HALVES = S // BANK
 CHUNKS = T2 // BANK
 GROUPS = N // P
+LATE = 256
 COLS = BANK // 16
 
 
@@ -45,6 +46,13 @@ def tile_list_inlet_speed_map_kernel(
         nc.vector.memset(w4s[:].rearrange("p a t -> p (a t)").bitcast(I32), 0)
 
         nc.sync.dma_start(idx[:], offs)
+        nc.sync.dma_start(idx3[:], offs3)
+        nc.sync.dma_start(idx2[:], offs2)
+        for r in range(4):
+            nc.sync.dma_start(
+                tscale[r:P:16, :].bitcast(I32),
+                tab_scales.bitcast(I32).rearrange("a (q r) t -> r q a t", r=4)[r],
+            )
         twords = []
         for a in range(PASSES):
             tw = keep.tile([P, T], I32, name=f"twords{a}", tag=f"twords{a}", align_bytes=64)
@@ -53,17 +61,12 @@ def tile_list_inlet_speed_map_kernel(
             if a == 0:
                 for r in range(4):
                     nc.sync.dma_start(
-                        tscale[r:P:16, :].bitcast(I32),
-                        tab_scales.bitcast(I32).rearrange("a (q r) t -> r q a t", r=4)[r],
+                        w4s[r:P:32, :, :].bitcast(I32),
+                        w4_scales.bitcast(I32).rearrange("a (q r) t -> r q a t", r=4)[r],
                     )
-        w4w = keep.tile([P, PASSES, 2 * H], U8, name="w4w", align_bytes=64)
-        nc.sync.dma_start(w4w[:].bitcast(I32), w4_words.bitcast(I32).rearrange("a p c -> p a c"))
-        for r in range(4):
-            nc.sync.dma_start(
-                w4s[r:P:32, :, :].bitcast(I32),
-                w4_scales.bitcast(I32).rearrange("a (q r) t -> r q a t", r=4)[r],
-            )
-        nc.sync.dma_start(idx3[:], offs3)
+        w4_rows = w4_words.bitcast(I32).rearrange("a p (b c) -> b p a c", b=2)
+        w4w = [keep.tile([P, PASSES, H], U8, name=f"w4w{b}", tag=f"w4w{b}", align_bytes=64) for b in range(2)]
+        nc.sync.dma_start(w4w[0][:].bitcast(I32), w4_rows[0])
         gain2 = keep.tile([P, S], F32, name="gain2")
         nc.sync.dma_start(gain2[:], wg2)
         w1raw = []
@@ -71,28 +74,26 @@ def tile_list_inlet_speed_map_kernel(
             wr = keep.tile([P, PACK, H], F32, name=f"w1raw{a}", tag=f"w1raw{a}", align_bytes=64)
             nc.sync.dma_start(wr[:], w1[a * 512 : (a + 1) * 512, :].rearrange("(p j) c -> p j c", j=PACK))
             w1raw.append(wr)
+        roughs = [keep.tile([P, T2], F32, name=f"rough{t}") for t in range(SLICES)]
+        nc.sync.dma_start(roughs[0][:], rough[0:P, :])
         woraw = keep.tile([P, PACK, N], F32, name="woraw")
         nc.sync.dma_start(woraw[:], wo.rearrange("(p j) n -> p j n", j=PACK))
-        nc.sync.dma_start(idx2[:], offs2)
         gain1 = keep.tile([P, S], F32, name="gain1")
         nc.sync.dma_start(gain1[:], wg1)
-        roughs = []
-        for t in range(SLICES):
-            rt = keep.tile([P, T2], F32, name=f"rough{t}")
-            nc.sync.dma_start(rt[:], rough[t * P : (t + 1) * P, :])
-            roughs.append(rt)
+        nc.sync.dma_start(w4w[1][:].bitcast(I32), w4_rows[1])
+        for t in range(1, SLICES):
+            nc.sync.dma_start(roughs[t][:], rough[t * P : (t + 1) * P, :])
 
         ident = keep.tile([P, P], F32, name="ident")
         make_identity(nc, ident[:])
-        warm = keep.tile([P, 1], F32, name="warm")
-        nc.scalar.activation(warm[:], ident[:, 0:1], ACT.Sqrt)
 
         pages_b = []
         for b in range(2):
             pg = keep.tile([P, T2], F32, name=f"pageb{b}")
-            nc.vector.memset(pg[:, : T2 // 2 - 1], 0.0)
-            nc.vector.memset(pg[:, T2 // 2 - 1 :], 0.0)
+            nc.vector.memset(pg[:], 0.0)
             pages_b.append(pg)
+        warm = keep.tile([P, 1], F32, name="warm")
+        nc.scalar.activation(warm[:], pages_b[0][:, 0:1], ACT.Sqrt)
 
         gwords = []
         gscale = [keep.tile([P, S], U8, name=f"gscale{a}", align_bytes=64) for a in range(PASSES)]
@@ -111,14 +112,12 @@ def tile_list_inlet_speed_map_kernel(
                     )
             gwords.append(gw)
 
-        w1bf = keep.tile([P, SLICES, PASSES, P, PACK], BF16, name="w1bf", align_bytes=64)
         w1c = keep.tile([P, SLICES, PASSES, P], U32, name="w1c", align_bytes=64)
         w1s = keep.tile([P, SLICES, PASSES, P], U8, name="w1s", align_bytes=64)
         wobf = keep.tile([P, N, PACK], BF16, name="wobf", align_bytes=64)
-        woc = keep.tile([P, N], U32, name="woc", align_bytes=64)
-        wos = keep.tile([P, N], U8, name="wos", align_bytes=64)
 
         def prepare_w1():
+            w1bf = keep.tile([P, SLICES, PASSES, P, PACK], BF16, name="w1bf", tag="w4w0", align_bytes=64)
             for a in range(PASSES):
                 nc.scalar.copy(w1bf[:, :, a, :, :], w1raw[a][:].rearrange("p j (t c) -> p t c j", t=SLICES))
             for lo, hi in ((0, 1), (1, 2), (2, 4)):
@@ -130,6 +129,8 @@ def tile_list_inlet_speed_map_kernel(
 
         def prepare_wo():
             nc.scalar.copy(wobf[:], woraw[:].rearrange("p j n -> p n j"))
+
+        def quantize_wo(woc, wos):
             for lo, hi in ((0, 256), (256, N)):
                 nc.vector.quantize_mx(
                     out=woc[:, lo:hi].bitcast(FP8X4),
@@ -137,33 +138,44 @@ def tile_list_inlet_speed_map_kernel(
                     in_=wobf[:, lo:hi, :].rearrange("p n j -> p (n j)"),
                 )
 
-        def produce(kind, t):
-            sq = keep.tile([P, S], F32, name="sq", tag="sq", bufs=2)
+        def produce(kind, t, held=0):
+            sq = ring([P, S], F32)
             for h in range(HALVES):
+                acc = multiply(kind, t, h)
+                done = BANK - held if h == HALVES - 1 else BANK
+                nc.scalar.activation(sq[:, h * BANK : h * BANK + done], acc[:, :done], ACT.Square)
+            return (sq, acc) if held else sq
+
+        def ring(shape, dtype):
+            return keep.tile(shape, dtype, name="sq", tag="sq", bufs=2, align_bytes=64)
+
+        def multiply(kind, t, h, acc=None):
+            if True:
                 cols = slice(h * BANK, (h + 1) * BANK)
-                acc = psum.tile([P, BANK], F32, name="acc", tag="acc")
+                if acc is None:
+                    acc = psum.tile([P, BANK], F32, name="acc", tag="acc")
                 for a in range(PASSES):
                     if kind == "a":
                         lhs, lhs_s = w1c[:, t, a, :].bitcast(FP8X4), w1s[:, t, a, :]
                     else:
-                        lhs = w4w[:, a, 2 * P * t : 2 * P * (t + 1)].bitcast(FP4X4)
+                        lhs = w4w[t // 2][:, a, 2 * P * (t % 2) : 2 * P * (t % 2 + 1)].bitcast(FP4X4)
                         lhs_s = w4s[:, a, P * t : P * (t + 1)]
                     nc.tensor.matmul_mx(
                         out=acc[:], lhsT=lhs, lhsT_scale=lhs_s,
                         rhs=gwords[a][:, cols].bitcast(FP8X4), rhs_scale=gscale[a][:, cols],
                         start=(a == 0), stop=(a == PASSES - 1),
                     )
-                nc.scalar.activation(sq[:, cols], acc[:], ACT.Square)
-            return sq
+            return acc
+
+        def scatter_part(page, offsets, values, gain, lo, hi):
+            nc.vector.tensor_tensor(
+                page[:].indirect(offsets[:, lo // 16 : hi // 16]), values, gain[:, lo:hi], MULT
+            )
 
         def scatter(page, offsets, sq, gain, pieces):
             width = S // pieces
             for h in range(pieces):
-                cols = slice(h * width, (h + 1) * width)
-                nc.vector.tensor_tensor(
-                    page[:].indirect(offsets[:, h * width // 16 : (h + 1) * width // 16]),
-                    sq[:, cols], gain[:, cols], MULT,
-                )
+                scatter_part(page, offsets, sq[:, h * width : (h + 1) * width], gain, h * width, (h + 1) * width)
 
         def add_transposed(bank, c, src, first, last):
             for mt in range(4):
@@ -190,7 +202,7 @@ def tile_list_inlet_speed_map_kernel(
                 ACT.Sqrt,
             )
 
-        def finish_chunk(c):
+        def finish_chunk(c, woc, wos):
             zq = keep.tile([P, BANK * PACK], BF16, name=f"zq{c}", align_bytes=64)
             words = zts[c][:].bitcast(F32)
             for hh in range(2):
@@ -221,16 +233,19 @@ def tile_list_inlet_speed_map_kernel(
                 nc.sync.dma_start(out[g * P : (g + 1) * P, c * BANK : (c + 1) * BANK], staged[:])
 
         sq_b0 = produce("b", 0)
-        sq_b1 = produce("b", 1)
+        sq_b1, acc_b1 = produce("b", 1, LATE)
         scatter(pages_b[0], idx3, sq_b0, gain2, 2)
+        scatter_part(pages_b[1], idx3, sq_b1[:, : S - LATE], gain2, 0, S - LATE)
         prepare_w1()
+        sq_late = keep.tile([P, LATE], F32, name="sq_late", tag="w1raw1", align_bytes=64)
+        nc.scalar.activation(sq_late[:], acc_b1[:, BANK - LATE :], ACT.Square)
         prepare_wo()
         pages_a = []
         for b, tag in enumerate(("twords1", "w1raw0")):
             pg = keep.tile([P, T2], F32, name=f"pagea{b}", tag=tag, align_bytes=64)
             nc.gpsimd.memset(pg[:], 0.0)
             pages_a.append(pg)
-        scatter(pages_b[1], idx3, sq_b1, gain2, 1)
+        scatter_part(pages_b[1], idx3, sq_late[:], gain2, S - LATE, S)
         sq_a0 = produce("a", 0)
         sq_a1 = produce("a", 1)
         banks = open_sum(0, pages_b[0])
@@ -240,15 +255,30 @@ def tile_list_inlet_speed_map_kernel(
             close_chunk(0, c, banks[c], pages_a[0])
         banks = open_sum(1, pages_b[1])
         scatter(pages_a[1], idx2, sq_a1, gain1, 1)
-        for t in range(2, SLICES):
-            sq_a = produce("a", t)
-            for c in range(CHUNKS):
-                close_chunk(t - 1, c, banks[c], pages_a[(t - 1) % 2])
-            scatter(pages_b[t % 2], idx3, sq_b, gain2, 1)
-            if t + 1 < SLICES:
-                sq_b = produce("b", t + 1)
-            banks = open_sum(t, pages_b[t % 2])
-            scatter(pages_a[t % 2], idx2, sq_a, gain1, 1)
+        sq_a = produce("a", 2)
+        for c in range(CHUNKS):
+            close_chunk(1, c, banks[c], pages_a[1])
+        scatter(pages_b[0], idx3, sq_b, gain2, 1)
+        sq_b = produce("b", 3)
+        banks = open_sum(2, pages_b[0])
+        scatter(pages_a[0], idx2, sq_a, gain1, 1)
+        accs = [multiply("a", 3, h) for h in range(HALVES)]
+        first = ring([P, BANK], F32)
+        nc.scalar.activation(first[:], accs[0][:], ACT.Square)
+        for c in range(CHUNKS):
+            close_chunk(2, c, banks[c], pages_a[0])
+        scatter(pages_b[1], idx3, sq_b, gain2, 1)
+        second = ring([P, LATE], F32)
+        nc.scalar.activation(second[:], accs[1][:, :LATE], ACT.Square)
+        banks = open_sum(3, pages_b[1])
+        scatter_part(pages_a[1], idx2, first[:], gain1, 0, BANK)
+        third = ring([P, LATE], F32)
+        nc.scalar.activation(third[:], accs[1][:, LATE:], ACT.Square)
+        scatter_part(pages_a[1], idx2, second[:], gain1, BANK, BANK + LATE)
+        scatter_part(pages_a[1], idx2, third[:], gain1, BANK + LATE, S)
+        wos = ring([P, N], U8)
+        woc = ring([P, N], U32)
+        quantize_wo(woc, wos)
         for c in range(CHUNKS):
             close_chunk(SLICES - 1, c, banks[c], pages_a[(SLICES - 1) % 2])
-            finish_chunk(c)
+            finish_chunk(c, woc, wos)

@@ -19,14 +19,18 @@ MULT = mybir.AluOpType.mult
 
 P = 128
 PACK = 4
-PASSES = K // (P * PACK)
+K_PASS = P * PACK
+PASSES = K // K_PASS
 SLICES = H // P
 BANK = 512
 HALVES = S // BANK
 CHUNKS = T2 // BANK
+TILES = BANK // P
 GROUPS = N // P
-LATE = 256
-COLS = BANK // 16
+PER_COLUMN = 16
+QUADRANT = 32
+SCALE_ROWS = 4
+SECOND_PASS_ROW = 16
 
 
 def tile_list_inlet_speed_map_kernel(
@@ -34,251 +38,243 @@ def tile_list_inlet_speed_map_kernel(
 ):
     nc = tc.nc
     with ExitStack() as ctx:
-        keep = ctx.enter_context(tc.tile_pool(name="keep", bufs=1))
+        sbuf = ctx.enter_context(tc.tile_pool(name="sbuf", bufs=1))
         psum = ctx.enter_context(tc.psum_pool(name="psum", bufs=4))
 
-        idx = keep.tile([P, S // 16], U16, name="idx")
-        idx2 = keep.tile([P, S // 16], U16, name="idx2")
-        idx3 = keep.tile([P, S // 16], U16, name="idx3")
-        tscale = keep.tile([P, T], U8, name="tscale", align_bytes=64)
-        w4s = keep.tile([P, PASSES, H], U8, name="w4s", align_bytes=64)
-        nc.vector.memset(tscale[:].bitcast(I32), 0)
-        nc.vector.memset(w4s[:].rearrange("p a t -> p (a t)").bitcast(I32), 0)
+        idx = sbuf.tile([P, S // PER_COLUMN], U16, name="idx")
+        idx2 = sbuf.tile([P, S // PER_COLUMN], U16, name="idx2")
+        idx3 = sbuf.tile([P, S // PER_COLUMN], U16, name="idx3")
+        tab_scale = sbuf.tile([P, T], U8, name="tab_scale", align_bytes=64)
+        w4_scale = sbuf.tile([P, PASSES, H], U8, name="w4_scale", align_bytes=64)
+        nc.vector.memset(tab_scale[:].bitcast(I32), 0)
+        nc.vector.memset(w4_scale[:].rearrange("p a c -> p (a c)").bitcast(I32), 0)
 
         nc.sync.dma_start(idx[:], offs)
         nc.sync.dma_start(idx3[:], offs3)
         nc.sync.dma_start(idx2[:], offs2)
-        for r in range(4):
-            nc.sync.dma_start(
-                tscale[r:P:16, :].bitcast(I32),
-                tab_scales.bitcast(I32).rearrange("a (q r) t -> r q a t", r=4)[r],
-            )
-        twords = []
-        for a in range(PASSES):
-            tw = keep.tile([P, T], I32, name=f"twords{a}", tag=f"twords{a}", align_bytes=64)
-            nc.sync.dma_start(tw[:], tab_words[a].rearrange("p t i -> p (t i)").bitcast(I32))
-            twords.append(tw)
-            if a == 0:
-                for r in range(4):
-                    nc.sync.dma_start(
-                        w4s[r:P:32, :, :].bitcast(I32),
-                        w4_scales.bitcast(I32).rearrange("a (q r) t -> r q a t", r=4)[r],
-                    )
-        w4_rows = w4_words.bitcast(I32).rearrange("a p (b c) -> b p a c", b=2)
-        w4w = [keep.tile([P, PASSES, H], U8, name=f"w4w{b}", tag=f"w4w{b}", align_bytes=64) for b in range(2)]
-        nc.sync.dma_start(w4w[0][:].bitcast(I32), w4_rows[0])
-        gain2 = keep.tile([P, S], F32, name="gain2")
+        tab_scale_rows = tab_scales.bitcast(I32).rearrange("a (q j) t -> j q a t", j=SCALE_ROWS)
+        for j in range(SCALE_ROWS):
+            nc.sync.dma_start(tab_scale[j:P:SECOND_PASS_ROW, :].bitcast(I32), tab_scale_rows[j])
+
+        def load_table_words(a):
+            words = sbuf.tile([P, T], I32, name=f"tab_word{a}", tag=f"tab_word{a}", align_bytes=64)
+            nc.sync.dma_start(words[:], tab_words[a].rearrange("p t i -> p (t i)").bitcast(I32))
+            return words
+
+        w4_word_rows = w4_words.bitcast(I32).rearrange("a p (b c) -> b p a c", b=2)
+        w4_word = [
+            sbuf.tile([P, PASSES, H], U8, name=f"w4_word{b}", tag=f"w4_word{b}", align_bytes=64) for b in range(2)
+        ]
+        w4_scale_rows = w4_scales.bitcast(I32).rearrange("a (q j) c -> j q a c", j=SCALE_ROWS)
+        tab_word = [load_table_words(0)]
+        for j in range(SCALE_ROWS):
+            nc.sync.dma_start(w4_scale[j:P:QUADRANT, :, :].bitcast(I32), w4_scale_rows[j])
+        nc.sync.dma_start(w4_word[0][:].bitcast(I32), w4_word_rows[0])
+        tab_word.append(load_table_words(1))
+        gain2 = sbuf.tile([P, S], F32, name="gain2")
         nc.sync.dma_start(gain2[:], wg2)
-        w1raw = []
+        w1_raw = []
         for a in range(PASSES):
-            wr = keep.tile([P, PACK, H], F32, name=f"w1raw{a}", tag=f"w1raw{a}", align_bytes=64)
-            nc.sync.dma_start(wr[:], w1[a * 512 : (a + 1) * 512, :].rearrange("(p j) c -> p j c", j=PACK))
-            w1raw.append(wr)
-        roughs = [keep.tile([P, T2], F32, name=f"rough{t}") for t in range(SLICES)]
+            raw = sbuf.tile([P, PACK, H], F32, name=f"w1_raw{a}", tag=f"w1_raw{a}", align_bytes=64)
+            nc.sync.dma_start(raw[:], w1[a * K_PASS : (a + 1) * K_PASS, :].rearrange("(p i) c -> p i c", i=PACK))
+            w1_raw.append(raw)
+        roughs = [sbuf.tile([P, T2], F32, name=f"rough{t}") for t in range(SLICES)]
         nc.sync.dma_start(roughs[0][:], rough[0:P, :])
-        woraw = keep.tile([P, PACK, N], F32, name="woraw")
-        nc.sync.dma_start(woraw[:], wo.rearrange("(p j) n -> p j n", j=PACK))
-        gain1 = keep.tile([P, S], F32, name="gain1")
+        wo_raw = sbuf.tile([P, PACK, N], F32, name="wo_raw")
+        nc.sync.dma_start(wo_raw[:], wo.rearrange("(p i) n -> p i n", i=PACK))
+        gain1 = sbuf.tile([P, S], F32, name="gain1")
         nc.sync.dma_start(gain1[:], wg1)
-        nc.sync.dma_start(w4w[1][:].bitcast(I32), w4_rows[1])
+        nc.sync.dma_start(w4_word[1][:].bitcast(I32), w4_word_rows[1])
         for t in range(1, SLICES):
             nc.sync.dma_start(roughs[t][:], rough[t * P : (t + 1) * P, :])
 
-        ident = keep.tile([P, P], F32, name="ident")
+        ident = sbuf.tile([P, P], F32, name="ident")
         make_identity(nc, ident[:])
 
         pages_b = []
         for b in range(2):
-            pg = keep.tile([P, T2], F32, name=f"pageb{b}")
-            nc.vector.memset(pg[:], 0.0)
-            pages_b.append(pg)
-        warm = keep.tile([P, 1], F32, name="warm")
-        nc.scalar.activation(warm[:], pages_b[0][:, 0:1], ACT.Sqrt)
+            page = sbuf.tile([P, T2], F32, name=f"page_b{b}")
+            nc.vector.memset(page[:], 0.0)
+            pages_b.append(page)
 
-        gwords = []
-        gscale = [keep.tile([P, S], U8, name=f"gscale{a}", align_bytes=64) for a in range(PASSES)]
-        nc.vector.memset(gscale[1][:].bitcast(I32), 0)
-        nc.vector.tensor_copy(gscale[0][:], tscale[:].indirect(idx[:]))
-        nc.scalar.dma_start(gscale[1][0 : P - 16, :].bitcast(I32), gscale[0][16:P, :].bitcast(I32))
-        for a in range(PASSES):
-            gw = keep.tile([P, S], U32, name=f"gwords{a}", align_bytes=64)
-            window = twords[a][:].bitcast(U32)
-            if a < PASSES - 1:
-                nc.vector.tensor_copy(gw[:], window.indirect(idx[:]))
-            else:
-                for h in range(HALVES):
-                    nc.vector.tensor_copy(
-                        gw[:, h * BANK : (h + 1) * BANK], window.indirect(idx[:, h * COLS : (h + 1) * COLS])
-                    )
-            gwords.append(gw)
+        v_scale = [sbuf.tile([P, S], U8, name=f"v_scale{a}", align_bytes=64) for a in range(PASSES)]
+        nc.vector.memset(v_scale[1][:].bitcast(I32), 0)
+        nc.vector.tensor_copy(v_scale[0][:], tab_scale[:].indirect(idx[:]))
+        nc.scalar.dma_start(
+            v_scale[1][0 : P - SECOND_PASS_ROW, :].bitcast(I32), v_scale[0][SECOND_PASS_ROW:P, :].bitcast(I32)
+        )
+        v_word = [sbuf.tile([P, S], U32, name=f"v_word{a}", align_bytes=64) for a in range(PASSES)]
+        nc.vector.tensor_copy(v_word[0][:], tab_word[0][:].bitcast(U32).indirect(idx[:]))
+        for h in range(HALVES):
+            entries = idx[:, h * BANK // PER_COLUMN : (h + 1) * BANK // PER_COLUMN]
+            nc.vector.tensor_copy(v_word[1][:, h * BANK : (h + 1) * BANK], tab_word[1][:].bitcast(U32).indirect(entries))
 
-        w1c = keep.tile([P, SLICES, PASSES, P], U32, name="w1c", align_bytes=64)
-        w1s = keep.tile([P, SLICES, PASSES, P], U8, name="w1s", align_bytes=64)
-        wobf = keep.tile([P, N, PACK], BF16, name="wobf", align_bytes=64)
+        w1_word = sbuf.tile([P, SLICES, PASSES, P], U32, name="w1_word", align_bytes=64)
+        w1_scale = sbuf.tile([P, SLICES, PASSES, P], U8, name="w1_scale", align_bytes=64)
+        wo_bf16 = sbuf.tile([P, N, PACK], BF16, name="wo_bf16", align_bytes=64)
 
-        def prepare_w1():
-            w1bf = keep.tile([P, SLICES, PASSES, P, PACK], BF16, name="w1bf", tag="w4w0", align_bytes=64)
+        def quantise_w1():
+            w1_bf16 = sbuf.tile([P, SLICES, PASSES, P, PACK], BF16, name="w1_bf16", tag="w4_word0", align_bytes=64)
             for a in range(PASSES):
-                nc.scalar.copy(w1bf[:, :, a, :, :], w1raw[a][:].rearrange("p j (t c) -> p t c j", t=SLICES))
-            for lo, hi in ((0, 1), (1, 2), (2, 4)):
+                nc.scalar.copy(w1_bf16[:, :, a, :, :], w1_raw[a][:].rearrange("p i (t c) -> p t c i", t=SLICES))
+            for first, end in ((0, 1), (1, 2), (2, SLICES)):
                 nc.vector.quantize_mx(
-                    out=w1c[:, lo:hi].rearrange("p t a c -> p (t a c)").bitcast(FP8X4),
-                    scales=w1s[:, lo:hi].rearrange("p t a c -> p (t a c)"),
-                    in_=w1bf[:, lo:hi].rearrange("p t a c j -> p (t a c j)"),
+                    out=w1_word[:, first:end].rearrange("p t a c -> p (t a c)").bitcast(FP8X4),
+                    scales=w1_scale[:, first:end].rearrange("p t a c -> p (t a c)"),
+                    in_=w1_bf16[:, first:end].rearrange("p t a c i -> p (t a c i)"),
                 )
-
-        def prepare_wo():
-            nc.scalar.copy(wobf[:], woraw[:].rearrange("p j n -> p n j"))
-
-        def quantize_wo(woc, wos):
-            for lo, hi in ((0, 256), (256, N)):
-                nc.vector.quantize_mx(
-                    out=woc[:, lo:hi].bitcast(FP8X4),
-                    scales=wos[:, lo:hi],
-                    in_=wobf[:, lo:hi, :].rearrange("p n j -> p (n j)"),
-                )
-
-        def produce(kind, t, held=0):
-            sq = ring([P, S], F32)
-            for h in range(HALVES):
-                acc = multiply(kind, t, h)
-                done = BANK - held if h == HALVES - 1 else BANK
-                nc.scalar.activation(sq[:, h * BANK : h * BANK + done], acc[:, :done], ACT.Square)
-            return (sq, acc) if held else sq
 
         def ring(shape, dtype):
-            return keep.tile(shape, dtype, name="sq", tag="sq", bufs=2, align_bytes=64)
+            return sbuf.tile(shape, dtype, name="ring", tag="ring", bufs=2, align_bytes=64)
 
-        def multiply(kind, t, h, acc=None):
-            if True:
-                cols = slice(h * BANK, (h + 1) * BANK)
-                if acc is None:
-                    acc = psum.tile([P, BANK], F32, name="acc", tag="acc")
-                for a in range(PASSES):
-                    if kind == "a":
-                        lhs, lhs_s = w1c[:, t, a, :].bitcast(FP8X4), w1s[:, t, a, :]
-                    else:
-                        lhs = w4w[t // 2][:, a, 2 * P * (t % 2) : 2 * P * (t % 2 + 1)].bitcast(FP4X4)
-                        lhs_s = w4s[:, a, P * t : P * (t + 1)]
-                    nc.tensor.matmul_mx(
-                        out=acc[:], lhsT=lhs, lhsT_scale=lhs_s,
-                        rhs=gwords[a][:, cols].bitcast(FP8X4), rhs_scale=gscale[a][:, cols],
-                        start=(a == 0), stop=(a == PASSES - 1),
-                    )
+        def multiply(weight, t, h):
+            cols = slice(h * BANK, (h + 1) * BANK)
+            acc = psum.tile([P, BANK], F32, name="acc", tag="acc")
+            for a in range(PASSES):
+                if weight == "w1":
+                    codes, scales = w1_word[:, t, a, :].bitcast(FP8X4), w1_scale[:, t, a, :]
+                else:
+                    codes = w4_word[t // 2][:, a, 2 * P * (t % 2) : 2 * P * (t % 2 + 1)].bitcast(FP4X4)
+                    scales = w4_scale[:, a, P * t : P * (t + 1)]
+                nc.tensor.matmul_mx(
+                    out=acc[:],
+                    lhsT=codes,
+                    lhsT_scale=scales,
+                    rhs=v_word[a][:, cols].bitcast(FP8X4),
+                    rhs_scale=v_scale[a][:, cols],
+                    start=(a == 0),
+                    stop=(a == PASSES - 1),
+                )
             return acc
 
-        def scatter_part(page, offsets, values, gain, lo, hi):
-            nc.vector.tensor_tensor(
-                page[:].indirect(offsets[:, lo // 16 : hi // 16]), values, gain[:, lo:hi], MULT
-            )
+        def squares(weight, t):
+            values = ring([P, S], F32)
+            for h in range(HALVES):
+                acc = multiply(weight, t, h)
+                nc.scalar.activation(values[:, h * BANK : (h + 1) * BANK], acc[:], ACT.Square)
+            return values
 
-        def scatter(page, offsets, sq, gain, pieces):
-            width = S // pieces
-            for h in range(pieces):
-                scatter_part(page, offsets, sq[:, h * width : (h + 1) * width], gain, h * width, (h + 1) * width)
+        def scatter(page, offsets, values, gain, first, end):
+            entries = offsets[:, first // PER_COLUMN : end // PER_COLUMN]
+            nc.vector.tensor_tensor(page[:].indirect(entries), values, gain[:, first:end], MULT)
 
-        def add_transposed(bank, c, src, first, last):
-            for mt in range(4):
+        def add_transposed(bank, c, rows, opens, closes):
+            for mt in range(TILES):
                 nc.tensor.matmul(
-                    bank[:, mt * P : (mt + 1) * P], src[:, c * BANK + mt * P : c * BANK + (mt + 1) * P], ident[:],
-                    is_transpose=True, start=(first and mt == 0), stop=(last and mt == 3),
+                    bank[:, mt * P : (mt + 1) * P],
+                    rows[:, c * BANK + mt * P : c * BANK + (mt + 1) * P],
+                    ident[:],
+                    is_transpose=True,
+                    start=(opens and mt == 0),
+                    stop=(closes and mt == TILES - 1),
                 )
 
-        zts = [keep.tile([P, 2, 4, 2 * P], BF16, name=f"zt{c}", align_bytes=64) for c in range(CHUNKS)]
-
-        def open_sum(t, page):
+        def open_sum(t, page_b):
             banks = [psum.tile([P, BANK], F32, name="total", tag="total") for c in range(CHUNKS)]
             for c in range(CHUNKS):
                 add_transposed(banks[c], c, roughs[t], True, False)
             for c in range(CHUNKS):
-                add_transposed(banks[c], c, page, False, False)
+                add_transposed(banks[c], c, page_b, False, False)
             return banks
 
-        def close_chunk(t, c, bank, page):
-            add_transposed(bank, c, page, False, True)
+        z_t = [sbuf.tile([P, 2, TILES, 2 * P], BF16, name=f"z_t{c}", align_bytes=64) for c in range(CHUNKS)]
+        span = 2 * P // SLICES
+
+        def close_sum(t, c, bank, page_a):
+            add_transposed(bank, c, page_a, False, True)
             nc.scalar.activation(
-                zts[c][:, :, :, 64 * t : 64 * (t + 1)].rearrange("m u mt (p e) -> m u mt p e", e=2),
-                bank[:].rearrange("m (mt p u e) -> m u mt p e", mt=4, u=2, e=2),
+                z_t[c][:, :, :, span * t : span * (t + 1)].rearrange("m u mt (p e) -> m u mt p e", e=2),
+                bank[:].rearrange("m (mt p u e) -> m u mt p e", mt=TILES, u=2, e=2),
                 ACT.Sqrt,
             )
 
-        def finish_chunk(c, woc, wos):
-            zq = keep.tile([P, BANK * PACK], BF16, name=f"zq{c}", align_bytes=64)
-            words = zts[c][:].bitcast(F32)
-            for hh in range(2):
+        def finish_chunk(c, wo_word, wo_scale):
+            z_bf16 = sbuf.tile([P, BANK * PACK], BF16, name=f"z_bf16_{c}", align_bytes=64)
+            pairs = z_t[c][:].bitcast(F32)
+            for b in range(2):
                 back = psum.tile([P, 2, 2 * P], F32, name="acc", tag="acc")
                 for u in range(2):
-                    for ml in range(2):
-                        nc.tensor.transpose(back[:, u, ml * P : (ml + 1) * P], words[:, u, 2 * hh + ml, :], ident[:])
-                dst = zq[:, hh * 1024 : (hh + 1) * 1024].bitcast(F32).rearrange("p (m u) -> p m u", u=2)
-                src = back[:].rearrange("p u m -> p m u")
-                if hh == 0:
-                    nc.vector.tensor_copy(dst, src)
+                    for j in range(2):
+                        nc.tensor.transpose(back[:, u, j * P : (j + 1) * P], pairs[:, u, 2 * b + j, :], ident[:])
+                cells = z_bf16[:, b * 2 * BANK : (b + 1) * 2 * BANK].bitcast(F32).rearrange("p (m u) -> p m u", u=2)
+                if b == 0:
+                    nc.vector.tensor_copy(cells, back[:].rearrange("p u m -> p m u"))
                 else:
-                    nc.scalar.copy(dst, src)
-            zc = keep.tile([P, BANK], U32, name=f"zc{c}", align_bytes=64)
-            zs = keep.tile([P, BANK], U8, name=f"zs{c}", align_bytes=64)
-            nc.vector.quantize_mx(out=zc[:].bitcast(FP8X4), scales=zs[:], in_=zq[:])
+                    nc.scalar.copy(cells, back[:].rearrange("p u m -> p m u"))
+            z_word = sbuf.tile([P, BANK], U32, name=f"z_word{c}", align_bytes=64)
+            z_scale = sbuf.tile([P, BANK], U8, name=f"z_scale{c}", align_bytes=64)
+            nc.vector.quantize_mx(out=z_word[:].bitcast(FP8X4), scales=z_scale[:], in_=z_bf16[:])
             for g in range(GROUPS):
-                res = psum.tile([P, BANK], F32, name="total", tag="total")
+                rows = slice(g * P, (g + 1) * P)
+                result = psum.tile([P, BANK], F32, name="total", tag="total")
                 nc.tensor.matmul_mx(
-                    out=res[:], lhsT=woc[:, g * P : (g + 1) * P].bitcast(FP8X4), lhsT_scale=wos[:, g * P : (g + 1) * P],
-                    rhs=zc[:].bitcast(FP8X4), rhs_scale=zs[:], start=True, stop=True,
+                    out=result[:],
+                    lhsT=wo_word[:, rows].bitcast(FP8X4),
+                    lhsT_scale=wo_scale[:, rows],
+                    rhs=z_word[:].bitcast(FP8X4),
+                    rhs_scale=z_scale[:],
+                    start=True,
+                    stop=True,
                 )
-                staged = keep.tile([P, BANK], F32, name=f"staged{c}_{g}")
+                staged = sbuf.tile([P, BANK], F32, name=f"staged{c}_{g}")
                 if (c * GROUPS + g) % 2 == 0:
-                    nc.scalar.copy(staged[:], res[:])
+                    nc.scalar.copy(staged[:], result[:])
                 else:
-                    nc.vector.tensor_copy(staged[:], res[:])
-                nc.sync.dma_start(out[g * P : (g + 1) * P, c * BANK : (c + 1) * BANK], staged[:])
+                    nc.vector.tensor_copy(staged[:], result[:])
+                nc.sync.dma_start(out[rows, c * BANK : (c + 1) * BANK], staged[:])
 
-        sq_b0 = produce("b", 0)
-        sq_b1, acc_b1 = produce("b", 1, LATE)
-        scatter(pages_b[0], idx3, sq_b0, gain2, 2)
-        scatter_part(pages_b[1], idx3, sq_b1[:, : S - LATE], gain2, 0, S - LATE)
-        prepare_w1()
-        sq_late = keep.tile([P, LATE], F32, name="sq_late", tag="w1raw1", align_bytes=64)
-        nc.scalar.activation(sq_late[:], acc_b1[:, BANK - LATE :], ACT.Square)
-        prepare_wo()
+        h2_0 = ring([P, S], F32)
+        h2_1_first = ring([P, BANK], F32)
+        nc.scalar.activation(h2_0[:, :BANK], multiply("w4", 0, 0)[:], ACT.Square)
+        nc.scalar.activation(h2_1_first[:], multiply("w4", 1, 0)[:], ACT.Square)
+        nc.scalar.activation(h2_0[:, BANK:], multiply("w4", 0, 1)[:], ACT.Square)
+        acc_1_second = multiply("w4", 1, 1)
+        scatter(pages_b[0], idx3, h2_0[:, :BANK], gain2, 0, BANK)
+        scatter(pages_b[1], idx3, h2_1_first[:], gain2, 0, BANK)
+        scatter(pages_b[0], idx3, h2_0[:, BANK:], gain2, BANK, S)
+        quantise_w1()
+        h2_1_second = sbuf.tile([P, BANK], F32, name="h2_1_second", tag="w1_raw1", align_bytes=64)
+        nc.scalar.activation(h2_1_second[:], acc_1_second[:], ACT.Square)
+        nc.scalar.copy(wo_bf16[:], wo_raw[:].rearrange("p i n -> p n i"))
         pages_a = []
-        for b, tag in enumerate(("twords1", "w1raw0")):
-            pg = keep.tile([P, T2], F32, name=f"pagea{b}", tag=tag, align_bytes=64)
-            nc.gpsimd.memset(pg[:], 0.0)
-            pages_a.append(pg)
-        scatter_part(pages_b[1], idx3, sq_late[:], gain2, S - LATE, S)
-        sq_a0 = produce("a", 0)
-        sq_a1 = produce("a", 1)
+        for b, spent in enumerate(("tab_word1", "w1_raw0")):
+            page = sbuf.tile([P, T2], F32, name=f"page_a{b}", tag=spent, align_bytes=64)
+            nc.gpsimd.memset(page[:], 0.0)
+            pages_a.append(page)
+        scatter(pages_b[1], idx3, h2_1_second[:], gain2, BANK, S)
+
+        h1_01 = [ring([P, S], F32), ring([P, S], F32)]
+        for h in range(HALVES):
+            for t in range(2):
+                nc.scalar.activation(h1_01[t][:, h * BANK : (h + 1) * BANK], multiply("w1", t, h)[:], ACT.Square)
         banks = open_sum(0, pages_b[0])
-        scatter(pages_a[0], idx2, sq_a0, gain1, 2)
-        sq_b = produce("b", 2)
+        scatter(pages_a[0], idx2, h1_01[0][:, :BANK], gain1, 0, BANK)
+        scatter(pages_a[1], idx2, h1_01[1][:, :BANK], gain1, 0, BANK)
+        scatter(pages_a[0], idx2, h1_01[0][:, BANK:], gain1, BANK, S)
+        h2 = squares("w4", 2)
         for c in range(CHUNKS):
-            close_chunk(0, c, banks[c], pages_a[0])
+            close_sum(0, c, banks[c], pages_a[0])
         banks = open_sum(1, pages_b[1])
-        scatter(pages_a[1], idx2, sq_a1, gain1, 1)
-        sq_a = produce("a", 2)
+        scatter(pages_a[1], idx2, h1_01[1][:, BANK:], gain1, BANK, S)
+
+        for t in range(2, SLICES):
+            h1 = squares("w1", t)
+            for c in range(CHUNKS):
+                close_sum(t - 1, c, banks[c], pages_a[(t - 1) % 2])
+            scatter(pages_b[t % 2], idx3, h2[:], gain2, 0, S)
+            if t + 1 < SLICES:
+                h2 = squares("w4", t + 1)
+            banks = open_sum(t, pages_b[t % 2])
+            scatter(pages_a[t % 2], idx2, h1[:], gain1, 0, S)
+
+        wo_scale = ring([P, N], U8)
+        wo_word = ring([P, N], U32)
+        for first, end in ((0, 2 * P), (2 * P, N)):
+            nc.vector.quantize_mx(
+                out=wo_word[:, first:end].bitcast(FP8X4),
+                scales=wo_scale[:, first:end],
+                in_=wo_bf16[:, first:end, :].rearrange("p n i -> p (n i)"),
+            )
         for c in range(CHUNKS):
-            close_chunk(1, c, banks[c], pages_a[1])
-        scatter(pages_b[0], idx3, sq_b, gain2, 1)
-        sq_b = produce("b", 3)
-        banks = open_sum(2, pages_b[0])
-        scatter(pages_a[0], idx2, sq_a, gain1, 1)
-        accs = [multiply("a", 3, h) for h in range(HALVES)]
-        first = ring([P, BANK], F32)
-        nc.scalar.activation(first[:], accs[0][:], ACT.Square)
-        for c in range(CHUNKS):
-            close_chunk(2, c, banks[c], pages_a[0])
-        scatter(pages_b[1], idx3, sq_b, gain2, 1)
-        second = ring([P, LATE], F32)
-        nc.scalar.activation(second[:], accs[1][:, :LATE], ACT.Square)
-        banks = open_sum(3, pages_b[1])
-        scatter_part(pages_a[1], idx2, first[:], gain1, 0, BANK)
-        third = ring([P, LATE], F32)
-        nc.scalar.activation(third[:], accs[1][:, LATE:], ACT.Square)
-        scatter_part(pages_a[1], idx2, second[:], gain1, BANK, BANK + LATE)
-        scatter_part(pages_a[1], idx2, third[:], gain1, BANK + LATE, S)
-        wos = ring([P, N], U8)
-        woc = ring([P, N], U32)
-        quantize_wo(woc, wos)
-        for c in range(CHUNKS):
-            close_chunk(SLICES - 1, c, banks[c], pages_a[(SLICES - 1) % 2])
-            finish_chunk(c, woc, wos)
+            close_sum(SLICES - 1, c, banks[c], pages_a[(SLICES - 1) % 2])
+            finish_chunk(c, wo_word, wo_scale)

@@ -30,6 +30,7 @@ GROUPS = N // P
 PER_COLUMN = 16
 QUADRANT = 32
 SCALE_ROWS = 4
+TABLE_HEAD = 1024
 SECOND_PASS_ROW = 16
 
 
@@ -49,28 +50,30 @@ def tile_list_inlet_speed_map_kernel(
         nc.vector.memset(tab_scale[:].bitcast(I32), 0)
         nc.vector.memset(w4_scale[:].rearrange("p a c -> p (a c)").bitcast(I32), 0)
 
-        nc.sync.dma_start(idx[:], offs)
-        nc.sync.dma_start(idx3[:], offs3)
-        nc.sync.dma_start(idx2[:], offs2)
-        tab_scale_rows = tab_scales.bitcast(I32).rearrange("a (q j) t -> j q a t", j=SCALE_ROWS)
-        for j in range(SCALE_ROWS):
-            nc.sync.dma_start(tab_scale[j:P:SECOND_PASS_ROW, :].bitcast(I32), tab_scale_rows[j])
+        tab_word = [sbuf.tile([P, T], I32, name=f"tab_word{a}", tag=f"tab_word{a}", align_bytes=64) for a in range(PASSES)]
 
-        def load_table_words(a):
-            words = sbuf.tile([P, T], I32, name=f"tab_word{a}", tag=f"tab_word{a}", align_bytes=64)
-            nc.sync.dma_start(words[:], tab_words[a].rearrange("p t i -> p (t i)").bitcast(I32))
-            return words
+        def load_table_words(a, first, end):
+            words = tab_words[a].rearrange("p t i -> p (t i)").bitcast(I32)
+            nc.sync.dma_start(tab_word[a][:, first:end], words[:, first:end])
 
         w4_word_rows = w4_words.bitcast(I32).rearrange("a p (b c) -> b p a c", b=2)
         w4_word = [
             sbuf.tile([P, PASSES, H], U8, name=f"w4_word{b}", tag=f"w4_word{b}", align_bytes=64) for b in range(2)
         ]
         w4_scale_rows = w4_scales.bitcast(I32).rearrange("a (q j) c -> j q a c", j=SCALE_ROWS)
-        tab_word = [load_table_words(0)]
+        tab_scale_rows = tab_scales.bitcast(I32).rearrange("a (q j) t -> j q a t", j=SCALE_ROWS)
+
+        nc.sync.dma_start(idx[:], offs)
+        load_table_words(0, 0, TABLE_HEAD)
+        nc.sync.dma_start(w4_word[0][:].bitcast(I32), w4_word_rows[0])
+        for j in range(SCALE_ROWS):
+            nc.sync.dma_start(tab_scale[j:P:SECOND_PASS_ROW, :].bitcast(I32), tab_scale_rows[j])
+        load_table_words(0, TABLE_HEAD, T)
+        load_table_words(1, 0, T // 2)
         for j in range(SCALE_ROWS):
             nc.sync.dma_start(w4_scale[j:P:QUADRANT, :, :].bitcast(I32), w4_scale_rows[j])
-        nc.sync.dma_start(w4_word[0][:].bitcast(I32), w4_word_rows[0])
-        tab_word.append(load_table_words(1))
+        nc.sync.dma_start(idx3[:], offs3)
+        load_table_words(1, T // 2, T)
         gain2 = sbuf.tile([P, S], F32, name="gain2")
         nc.sync.dma_start(gain2[:], wg2)
         w1_raw = []
@@ -78,13 +81,14 @@ def tile_list_inlet_speed_map_kernel(
             raw = sbuf.tile([P, PACK, H], F32, name=f"w1_raw{a}", tag=f"w1_raw{a}", align_bytes=64)
             nc.sync.dma_start(raw[:], w1[a * K_PASS : (a + 1) * K_PASS, :].rearrange("(p i) c -> p i c", i=PACK))
             w1_raw.append(raw)
+        nc.sync.dma_start(w4_word[1][:].bitcast(I32), w4_word_rows[1])
         roughs = [sbuf.tile([P, T2], F32, name=f"rough{t}") for t in range(SLICES)]
         nc.sync.dma_start(roughs[0][:], rough[0:P, :])
-        wo_raw = sbuf.tile([P, PACK, N], F32, name="wo_raw")
-        nc.sync.dma_start(wo_raw[:], wo.rearrange("(p i) n -> p i n", i=PACK))
         gain1 = sbuf.tile([P, S], F32, name="gain1")
         nc.sync.dma_start(gain1[:], wg1)
-        nc.sync.dma_start(w4_word[1][:].bitcast(I32), w4_word_rows[1])
+        nc.sync.dma_start(idx2[:], offs2)
+        wo_raw = sbuf.tile([P, PACK, N], F32, name="wo_raw")
+        nc.sync.dma_start(wo_raw[:], wo.rearrange("(p i) n -> p i n", i=PACK))
         for t in range(1, SLICES):
             nc.sync.dma_start(roughs[t][:], rough[t * P : (t + 1) * P, :])
 
@@ -103,29 +107,27 @@ def tile_list_inlet_speed_map_kernel(
         nc.scalar.dma_start(
             v_scale[1][0 : P - SECOND_PASS_ROW, :].bitcast(I32), v_scale[0][SECOND_PASS_ROW:P, :].bitcast(I32)
         )
-        v_word = [sbuf.tile([P, S], U32, name=f"v_word{a}", align_bytes=64) for a in range(PASSES)]
+        v_word = [sbuf.tile([P, S], U32, name=f"v_word{a}", tag=f"v_word{a}", align_bytes=64) for a in range(PASSES)]
         nc.vector.tensor_copy(v_word[0][:], tab_word[0][:].bitcast(U32).indirect(idx[:]))
         for h in range(HALVES):
             entries = idx[:, h * BANK // PER_COLUMN : (h + 1) * BANK // PER_COLUMN]
             nc.vector.tensor_copy(v_word[1][:, h * BANK : (h + 1) * BANK], tab_word[1][:].bitcast(U32).indirect(entries))
 
-        w1_word = sbuf.tile([P, SLICES, PASSES, P], U32, name="w1_word", align_bytes=64)
         w1_scale = sbuf.tile([P, SLICES, PASSES, P], U8, name="w1_scale", align_bytes=64)
-        wo_bf16 = sbuf.tile([P, N, PACK], BF16, name="wo_bf16", align_bytes=64)
 
-        def quantise_w1():
+        def round_w1():
             w1_bf16 = sbuf.tile([P, SLICES, PASSES, P, PACK], BF16, name="w1_bf16", tag="w4_word0", align_bytes=64)
             for a in range(PASSES):
                 nc.scalar.copy(w1_bf16[:, :, a, :, :], w1_raw[a][:].rearrange("p i (t c) -> p t c i", t=SLICES))
-            for first, end in ((0, 1), (1, 2), (2, SLICES)):
+            return w1_bf16
+
+        def quantise_w1(w1_bf16):
+            for first, end in ((2, SLICES), (0, 2)):
                 nc.vector.quantize_mx(
                     out=w1_word[:, first:end].rearrange("p t a c -> p (t a c)").bitcast(FP8X4),
                     scales=w1_scale[:, first:end].rearrange("p t a c -> p (t a c)"),
                     in_=w1_bf16[:, first:end].rearrange("p t a c i -> p (t a c i)"),
                 )
-
-        def ring(shape, dtype):
-            return sbuf.tile(shape, dtype, name="ring", tag="ring", bufs=2, align_bytes=64)
 
         def multiply(weight, t, h):
             cols = slice(h * BANK, (h + 1) * BANK)
@@ -147,12 +149,8 @@ def tile_list_inlet_speed_map_kernel(
                 )
             return acc
 
-        def squares(weight, t):
-            values = ring([P, S], F32)
-            for h in range(HALVES):
-                acc = multiply(weight, t, h)
-                nc.scalar.activation(values[:, h * BANK : (h + 1) * BANK], acc[:], ACT.Square)
-            return values
+        def square(values, weight, t, h):
+            nc.scalar.activation(values[:, h * BANK : (h + 1) * BANK], multiply(weight, t, h)[:], ACT.Square)
 
         def scatter(page, offsets, values, gain, first, end):
             entries = offsets[:, first // PER_COLUMN : end // PER_COLUMN]
@@ -170,11 +168,12 @@ def tile_list_inlet_speed_map_kernel(
                 )
 
         def open_sum(t, page_b):
-            banks = [psum.tile([P, BANK], F32, name="total", tag="total") for c in range(CHUNKS)]
+            tag = "total" if t % 2 == 0 else "acc"
+            banks = [psum.tile([P, BANK], F32, name=tag, tag=tag) for c in range(CHUNKS)]
             for c in range(CHUNKS):
-                add_transposed(banks[c], c, roughs[t], True, False)
+                add_transposed(banks[c], c, page_b, True, False)
             for c in range(CHUNKS):
-                add_transposed(banks[c], c, page_b, False, False)
+                add_transposed(banks[c], c, roughs[t], False, False)
             return banks
 
         z_t = [sbuf.tile([P, 2, TILES, 2 * P], BF16, name=f"z_t{c}", align_bytes=64) for c in range(CHUNKS)]
@@ -192,7 +191,7 @@ def tile_list_inlet_speed_map_kernel(
             z_bf16 = sbuf.tile([P, BANK * PACK], BF16, name=f"z_bf16_{c}", align_bytes=64)
             pairs = z_t[c][:].bitcast(F32)
             for b in range(2):
-                back = psum.tile([P, 2, 2 * P], F32, name="acc", tag="acc")
+                back = psum.tile([P, 2, 2 * P], F32, name="total", tag="total")
                 for u in range(2):
                     for j in range(2):
                         nc.tensor.transpose(back[:, u, j * P : (j + 1) * P], pairs[:, u, 2 * b + j, :], ident[:])
@@ -206,7 +205,7 @@ def tile_list_inlet_speed_map_kernel(
             nc.vector.quantize_mx(out=z_word[:].bitcast(FP8X4), scales=z_scale[:], in_=z_bf16[:])
             for g in range(GROUPS):
                 rows = slice(g * P, (g + 1) * P)
-                result = psum.tile([P, BANK], F32, name="total", tag="total")
+                result = psum.tile([P, BANK], F32, name="acc", tag="acc")
                 nc.tensor.matmul_mx(
                     out=result[:],
                     lhsT=wo_word[:, rows].bitcast(FP8X4),
@@ -223,52 +222,52 @@ def tile_list_inlet_speed_map_kernel(
                     nc.vector.tensor_copy(staged[:], result[:])
                 nc.sync.dma_start(out[rows, c * BANK : (c + 1) * BANK], staged[:])
 
-        h2_0 = ring([P, S], F32)
-        h2_1_first = ring([P, BANK], F32)
-        nc.scalar.activation(h2_0[:, :BANK], multiply("w4", 0, 0)[:], ACT.Square)
-        nc.scalar.activation(h2_1_first[:], multiply("w4", 1, 0)[:], ACT.Square)
-        nc.scalar.activation(h2_0[:, BANK:], multiply("w4", 0, 1)[:], ACT.Square)
-        acc_1_second = multiply("w4", 1, 1)
-        scatter(pages_b[0], idx3, h2_0[:, :BANK], gain2, 0, BANK)
-        scatter(pages_b[1], idx3, h2_1_first[:], gain2, 0, BANK)
-        scatter(pages_b[0], idx3, h2_0[:, BANK:], gain2, BANK, S)
-        quantise_w1()
-        h2_1_second = sbuf.tile([P, BANK], F32, name="h2_1_second", tag="w1_raw1", align_bytes=64)
-        nc.scalar.activation(h2_1_second[:], acc_1_second[:], ACT.Square)
-        nc.scalar.copy(wo_bf16[:], wo_raw[:].rearrange("p i n -> p n i"))
+        def close_slice(t, banks):
+            for c in range(CHUNKS):
+                close_sum(t, c, banks[c], pages_a[t % 2])
+
+        h2_01 = [sbuf.tile([P, S], F32, name=f"h2_{t}", tag=f"h2_{t}", align_bytes=64) for t in range(2)]
+        for h in range(HALVES):
+            for t in range(2):
+                square(h2_01[t], "w4", t, h)
+        for h in range(HALVES):
+            for t in range(2):
+                scatter(pages_b[t], idx3, h2_01[t][:, h * BANK : (h + 1) * BANK], gain2, h * BANK, (h + 1) * BANK)
+        banks0 = open_sum(0, pages_b[0])
+        w1_bf16 = round_w1()
+        h2_23 = sbuf.tile([P, 2, S], F32, name="h2_23", tag="w1_raw1", align_bytes=64)
+        for t in range(2, SLICES):
+            for h in range(HALVES):
+                square(h2_23[:, t - 2, :], "w4", t, h)
         pages_a = []
         for b, spent in enumerate(("tab_word1", "w1_raw0")):
             page = sbuf.tile([P, T2], F32, name=f"page_a{b}", tag=spent, align_bytes=64)
             nc.gpsimd.memset(page[:], 0.0)
             pages_a.append(page)
-        scatter(pages_b[1], idx3, h2_1_second[:], gain2, BANK, S)
+        w1_word = sbuf.tile([P, SLICES, PASSES, P], U32, name="w1_word", tag="h2_1", align_bytes=64)
+        quantise_w1(w1_bf16)
+        scatter(pages_b[0], idx3, h2_23[:, 0, :], gain2, 0, S)
 
-        h1_01 = [ring([P, S], F32), ring([P, S], F32)]
-        for h in range(HALVES):
-            for t in range(2):
-                nc.scalar.activation(h1_01[t][:, h * BANK : (h + 1) * BANK], multiply("w1", t, h)[:], ACT.Square)
-        banks = open_sum(0, pages_b[0])
-        scatter(pages_a[0], idx2, h1_01[0][:, :BANK], gain1, 0, BANK)
-        scatter(pages_a[1], idx2, h1_01[1][:, :BANK], gain1, 0, BANK)
-        scatter(pages_a[0], idx2, h1_01[0][:, BANK:], gain1, BANK, S)
-        h2 = squares("w4", 2)
-        for c in range(CHUNKS):
-            close_sum(0, c, banks[c], pages_a[0])
-        banks = open_sum(1, pages_b[1])
-        scatter(pages_a[1], idx2, h1_01[1][:, BANK:], gain1, BANK, S)
+        h1 = sbuf.tile([P, SLICES, S], F32, name="h1", tag="tab_word0", align_bytes=64)
+        for t in (2, 3, 0, 1):
+            for h in range(HALVES):
+                square(h1[:, t, :], "w1", t, h)
+        wo_bf16 = sbuf.tile([P, N, PACK], BF16, name="wo_bf16", tag="v_word1", align_bytes=64)
+        nc.scalar.copy(wo_bf16[:], wo_raw[:].rearrange("p i n -> p n i"))
+        banks1 = open_sum(1, pages_b[1])
+        scatter(pages_a[0], idx2, h1[:, 0, :], gain1, 0, S)
+        close_slice(0, banks0)
+        banks2 = open_sum(2, pages_b[0])
+        scatter(pages_a[1], idx2, h1[:, 1, :], gain1, 0, S)
+        close_slice(1, banks1)
+        scatter(pages_b[1], idx3, h2_23[:, 1, :], gain2, 0, S)
+        banks3 = open_sum(3, pages_b[1])
+        scatter(pages_a[0], idx2, h1[:, 2, :], gain1, 0, S)
+        close_slice(2, banks2)
+        scatter(pages_a[1], idx2, h1[:, 3, :], gain1, 0, S)
 
-        for t in range(2, SLICES):
-            h1 = squares("w1", t)
-            for c in range(CHUNKS):
-                close_sum(t - 1, c, banks[c], pages_a[(t - 1) % 2])
-            scatter(pages_b[t % 2], idx3, h2[:], gain2, 0, S)
-            if t + 1 < SLICES:
-                h2 = squares("w4", t + 1)
-            banks = open_sum(t, pages_b[t % 2])
-            scatter(pages_a[t % 2], idx2, h1[:], gain1, 0, S)
-
-        wo_scale = ring([P, N], U8)
-        wo_word = ring([P, N], U32)
+        wo_scale = sbuf.tile([P, N], U8, name="wo_scale", align_bytes=64)
+        wo_word = sbuf.tile([P, N], U32, name="wo_word", tag="tab_word0", align_bytes=64)
         for first, end in ((0, 2 * P), (2 * P, N)):
             nc.vector.quantize_mx(
                 out=wo_word[:, first:end].bitcast(FP8X4),
@@ -276,5 +275,5 @@ def tile_list_inlet_speed_map_kernel(
                 in_=wo_bf16[:, first:end, :].rearrange("p n i -> p (n i)"),
             )
         for c in range(CHUNKS):
-            close_sum(SLICES - 1, c, banks[c], pages_a[(SLICES - 1) % 2])
+            close_sum(SLICES - 1, c, banks3[c], pages_a[1])
             finish_chunk(c, wo_word, wo_scale)

@@ -45,7 +45,7 @@ def tile_list_inlet_speed_map_kernel(
         idx = sbuf.tile([P, S // PER_COLUMN], U16, name="idx")
         idx2 = sbuf.tile([P, S // PER_COLUMN], U16, name="idx2")
         idx3 = sbuf.tile([P, S // PER_COLUMN], U16, name="idx3")
-        tab_scale = sbuf.tile([P, T], U8, name="tab_scale", align_bytes=64)
+        tab_scale = sbuf.tile([P, T], U8, name="tab_scale", tag="tab_scale", align_bytes=64)
         w4_scale = sbuf.tile([P, PASSES, H], U8, name="w4_scale", align_bytes=64)
         nc.vector.memset(tab_scale[:].bitcast(I32), 0)
         nc.vector.memset(w4_scale[:].rearrange("p a c -> p (a c)").bitcast(I32), 0)
@@ -66,31 +66,19 @@ def tile_list_inlet_speed_map_kernel(
         nc.sync.dma_start(idx[:], offs)
         load_table_words(0, 0, TABLE_HEAD)
         nc.sync.dma_start(w4_word[0][:].bitcast(I32), w4_word_rows[0])
+        load_table_words(0, TABLE_HEAD, 2 * TABLE_HEAD)
+        nc.sync.dma_start(idx3[:], offs3)
         for j in range(SCALE_ROWS):
             nc.sync.dma_start(tab_scale[j:P:SECOND_PASS_ROW, :].bitcast(I32), tab_scale_rows[j])
-        load_table_words(0, TABLE_HEAD, T)
+        load_table_words(0, 2 * TABLE_HEAD, T)
         load_table_words(1, 0, T // 2)
         for j in range(SCALE_ROWS):
             nc.sync.dma_start(w4_scale[j:P:QUADRANT, :, :].bitcast(I32), w4_scale_rows[j])
-        nc.sync.dma_start(idx3[:], offs3)
         load_table_words(1, T // 2, T)
         gain2 = sbuf.tile([P, S], F32, name="gain2")
         nc.sync.dma_start(gain2[:], wg2)
-        w1_raw = []
-        for a in range(PASSES):
-            raw = sbuf.tile([P, PACK, H], F32, name=f"w1_raw{a}", tag=f"w1_raw{a}", align_bytes=64)
-            nc.sync.dma_start(raw[:], w1[a * K_PASS : (a + 1) * K_PASS, :].rearrange("(p i) c -> p i c", i=PACK))
-            w1_raw.append(raw)
         nc.sync.dma_start(w4_word[1][:].bitcast(I32), w4_word_rows[1])
-        roughs = [sbuf.tile([P, T2], F32, name=f"rough{t}") for t in range(SLICES)]
-        nc.sync.dma_start(roughs[0][:], rough[0:P, :])
-        gain1 = sbuf.tile([P, S], F32, name="gain1")
-        nc.sync.dma_start(gain1[:], wg1)
         nc.sync.dma_start(idx2[:], offs2)
-        wo_raw = sbuf.tile([P, PACK, N], F32, name="wo_raw")
-        nc.sync.dma_start(wo_raw[:], wo.rearrange("(p i) n -> p i n", i=PACK))
-        for t in range(1, SLICES):
-            nc.sync.dma_start(roughs[t][:], rough[t * P : (t + 1) * P, :])
 
         ident = sbuf.tile([P, P], F32, name="ident")
         make_identity(nc, ident[:])
@@ -109,16 +97,27 @@ def tile_list_inlet_speed_map_kernel(
         )
         v_word = [sbuf.tile([P, S], U32, name=f"v_word{a}", tag=f"v_word{a}", align_bytes=64) for a in range(PASSES)]
         nc.vector.tensor_copy(v_word[0][:], tab_word[0][:].bitcast(U32).indirect(idx[:]))
+        w1_raw = sbuf.tile([P, PASSES, PACK, H], F32, name="w1_raw", tag="tab_word0", align_bytes=64)
+        for a in range(PASSES):
+            nc.sync.dma_start(w1_raw[:, a], w1[a * K_PASS : (a + 1) * K_PASS, :].rearrange("(p i) c -> p i c", i=PACK))
         for h in range(HALVES):
             entries = idx[:, h * BANK // PER_COLUMN : (h + 1) * BANK // PER_COLUMN]
             nc.vector.tensor_copy(v_word[1][:, h * BANK : (h + 1) * BANK], tab_word[1][:].bitcast(U32).indirect(entries))
 
+
+        def load_rough(first, spent):
+            pair = sbuf.tile([P, 2, T2], F32, name=f"rough{first}", tag=spent, align_bytes=64)
+            for b in range(2):
+                nc.sync.dma_start(pair[:, b, :], rough[(first + b) * P : (first + b + 1) * P, :])
+            return [pair[:, b, :] for b in range(2)]
+
+        roughs = load_rough(0, "tab_word1")
         w1_scale = sbuf.tile([P, SLICES, PASSES, P], U8, name="w1_scale", align_bytes=64)
 
         def round_w1():
             w1_bf16 = sbuf.tile([P, SLICES, PASSES, P, PACK], BF16, name="w1_bf16", tag="w4_word0", align_bytes=64)
             for a in range(PASSES):
-                nc.scalar.copy(w1_bf16[:, :, a, :, :], w1_raw[a][:].rearrange("p i (t c) -> p t c i", t=SLICES))
+                nc.scalar.copy(w1_bf16[:, :, a, :, :], w1_raw[:, a].rearrange("p i (t c) -> p t c i", t=SLICES))
             return w1_bf16
 
         def quantise_w1(w1_bf16):
@@ -233,25 +232,30 @@ def tile_list_inlet_speed_map_kernel(
         for h in range(HALVES):
             for t in range(2):
                 scatter(pages_b[t], idx3, h2_01[t][:, h * BANK : (h + 1) * BANK], gain2, h * BANK, (h + 1) * BANK)
+        gain1 = sbuf.tile([P, S], F32, name="gain1", tag="h2_0", align_bytes=64)
+        nc.sync.dma_start(gain1[:], wg1)
         banks0 = open_sum(0, pages_b[0])
         w1_bf16 = round_w1()
-        h2_23 = sbuf.tile([P, 2, S], F32, name="h2_23", tag="w1_raw1", align_bytes=64)
+        h2_23 = sbuf.tile([P, 2, S], F32, name="h2_23", tag="tab_word0", align_bytes=64)
         for t in range(2, SLICES):
             for h in range(HALVES):
                 square(h2_23[:, t - 2, :], "w4", t, h)
         pages_a = []
-        for b, spent in enumerate(("tab_word1", "w1_raw0")):
+        for b, spent in enumerate(("tab_scale", "w4_word1")):
             page = sbuf.tile([P, T2], F32, name=f"page_a{b}", tag=spent, align_bytes=64)
             nc.gpsimd.memset(page[:], 0.0)
             pages_a.append(page)
         w1_word = sbuf.tile([P, SLICES, PASSES, P], U32, name="w1_word", tag="h2_1", align_bytes=64)
         quantise_w1(w1_bf16)
+        wo_raw = sbuf.tile([P, PACK, N], F32, name="wo_raw", tag="w4_word0", align_bytes=64)
+        nc.sync.dma_start(wo_raw[:], wo.rearrange("(p i) n -> p i n", i=PACK))
         scatter(pages_b[0], idx3, h2_23[:, 0, :], gain2, 0, S)
 
-        h1 = sbuf.tile([P, SLICES, S], F32, name="h1", tag="tab_word0", align_bytes=64)
+        h1 = sbuf.tile([P, SLICES, S], F32, name="h1", tag="h1", align_bytes=64)
         for t in (2, 3, 0, 1):
             for h in range(HALVES):
                 square(h1[:, t, :], "w1", t, h)
+        roughs.extend(load_rough(2, "v_word0"))
         wo_bf16 = sbuf.tile([P, N, PACK], BF16, name="wo_bf16", tag="v_word1", align_bytes=64)
         nc.scalar.copy(wo_bf16[:], wo_raw[:].rearrange("p i n -> p n i"))
         banks1 = open_sum(1, pages_b[1])
@@ -267,7 +271,7 @@ def tile_list_inlet_speed_map_kernel(
         scatter(pages_a[1], idx2, h1[:, 3, :], gain1, 0, S)
 
         wo_scale = sbuf.tile([P, N], U8, name="wo_scale", align_bytes=64)
-        wo_word = sbuf.tile([P, N], U32, name="wo_word", tag="tab_word0", align_bytes=64)
+        wo_word = sbuf.tile([P, N], U32, name="wo_word", tag="h1", align_bytes=64)
         for first, end in ((0, 2 * P), (2 * P, N)):
             nc.vector.quantize_mx(
                 out=wo_word[:, first:end].bitcast(FP8X4),

@@ -105,13 +105,6 @@ def tile_list_inlet_speed_map_kernel(
             nc.vector.tensor_copy(v_word[1][:, h * BANK : (h + 1) * BANK], tab_word[1][:].bitcast(U32).indirect(entries))
 
 
-        def load_rough(first, spent):
-            pair = sbuf.tile([P, 2, T2], F32, name=f"rough{first}", tag=spent, align_bytes=64)
-            for b in range(2):
-                nc.sync.dma_start(pair[:, b, :], rough[(first + b) * P : (first + b + 1) * P, :])
-            return [pair[:, b, :] for b in range(2)]
-
-        roughs = load_rough(0, "tab_word1")
         w1_scale = sbuf.tile([P, SLICES, PASSES, P], U8, name="w1_scale", align_bytes=64)
 
         def round_w1():
@@ -155,65 +148,75 @@ def tile_list_inlet_speed_map_kernel(
             entries = offsets[:, first // PER_COLUMN : end // PER_COLUMN]
             nc.vector.tensor_tensor(page[:].indirect(entries), values, gain[:, first:end], MULT)
 
-        def add_transposed(bank, c, rows, opens, closes):
-            for mt in range(TILES):
+        def add_transposed(t, bank, c, rows, opens, closes):
+            for place in range(TILES):
+                k, half = divmod(place, 2)
+                tile = k + 2 * ((half + t // 2) % 2)
                 nc.tensor.matmul(
-                    bank[:, mt * P : (mt + 1) * P],
-                    rows[:, c * BANK + mt * P : c * BANK + (mt + 1) * P],
+                    bank[:, place * P : (place + 1) * P],
+                    rows[:, c * BANK + tile * P : c * BANK + (tile + 1) * P],
                     ident[:],
                     is_transpose=True,
-                    start=(opens and mt == 0),
-                    stop=(closes and mt == TILES - 1),
+                    start=(opens and place == 0),
+                    stop=(closes and place == TILES - 1),
                 )
 
         def open_sum(t, page_b):
             tag = "total" if t % 2 == 0 else "acc"
             banks = [psum.tile([P, BANK], F32, name=tag, tag=tag) for c in range(CHUNKS)]
             for c in range(CHUNKS):
-                add_transposed(banks[c], c, page_b, True, False)
+                add_transposed(t, banks[c], c, page_b, True, False)
             for c in range(CHUNKS):
-                add_transposed(banks[c], c, roughs[t], False, False)
+                add_transposed(t, banks[c], c, roughs[t], False, False)
             return banks
 
-        z_t = [sbuf.tile([P, 2, TILES, 2 * P], BF16, name=f"z_t{c}", align_bytes=64) for c in range(CHUNKS)]
-        span = 2 * P // SLICES
+        z_t = [
+            [sbuf.tile([P, 2, TILES, P], BF16, name=f"z_t{pair}_{c}", align_bytes=64) for c in range(CHUNKS)]
+            for pair in range(2)
+        ]
+        z_bf16 = [sbuf.tile([P, BANK * PACK], BF16, name=f"z_bf16_{c}", align_bytes=64) for c in range(CHUNKS)]
+        span = P // 2
 
         def close_sum(t, c, bank, page_a):
-            add_transposed(bank, c, page_a, False, True)
+            add_transposed(t, bank, c, page_a, False, True)
             nc.scalar.activation(
-                z_t[c][:, :, :, span * t : span * (t + 1)].rearrange("m u mt (p e) -> m u mt p e", e=2),
-                bank[:].rearrange("m (mt p u e) -> m u mt p e", mt=TILES, u=2, e=2),
+                z_t[t // 2][c][:, :, :, span * (t % 2) : span * (t % 2 + 1)].rearrange("m u x (p e) -> m u x p e", e=2),
+                bank[:].rearrange("m (x p u e) -> m u x p e", x=TILES, u=2, e=2),
                 ACT.Sqrt,
             )
 
+        def turn_back(pair, c, ks, tag, copy):
+            words = z_t[pair][c][:].rearrange("m u x v -> m u (x v)").bitcast(F32)
+            back = psum.tile([P, 2, len(ks) * P], F32, name=tag, tag=tag)
+            for u in range(2):
+                for j, k in enumerate(ks):
+                    nc.tensor.transpose(back[:, u, j * P : (j + 1) * P], words[:, u, k * P : (k + 1) * P], ident[:])
+            cells = z_bf16[c][:].bitcast(F32).rearrange("p (m u) -> p m u", u=2)
+            for half in range(2):
+                rows = slice(half * P // 2, (half + 1) * P // 2)
+                first = (ks[0] + 2 * ((half + pair) % 2)) * P
+                copy(cells[rows, first : first + len(ks) * P, :], back[rows].rearrange("p u m -> p m u"))
+
         def finish_chunk(c, wo_word, wo_scale):
-            z_bf16 = sbuf.tile([P, BANK * PACK], BF16, name=f"z_bf16_{c}", align_bytes=64)
-            pairs = z_t[c][:].bitcast(F32)
-            for b in range(2):
-                back = psum.tile([P, 2, 2 * P], F32, name="total", tag="total")
-                for u in range(2):
-                    for j in range(2):
-                        nc.tensor.transpose(back[:, u, j * P : (j + 1) * P], pairs[:, u, 2 * b + j, :], ident[:])
-                cells = z_bf16[:, b * 2 * BANK : (b + 1) * 2 * BANK].bitcast(F32).rearrange("p (m u) -> p m u", u=2)
-                if b == 0:
-                    nc.vector.tensor_copy(cells, back[:].rearrange("p u m -> p m u"))
-                else:
-                    nc.scalar.copy(cells, back[:].rearrange("p u m -> p m u"))
+            turn_back(1, c, (0,), "total", nc.vector.tensor_copy)
+            turn_back(1, c, (1,), "total", nc.scalar.copy)
             z_word = sbuf.tile([P, BANK], U32, name=f"z_word{c}", align_bytes=64)
             z_scale = sbuf.tile([P, BANK], U8, name=f"z_scale{c}", align_bytes=64)
-            nc.vector.quantize_mx(out=z_word[:].bitcast(FP8X4), scales=z_scale[:], in_=z_bf16[:])
+            nc.vector.quantize_mx(out=z_word[:].bitcast(FP8X4), scales=z_scale[:], in_=z_bf16[c][:])
             for g in range(GROUPS):
                 rows = slice(g * P, (g + 1) * P)
                 result = psum.tile([P, BANK], F32, name="acc", tag="acc")
-                nc.tensor.matmul_mx(
-                    out=result[:],
-                    lhsT=wo_word[:, rows].bitcast(FP8X4),
-                    lhsT_scale=wo_scale[:, rows],
-                    rhs=z_word[:].bitcast(FP8X4),
-                    rhs_scale=z_scale[:],
-                    start=True,
-                    stop=True,
-                )
+                for side in range(2):
+                    cols = slice(side * BANK // 2, (side + 1) * BANK // 2)
+                    nc.tensor.matmul_mx(
+                        out=result[:, cols],
+                        lhsT=wo_word[:, side, rows].bitcast(FP8X4),
+                        lhsT_scale=wo_scale[:, side, rows],
+                        rhs=z_word[:, cols].bitcast(FP8X4),
+                        rhs_scale=z_scale[:, cols],
+                        start=True,
+                        stop=True,
+                    )
                 staged = sbuf.tile([P, BANK], F32, name=f"staged{c}_{g}")
                 if (c * GROUPS + g) % 2 == 0:
                     nc.scalar.copy(staged[:], result[:])
@@ -232,16 +235,20 @@ def tile_list_inlet_speed_map_kernel(
         for h in range(HALVES):
             for t in range(2):
                 scatter(pages_b[t], idx3, h2_01[t][:, h * BANK : (h + 1) * BANK], gain2, h * BANK, (h + 1) * BANK)
-        gain1 = sbuf.tile([P, S], F32, name="gain1", tag="h2_0", align_bytes=64)
-        nc.sync.dma_start(gain1[:], wg1)
-        banks0 = open_sum(0, pages_b[0])
         w1_bf16 = round_w1()
         h2_23 = sbuf.tile([P, 2, S], F32, name="h2_23", tag="tab_word0", align_bytes=64)
         for t in range(2, SLICES):
             for h in range(HALVES):
                 square(h2_23[:, t - 2, :], "w4", t, h)
+        late = sbuf.tile([P, 2 * T2 + S], F32, name="late", tag="w4_word1", align_bytes=64)
+        roughs = [late[:, b * T2 : (b + 1) * T2] for b in range(2)]
+        gain1 = late[:, 2 * T2 :]
+        nc.sync.dma_start(roughs[0], rough[0:P, :])
+        nc.sync.dma_start(gain1, wg1)
+        nc.sync.dma_start(roughs[1], rough[P : 2 * P, :])
+        banks0 = open_sum(0, pages_b[0])
         pages_a = []
-        for b, spent in enumerate(("tab_scale", "w4_word1")):
+        for b, spent in enumerate(("tab_word1", "h2_0")):
             page = sbuf.tile([P, T2], F32, name=f"page_a{b}", tag=spent, align_bytes=64)
             nc.gpsimd.memset(page[:], 0.0)
             pages_a.append(page)
@@ -255,28 +262,37 @@ def tile_list_inlet_speed_map_kernel(
         for t in (2, 3, 0, 1):
             for h in range(HALVES):
                 square(h1[:, t, :], "w1", t, h)
-        roughs.extend(load_rough(2, "v_word0"))
-        wo_bf16 = sbuf.tile([P, N, PACK], BF16, name="wo_bf16", tag="v_word1", align_bytes=64)
-        nc.scalar.copy(wo_bf16[:], wo_raw[:].rearrange("p i n -> p n i"))
+        rough23 = sbuf.tile([P, 2, T2], F32, name="rough23", tag="v_word0", align_bytes=64)
+        for b in range(2):
+            nc.sync.dma_start(rough23[:, b, :], rough[(2 + b) * P : (3 + b) * P, :])
+            roughs.append(rough23[:, b, :])
+        wo_bf16 = sbuf.tile([P, 2, N, PACK], BF16, name="wo_bf16", tag="v_word1", align_bytes=64)
+        nc.scalar.copy(wo_bf16[:, 0], wo_raw[:].rearrange("p i n -> p n i"))
+        for half in range(2):
+            nc.sync.dma_start(
+                wo_bf16[half * P // 2 : (half + 1) * P // 2, 1], wo_bf16[(1 - half) * P // 2 : (2 - half) * P // 2, 0]
+            )
         banks1 = open_sum(1, pages_b[1])
         scatter(pages_a[0], idx2, h1[:, 0, :], gain1, 0, S)
         close_slice(0, banks0)
         banks2 = open_sum(2, pages_b[0])
         scatter(pages_a[1], idx2, h1[:, 1, :], gain1, 0, S)
         close_slice(1, banks1)
+        for c in range(CHUNKS):
+            turn_back(0, c, (0, 1), "acc", nc.scalar.copy)
         scatter(pages_b[1], idx3, h2_23[:, 1, :], gain2, 0, S)
         banks3 = open_sum(3, pages_b[1])
         scatter(pages_a[0], idx2, h1[:, 2, :], gain1, 0, S)
         close_slice(2, banks2)
         scatter(pages_a[1], idx2, h1[:, 3, :], gain1, 0, S)
 
-        wo_scale = sbuf.tile([P, N], U8, name="wo_scale", align_bytes=64)
-        wo_word = sbuf.tile([P, N], U32, name="wo_word", tag="h1", align_bytes=64)
-        for first, end in ((0, 2 * P), (2 * P, N)):
+        wo_scale = sbuf.tile([P, 2, N], U8, name="wo_scale", align_bytes=64)
+        wo_word = sbuf.tile([P, 2, N], U32, name="wo_word", tag="h1", align_bytes=64)
+        for first, end in ((0, BANK), (BANK, 2 * N)):
             nc.vector.quantize_mx(
-                out=wo_word[:, first:end].bitcast(FP8X4),
-                scales=wo_scale[:, first:end],
-                in_=wo_bf16[:, first:end, :].rearrange("p n i -> p (n i)"),
+                out=wo_word[:].rearrange("p s n -> p (s n)")[:, first:end].bitcast(FP8X4),
+                scales=wo_scale[:].rearrange("p s n -> p (s n)")[:, first:end],
+                in_=wo_bf16[:].rearrange("p s n i -> p (s n i)")[:, PACK * first : PACK * end],
             )
         for c in range(CHUNKS):
             close_sum(SLICES - 1, c, banks3[c], pages_a[1])

@@ -30,8 +30,6 @@ GROUPS = N // P
 PER_COLUMN = 16
 QUADRANT = 32
 SCALE_ROWS = 4
-TABLE_HEAD = 1024
-SECOND_PASS_ROW = 16
 
 
 def tile_list_inlet_speed_map_kernel(
@@ -47,34 +45,30 @@ def tile_list_inlet_speed_map_kernel(
         idx3 = sbuf.tile([P, S // PER_COLUMN], U16, name="idx3")
         tab_scale = sbuf.tile([P, T], U8, name="tab_scale", tag="tab_scale", align_bytes=64)
         w4_scale = sbuf.tile([P, PASSES, H], U8, name="w4_scale", align_bytes=64)
-        nc.vector.memset(tab_scale[:].bitcast(I32), 0)
+        v_scale = sbuf.tile([P, PASSES, S], U8, name="v_scale", align_bytes=64)
         nc.vector.memset(w4_scale[:].rearrange("p a c -> p (a c)").bitcast(I32), 0)
+        nc.vector.memset(tab_scale[QUADRANT : 2 * QUADRANT, :].bitcast(I32), 0)
+        nc.vector.memset(tab_scale[2 * QUADRANT : P, :].bitcast(I32), 0)
+        nc.vector.memset(v_scale[:].rearrange("p a c -> p (a c)").bitcast(I32), 0)
 
         tab_word = [sbuf.tile([P, T], I32, name=f"tab_word{a}", tag=f"tab_word{a}", align_bytes=64) for a in range(PASSES)]
 
-        def load_table_words(a, first, end):
-            words = tab_words[a].rearrange("p t i -> p (t i)").bitcast(I32)
-            nc.sync.dma_start(tab_word[a][:, first:end], words[:, first:end])
+        def load_table_words(a):
+            nc.sync.dma_start(tab_word[a][:], tab_words[a].rearrange("p t i -> p (t i)").bitcast(I32))
 
         w4_word_rows = w4_words.bitcast(I32).rearrange("a p (b c) -> b p a c", b=2)
         w4_word = [
             sbuf.tile([P, PASSES, H], U8, name=f"w4_word{b}", tag=f"w4_word{b}", align_bytes=64) for b in range(2)
         ]
         w4_scale_rows = w4_scales.bitcast(I32).rearrange("a (q j) c -> j q a c", j=SCALE_ROWS)
-        tab_scale_rows = tab_scales.bitcast(I32).rearrange("a (q j) t -> j q a t", j=SCALE_ROWS)
-
         nc.sync.dma_start(idx[:], offs)
-        load_table_words(0, 0, TABLE_HEAD)
-        nc.sync.dma_start(w4_word[0][:].bitcast(I32), w4_word_rows[0])
-        load_table_words(0, TABLE_HEAD, 2 * TABLE_HEAD)
+        nc.sync.dma_start(tab_scale[0:QUADRANT, :].bitcast(I32), tab_scales.bitcast(I32).rearrange("a r t -> r a t"))
+        nc.scalar.dma_start(w4_word[0][:].bitcast(I32), w4_word_rows[0])
+        load_table_words(0)
+        load_table_words(1)
+        for j in range(SCALE_ROWS):
+            nc.scalar.dma_start(w4_scale[j:P:QUADRANT, :, :].bitcast(I32), w4_scale_rows[j])
         nc.sync.dma_start(idx3[:], offs3)
-        for j in range(SCALE_ROWS):
-            nc.sync.dma_start(tab_scale[j:P:SECOND_PASS_ROW, :].bitcast(I32), tab_scale_rows[j])
-        load_table_words(0, 2 * TABLE_HEAD, T)
-        load_table_words(1, 0, T // 2)
-        for j in range(SCALE_ROWS):
-            nc.sync.dma_start(w4_scale[j:P:QUADRANT, :, :].bitcast(I32), w4_scale_rows[j])
-        load_table_words(1, T // 2, T)
         gain2 = sbuf.tile([P, S], F32, name="gain2")
         nc.sync.dma_start(gain2[:], wg2)
         nc.sync.dma_start(w4_word[1][:].bitcast(I32), w4_word_rows[1])
@@ -83,18 +77,20 @@ def tile_list_inlet_speed_map_kernel(
         ident = sbuf.tile([P, P], F32, name="ident")
         make_identity(nc, ident[:])
 
+        picked_scale = sbuf.tile([P, S], U8, name="picked_scale", align_bytes=64)
+        nc.vector.tensor_copy(picked_scale[:], tab_scale[:].indirect(idx[:]))
+        rows_a_quadrant = PASSES * SCALE_ROWS
+        for q in range(P // QUADRANT):
+            nc.scalar.dma_start(
+                v_scale[q * QUADRANT : q * QUADRANT + SCALE_ROWS, :, :].bitcast(I32),
+                picked_scale[q * rows_a_quadrant : (q + 1) * rows_a_quadrant, :].bitcast(I32),
+            )
         pages_b = []
         for b in range(2):
             page = sbuf.tile([P, T2], F32, name=f"page_b{b}")
             nc.vector.memset(page[:], 0.0)
             pages_b.append(page)
 
-        v_scale = [sbuf.tile([P, S], U8, name=f"v_scale{a}", align_bytes=64) for a in range(PASSES)]
-        nc.vector.memset(v_scale[1][:].bitcast(I32), 0)
-        nc.vector.tensor_copy(v_scale[0][:], tab_scale[:].indirect(idx[:]))
-        nc.scalar.dma_start(
-            v_scale[1][0 : P - SECOND_PASS_ROW, :].bitcast(I32), v_scale[0][SECOND_PASS_ROW:P, :].bitcast(I32)
-        )
         v_word = [sbuf.tile([P, S], U32, name=f"v_word{a}", tag=f"v_word{a}", align_bytes=64) for a in range(PASSES)]
         nc.vector.tensor_copy(v_word[0][:], tab_word[0][:].bitcast(U32).indirect(idx[:]))
         w1_raw = sbuf.tile([P, PASSES, PACK, H], F32, name="w1_raw", tag="tab_word0", align_bytes=64)
@@ -135,7 +131,7 @@ def tile_list_inlet_speed_map_kernel(
                     lhsT=codes,
                     lhsT_scale=scales,
                     rhs=v_word[a][:, cols].bitcast(FP8X4),
-                    rhs_scale=v_scale[a][:, cols],
+                    rhs_scale=v_scale[:, a, cols],
                     start=(a == 0),
                     stop=(a == PASSES - 1),
                 )

@@ -38,6 +38,7 @@ def tile_list_inlet_speed_map_kernel(
     nc = tc.nc
     with ExitStack() as ctx:
         sbuf = ctx.enter_context(tc.tile_pool(name="sbuf", bufs=1))
+        shared = ctx.enter_context(tc.tile_pool(name="shared", bufs=1))
         psum = ctx.enter_context(tc.psum_pool(name="psum", bufs=4))
 
         idx = sbuf.tile([P, S // PER_COLUMN], U16, name="idx")
@@ -51,7 +52,7 @@ def tile_list_inlet_speed_map_kernel(
         nc.vector.memset(tab_scale[2 * QUADRANT : P, :].bitcast(I32), 0)
         nc.vector.memset(v_scale[:].rearrange("p a c -> p (a c)").bitcast(I32), 0)
 
-        tab_word = [sbuf.tile([P, T], I32, name=f"tab_word{a}", tag=f"tab_word{a}", align_bytes=64) for a in range(PASSES)]
+        tab_word = [shared.tile([P, T], I32, name="tab_word0", offset=0), sbuf.tile([P, T], I32, name="tab_word1")]
 
         def load_table_words(a):
             nc.sync.dma_start(tab_word[a][:], tab_words[a].rearrange("p t i -> p (t i)").bitcast(I32))
@@ -73,6 +74,9 @@ def tile_list_inlet_speed_map_kernel(
         nc.sync.dma_start(gain2[:], wg2)
         nc.sync.dma_start(w4_word[1][:].bitcast(I32), w4_word_rows[1])
         nc.sync.dma_start(idx2[:], offs2)
+        w1_raw = sbuf.tile([P, PASSES, PACK, H], F32, name="w1_raw", tag="w1_raw", align_bytes=64)
+        for a in range(PASSES):
+            nc.sync.dma_start(w1_raw[:, a], w1[a * K_PASS : (a + 1) * K_PASS, :].rearrange("(p i) c -> p i c", i=PACK))
 
         ident = sbuf.tile([P, P], F32, name="ident")
         make_identity(nc, ident[:])
@@ -93,9 +97,11 @@ def tile_list_inlet_speed_map_kernel(
 
         v_word = [sbuf.tile([P, S], U32, name=f"v_word{a}", tag=f"v_word{a}", align_bytes=64) for a in range(PASSES)]
         nc.vector.tensor_copy(v_word[0][:], tab_word[0][:].bitcast(U32).indirect(idx[:]))
-        w1_raw = sbuf.tile([P, PASSES, PACK, H], F32, name="w1_raw", tag="tab_word0", align_bytes=64)
-        for a in range(PASSES):
-            nc.sync.dma_start(w1_raw[:, a], w1[a * K_PASS : (a + 1) * K_PASS, :].rearrange("(p i) c -> p i c", i=PACK))
+        pages_a = []
+        for b in range(2):
+            page = shared.tile([P, T2], F32, name=f"page_a{b}", offset=b * T2 * 4)
+            nc.vector.memset(page[:], 0.0)
+            pages_a.append(page)
         for h in range(HALVES):
             entries = idx[:, h * BANK // PER_COLUMN : (h + 1) * BANK // PER_COLUMN]
             nc.vector.tensor_copy(v_word[1][:, h * BANK : (h + 1) * BANK], tab_word[1][:].bitcast(U32).indirect(entries))
@@ -232,7 +238,7 @@ def tile_list_inlet_speed_map_kernel(
             for t in range(2):
                 scatter(pages_b[t], idx3, h2_01[t][:, h * BANK : (h + 1) * BANK], gain2, h * BANK, (h + 1) * BANK)
         w1_bf16 = round_w1()
-        h2_23 = sbuf.tile([P, 2, S], F32, name="h2_23", tag="tab_word0", align_bytes=64)
+        h2_23 = sbuf.tile([P, 2, S], F32, name="h2_23", tag="w1_raw", align_bytes=64)
         for t in range(2, SLICES):
             for h in range(HALVES):
                 square(h2_23[:, t - 2, :], "w4", t, h)
@@ -243,11 +249,6 @@ def tile_list_inlet_speed_map_kernel(
         nc.sync.dma_start(gain1, wg1)
         nc.sync.dma_start(roughs[1], rough[P : 2 * P, :])
         banks0 = open_sum(0, pages_b[0])
-        pages_a = []
-        for b, spent in enumerate(("tab_word1", "h2_0")):
-            page = sbuf.tile([P, T2], F32, name=f"page_a{b}", tag=spent, align_bytes=64)
-            nc.gpsimd.memset(page[:], 0.0)
-            pages_a.append(page)
         w1_word = sbuf.tile([P, SLICES, PASSES, P], U32, name="w1_word", tag="h2_1", align_bytes=64)
         quantise_w1(w1_bf16)
         wo_raw = sbuf.tile([P, PACK, N], F32, name="wo_raw", tag="w4_word0", align_bytes=64)

@@ -48,8 +48,7 @@ def tile_list_inlet_speed_map_kernel(
         w4_scale = sbuf.tile([P, PASSES, H], U8, name="w4_scale", align_bytes=64)
         v_scale = sbuf.tile([P, PASSES, S], U8, name="v_scale", align_bytes=64)
         nc.vector.memset(w4_scale[:].rearrange("p a c -> p (a c)").bitcast(I32), 0)
-        nc.vector.memset(tab_scale[QUADRANT : 2 * QUADRANT, :].bitcast(I32), 0)
-        nc.vector.memset(tab_scale[2 * QUADRANT : P, :].bitcast(I32), 0)
+        nc.vector.memset(tab_scale[0 : P - QUADRANT, :].bitcast(I32), 0)
         nc.vector.memset(v_scale[:].rearrange("p a c -> p (a c)").bitcast(I32), 0)
 
         tab_word = [shared.tile([P, T], I32, name="tab_word0", offset=0), sbuf.tile([P, T], I32, name="tab_word1")]
@@ -63,7 +62,7 @@ def tile_list_inlet_speed_map_kernel(
         ]
         w4_scale_rows = w4_scales.bitcast(I32).rearrange("a (q j) c -> j q a c", j=SCALE_ROWS)
         nc.sync.dma_start(idx[:], offs)
-        nc.sync.dma_start(tab_scale[0:QUADRANT, :].bitcast(I32), tab_scales.bitcast(I32).rearrange("a r t -> r a t"))
+        nc.sync.dma_start(tab_scale[P - QUADRANT : P, :].bitcast(I32), tab_scales.bitcast(I32).rearrange("a r t -> r a t"))
         nc.scalar.dma_start(w4_word[0][:].bitcast(I32), w4_word_rows[0])
         load_table_words(0)
         load_table_words(1)
@@ -87,7 +86,7 @@ def tile_list_inlet_speed_map_kernel(
         for q in range(P // QUADRANT):
             nc.scalar.dma_start(
                 v_scale[q * QUADRANT : q * QUADRANT + SCALE_ROWS, :, :].bitcast(I32),
-                picked_scale[q * rows_a_quadrant : (q + 1) * rows_a_quadrant, :].bitcast(I32),
+                picked_scale[P - QUADRANT + q * rows_a_quadrant : P - QUADRANT + (q + 1) * rows_a_quadrant, :].bitcast(I32),
             )
         pages_b = []
         for b in range(2):
@@ -126,7 +125,8 @@ def tile_list_inlet_speed_map_kernel(
         def multiply(weight, t, h):
             cols = slice(h * BANK, (h + 1) * BANK)
             acc = psum.tile([P, BANK], F32, name="acc", tag="acc")
-            for a in range(PASSES):
+            passes = (0, 1) if (weight, t, h) == ("w4", 0, 0) else (1, 0)
+            for a in passes:
                 if weight == "w1":
                     codes, scales = w1_word[:, t, a, :].bitcast(FP8X4), w1_scale[:, t, a, :]
                 else:
@@ -138,8 +138,8 @@ def tile_list_inlet_speed_map_kernel(
                     lhsT_scale=scales,
                     rhs=v_word[a][:, cols].bitcast(FP8X4),
                     rhs_scale=v_scale[:, a, cols],
-                    start=(a == 0),
-                    stop=(a == PASSES - 1),
+                    start=(a == passes[0]),
+                    stop=(a == passes[-1]),
                 )
             return acc
 
@@ -199,12 +199,15 @@ def tile_list_inlet_speed_map_kernel(
                 first = (ks[0] + 2 * ((half + pair) % 2)) * P
                 copy(cells[rows, first : first + len(ks) * P, :], back[rows].rearrange("p u m -> p m u"))
 
-        def finish_chunk(c, wo_word, wo_scale):
+        def quantise_chunk(c):
             turn_back(1, c, (0,), "total", nc.vector.tensor_copy)
             turn_back(1, c, (1,), "total", nc.scalar.copy)
             z_word = sbuf.tile([P, BANK], U32, name=f"z_word{c}", align_bytes=64)
             z_scale = sbuf.tile([P, BANK], U8, name=f"z_scale{c}", align_bytes=64)
             nc.vector.quantize_mx(out=z_word[:].bitcast(FP8X4), scales=z_scale[:], in_=z_bf16[c][:])
+            return z_word, z_scale
+
+        def multiply_chunk(c, z_word, z_scale):
             for g in range(GROUPS):
                 rows = slice(g * P, (g + 1) * P)
                 result = psum.tile([P, BANK], F32, name="acc", tag="acc")
@@ -220,7 +223,7 @@ def tile_list_inlet_speed_map_kernel(
                         stop=True,
                     )
                 staged = sbuf.tile([P, BANK], F32, name=f"staged{c}_{g}")
-                if (c * GROUPS + g) % 2 == 0:
+                if g != 1:
                     nc.scalar.copy(staged[:], result[:])
                 else:
                     nc.vector.tensor_copy(staged[:], result[:])
@@ -291,6 +294,10 @@ def tile_list_inlet_speed_map_kernel(
                 scales=wo_scale[:].rearrange("p s n -> p (s n)")[:, first:end],
                 in_=wo_bf16[:].rearrange("p s n i -> p (s n i)")[:, PACK * first : PACK * end],
             )
+        quantised = []
         for c in range(CHUNKS):
             close_sum(SLICES - 1, c, banks3[c], pages_a[1])
-            finish_chunk(c, wo_word, wo_scale)
+            quantised.append(quantise_chunk(c))
+            if c > 0:
+                multiply_chunk(c - 1, *quantised[c - 1])
+        multiply_chunk(CHUNKS - 1, *quantised[-1])

@@ -47,7 +47,7 @@ def tile_list_inlet_speed_map_kernel(
         tab_scale = sbuf.tile([P, T], U8, name="tab_scale", tag="tab_scale", align_bytes=64)
         w4_scale = sbuf.tile([P, PASSES, H], U8, name="w4_scale", align_bytes=64)
         v_scale = sbuf.tile([P, PASSES, S], U8, name="v_scale", align_bytes=64)
-        nc.vector.memset(w4_scale[:].rearrange("p a c -> p (a c)").bitcast(I32), 0)
+        nc.gpsimd.memset(w4_scale[:].rearrange("p a c -> p (a c)").bitcast(I32), 0)
         nc.vector.memset(tab_scale[0 : P - QUADRANT, :].bitcast(I32), 0)
         nc.vector.memset(v_scale[:].rearrange("p a c -> p (a c)").bitcast(I32), 0)
 
@@ -63,11 +63,11 @@ def tile_list_inlet_speed_map_kernel(
         w4_scale_rows = w4_scales.bitcast(I32).rearrange("a (q j) c -> j q a c", j=SCALE_ROWS)
         nc.sync.dma_start(idx[:], offs)
         nc.sync.dma_start(tab_scale[P - QUADRANT : P, :].bitcast(I32), tab_scales.bitcast(I32).rearrange("a r t -> r a t"))
-        nc.scalar.dma_start(w4_word[0][:].bitcast(I32), w4_word_rows[0])
+        nc.sync.dma_start(w4_word[0][:].bitcast(I32), w4_word_rows[0])
+        for j in range(SCALE_ROWS):
+            nc.sync.dma_start(w4_scale[j:P:QUADRANT, :, :].bitcast(I32), w4_scale_rows[j])
         load_table_words(0)
         load_table_words(1)
-        for j in range(SCALE_ROWS):
-            nc.scalar.dma_start(w4_scale[j:P:QUADRANT, :, :].bitcast(I32), w4_scale_rows[j])
         nc.sync.dma_start(idx3[:], offs3)
         gain2 = sbuf.tile([P, S], F32, name="gain2")
         nc.sync.dma_start(gain2[:], wg2)
@@ -89,8 +89,8 @@ def tile_list_inlet_speed_map_kernel(
                 picked_scale[P - QUADRANT + q * rows_a_quadrant : P - QUADRANT + (q + 1) * rows_a_quadrant, :].bitcast(I32),
             )
         pages_b = []
-        for b in range(2):
-            page = sbuf.tile([P, T2], F32, name=f"page_b{b}")
+        for b, tag in enumerate(("page_b0", "tab_scale")):
+            page = sbuf.tile([P, T2], F32, name=f"page_b{b}", tag=tag, align_bytes=64)
             nc.vector.memset(page[:], 0.0)
             pages_b.append(page)
 

@@ -16,12 +16,13 @@ FP8X4 = mybir.dt.float8_e4m3fn_x4
 FP4X4 = mybir.dt.float4_e2m1fn_x4
 ACT = mybir.ActivationFunctionType
 MULT = mybir.AluOpType.mult
+ADD = mybir.AluOpType.add
 
 P = 128
 PACK = 4
 K_PASS = P * PACK
 PASSES = K // K_PASS
-SLICES = H // P
+SLICES = PACK
 BANK = 512
 HALVES = S // BANK
 CHUNKS = T2 // BANK
@@ -30,6 +31,8 @@ GROUPS = N // P
 PER_COLUMN = 16
 QUADRANT = 32
 SCALE_ROWS = 4
+KB = 1024
+UNITS = ((0, 256), (256, 256), (512, 512), (1024, 512), (1536, 512))
 
 
 def tile_list_inlet_speed_map_kernel(
@@ -38,49 +41,77 @@ def tile_list_inlet_speed_map_kernel(
     nc = tc.nc
     with ExitStack() as ctx:
         sbuf = ctx.enter_context(tc.tile_pool(name="sbuf", bufs=1))
-        shared = ctx.enter_context(tc.tile_pool(name="shared", bufs=1))
+        arena = ctx.enter_context(tc.tile_pool(name="arena", bufs=1))
         psum = ctx.enter_context(tc.psum_pool(name="psum", bufs=4))
+
+        def own(shape, dtype, name):
+            return sbuf.tile(shape, dtype, name=name, align_bytes=64)
+
+        def at(offset, shape, dtype, name):
+            return arena.tile(shape, dtype, name=name, offset=offset, align_bytes=64)
 
         idx = sbuf.tile([P, S // PER_COLUMN], U16, name="idx")
         idx2 = sbuf.tile([P, S // PER_COLUMN], U16, name="idx2")
         idx3 = sbuf.tile([P, S // PER_COLUMN], U16, name="idx3")
-        tab_scale = sbuf.tile([P, T], U8, name="tab_scale", tag="tab_scale", align_bytes=64)
-        w4_scale = sbuf.tile([P, PASSES, H], U8, name="w4_scale", align_bytes=64)
-        v_scale = sbuf.tile([P, PASSES, S], U8, name="v_scale", align_bytes=64)
-        nc.gpsimd.memset(w4_scale[:].rearrange("p a c -> p (a c)").bitcast(I32), 0)
+        tab_scale = at(120 * KB, [P, T], U8, "tab_scale")
+        w4_scale_raw = own([P, PASSES, H], U8, "w4_scale_raw")
+        v_scale = own([P, PASSES, S], U8, "v_scale")
+        nc.gpsimd.memset(w4_scale_raw[:].rearrange("p a c -> p (a c)").bitcast(I32), 0)
         nc.vector.memset(tab_scale[0 : P - QUADRANT, :].bitcast(I32), 0)
         nc.vector.memset(v_scale[:].rearrange("p a c -> p (a c)").bitcast(I32), 0)
 
-        tab_word = [shared.tile([P, T], I32, name="tab_word0", offset=0), sbuf.tile([P, T], I32, name="tab_word1")]
-
-        def load_table_words(a):
-            nc.sync.dma_start(tab_word[a][:], tab_words[a].rearrange("p t i -> p (t i)").bitcast(I32))
-
-        w4_word_rows = w4_words.bitcast(I32).rearrange("a p (b c) -> b p a c", b=2)
-        w4_word = [
-            sbuf.tile([P, PASSES, H], U8, name=f"w4_word{b}", tag=f"w4_word{b}", align_bytes=64) for b in range(2)
-        ]
+        tab_word = [at(16 * KB * a, [P, T], I32, f"tab_word{a}") for a in range(PASSES)]
+        w4_raw = own([P, PASSES, 2 * H], U8, "w4_raw")
         w4_scale_rows = w4_scales.bitcast(I32).rearrange("a (q j) c -> j q a c", j=SCALE_ROWS)
         nc.sync.dma_start(idx[:], offs)
         nc.sync.dma_start(tab_scale[P - QUADRANT : P, :].bitcast(I32), tab_scales.bitcast(I32).rearrange("a r t -> r a t"))
-        nc.sync.dma_start(w4_word[0][:].bitcast(I32), w4_word_rows[0])
+        nc.sync.dma_start(w4_raw[:].bitcast(I32), w4_words.bitcast(I32).rearrange("a p c -> p a c"))
         for j in range(SCALE_ROWS):
-            nc.sync.dma_start(w4_scale[j:P:QUADRANT, :, :].bitcast(I32), w4_scale_rows[j])
-        load_table_words(0)
-        load_table_words(1)
-        nc.sync.dma_start(idx3[:], offs3)
-        gain2 = sbuf.tile([P, S], F32, name="gain2")
-        nc.sync.dma_start(gain2[:], wg2)
-        nc.sync.dma_start(w4_word[1][:].bitcast(I32), w4_word_rows[1])
-        nc.sync.dma_start(idx2[:], offs2)
-        w1_raw = sbuf.tile([P, PASSES, PACK, H], F32, name="w1_raw", tag="w1_raw", align_bytes=64)
+            nc.sync.dma_start(w4_scale_raw[j:P:QUADRANT, :, :].bitcast(I32), w4_scale_rows[j])
         for a in range(PASSES):
-            nc.sync.dma_start(w1_raw[:, a], w1[a * K_PASS : (a + 1) * K_PASS, :].rearrange("(p i) c -> p i c", i=PACK))
+            nc.sync.dma_start(tab_word[a][:], tab_words[a].rearrange("p t i -> p (t i)").bitcast(I32))
+        nc.sync.dma_start(idx3[:], offs3)
+
+        def load_gain(wg, offset, name, first, end, h_first, h_end):
+            cols = slice(h_first * BANK, h_end * BANK)
+            gain = at(offset, [P, end - first, (h_end - h_first) * BANK], F32, name)
+            rows = wg.rearrange("(p t) j -> p t j", t=SLICES)[:, first:end, cols]
+            for q in (0, 2, 1, 3):
+                nc.sync.dma_start(gain[q * QUADRANT : (q + 1) * QUADRANT], rows)
+            return gain
+
+        gain2_0a = load_gain(wg2, 32 * KB, "gain2_0a", 0, 1, 0, 1)
+        gain2_1a = load_gain(wg2, 34 * KB, "gain2_1a", 1, 2, 0, 1)
+        w1_raw = [at((48 + 8 * a) * KB, [P, PACK, H], F32, f"w1_raw{a}") for a in range(PASSES)]
+
+        def load_w1(a):
+            nc.sync.dma_start(w1_raw[a][:], w1[a * K_PASS : (a + 1) * K_PASS, :].rearrange("(p i) c -> p i c", i=PACK))
+
+        load_w1(0)
+        gain2_01b = load_gain(wg2, 36 * KB, "gain2_01b", 0, 2, 1, 2)
+        load_w1(1)
+        nc.sync.dma_start(idx2[:], offs2)
+        gain2_2 = load_gain(wg2, 40 * KB, "gain2_2", 2, 3, 0, 2)
+        rough_rows = rough.rearrange("(p t) m -> t p m", t=SLICES)
+        roughs = [at((80 + 8 * t) * KB, [P, T2], F32, f"rough{t}") for t in range(SLICES)]
+        nc.sync.dma_start(roughs[0][:], rough_rows[0])
+        gain1_01 = load_gain(wg1, 16 * KB, "gain1_01", 0, 2, 0, 2)
+        nc.sync.dma_start(roughs[1][:], rough_rows[1])
+        gain1_2 = load_gain(wg1, 24 * KB, "gain1_2", 2, 3, 0, 2)
+        nc.sync.dma_start(roughs[2][:], rough_rows[2])
+        nc.sync.dma_start(roughs[3][:], rough_rows[3])
 
         ident = sbuf.tile([P, P], F32, name="ident")
         make_identity(nc, ident[:])
 
-        picked_scale = sbuf.tile([P, S], U8, name="picked_scale", align_bytes=64)
+        w4_word = [at((144 + 8 * b) * KB, [P, 2, PASSES, 2 * P], U8, f"w4_word{b}") for b in range(2)]
+        w4_scale = own([P, SLICES, PASSES, P], U8, "w4_scale")
+        w4_by_slice = w4_raw[:].bitcast(U16).rearrange("p a (m t) -> p t a m", t=SLICES)
+        for b in range(2):
+            nc.vector.tensor_copy(w4_word[b][:].bitcast(U16), w4_by_slice[:, 2 * b : 2 * b + 2])
+        nc.vector.tensor_copy(w4_scale[:], w4_scale_raw[:].rearrange("p a (m t) -> p t a m", t=SLICES))
+
+        picked_scale = own([P, S], U8, "picked_scale")
         nc.vector.tensor_copy(picked_scale[:], tab_scale[:].indirect(idx[:]))
         rows_a_quadrant = PASSES * SCALE_ROWS
         for q in range(P // QUADRANT):
@@ -89,38 +120,23 @@ def tile_list_inlet_speed_map_kernel(
                 picked_scale[P - QUADRANT + q * rows_a_quadrant : P - QUADRANT + (q + 1) * rows_a_quadrant, :].bitcast(I32),
             )
         pages_b = []
-        for b, tag in enumerate(("page_b0", "tab_scale")):
-            page = sbuf.tile([P, T2], F32, name=f"page_b{b}", tag=tag, align_bytes=64)
+        for b in range(2):
+            page = at((112 + 8 * b) * KB, [P, T2], F32, f"page_b{b}")
             nc.vector.memset(page[:], 0.0)
             pages_b.append(page)
 
-        v_word = [sbuf.tile([P, S], U32, name=f"v_word{a}", tag=f"v_word{a}", align_bytes=64) for a in range(PASSES)]
+        v_word = [at((128 + 4 * a) * KB, [P, S], U32, f"v_word{a}") for a in range(PASSES)]
         nc.vector.tensor_copy(v_word[0][:], tab_word[0][:].bitcast(U32).indirect(idx[:]))
         pages_a = []
         for b in range(2):
-            page = shared.tile([P, T2], F32, name=f"page_a{b}", offset=b * T2 * 4)
+            page = at(8 * b * KB, [P, T2], F32, f"page_a{b}")
             nc.vector.memset(page[:], 0.0)
             pages_a.append(page)
         for h in range(HALVES):
             entries = idx[:, h * BANK // PER_COLUMN : (h + 1) * BANK // PER_COLUMN]
             nc.vector.tensor_copy(v_word[1][:, h * BANK : (h + 1) * BANK], tab_word[1][:].bitcast(U32).indirect(entries))
 
-
-        w1_scale = sbuf.tile([P, SLICES, PASSES, P], U8, name="w1_scale", align_bytes=64)
-
-        def round_w1():
-            w1_bf16 = sbuf.tile([P, SLICES, PASSES, P, PACK], BF16, name="w1_bf16", tag="w4_word0", align_bytes=64)
-            for a in range(PASSES):
-                nc.scalar.copy(w1_bf16[:, :, a, :, :], w1_raw[:, a].rearrange("p i (t c) -> p t c i", t=SLICES))
-            return w1_bf16
-
-        def quantise_w1(w1_bf16):
-            for first, end in ((2, SLICES), (0, 2)):
-                nc.vector.quantize_mx(
-                    out=w1_word[:, first:end].rearrange("p t a c -> p (t a c)").bitcast(FP8X4),
-                    scales=w1_scale[:, first:end].rearrange("p t a c -> p (t a c)"),
-                    in_=w1_bf16[:, first:end].rearrange("p t a c i -> p (t a c i)"),
-                )
+        w1_scale = own([P, SLICES, PASSES, P], U8, "w1_scale")
 
         def multiply(weight, t, h):
             cols = slice(h * BANK, (h + 1) * BANK)
@@ -130,8 +146,7 @@ def tile_list_inlet_speed_map_kernel(
                 if weight == "w1":
                     codes, scales = w1_word[:, t, a, :].bitcast(FP8X4), w1_scale[:, t, a, :]
                 else:
-                    codes = w4_word[t // 2][:, a, 2 * P * (t % 2) : 2 * P * (t % 2 + 1)].bitcast(FP4X4)
-                    scales = w4_scale[:, a, P * t : P * (t + 1)]
+                    codes, scales = w4_word[t // 2][:, t % 2, a, :].bitcast(FP4X4), w4_scale[:, t, a, :]
                 nc.tensor.matmul_mx(
                     out=acc[:],
                     lhsT=codes,
@@ -148,156 +163,219 @@ def tile_list_inlet_speed_map_kernel(
 
         def scatter(page, offsets, values, gain, first, end):
             entries = offsets[:, first // PER_COLUMN : end // PER_COLUMN]
-            nc.vector.tensor_tensor(page[:].indirect(entries), values, gain[:, first:end], MULT)
+            nc.vector.tensor_tensor(page[:].indirect(entries), values, gain, MULT)
 
-        def add_transposed(t, bank, c, rows, opens, closes):
-            for place in range(TILES):
-                k, half = divmod(place, 2)
-                tile = k + 2 * ((half + t // 2) % 2)
+        def add_transposed(bank, c, rows, opens, closes):
+            for j in range(TILES):
                 nc.tensor.matmul(
-                    bank[:, place * P : (place + 1) * P],
-                    rows[:, c * BANK + tile * P : c * BANK + (tile + 1) * P],
+                    bank[:, j * P : (j + 1) * P],
+                    rows[:, c * BANK + j * P : c * BANK + (j + 1) * P],
                     ident[:],
                     is_transpose=True,
-                    start=(opens and place == 0),
-                    stop=(closes and place == TILES - 1),
+                    start=(opens and j == 0),
+                    stop=(closes and j == TILES - 1),
                 )
 
-        def open_sum(t, page_b):
-            tag = "total" if t % 2 == 0 else "acc"
-            banks = [psum.tile([P, BANK], F32, name=tag, tag=tag) for c in range(CHUNKS)]
+        def new_banks(tag):
+            return [psum.tile([P, BANK], F32, name=tag, tag=tag) for c in range(CHUNKS)]
+
+        def add_all(banks, rows, opens, closes):
             for c in range(CHUNKS):
-                add_transposed(t, banks[c], c, page_b, True, False)
-            for c in range(CHUNKS):
-                add_transposed(t, banks[c], c, roughs[t], False, False)
+                add_transposed(banks[c], c, rows, opens, closes)
+
+        def open_sum(t, tag, page_b):
+            banks = new_banks(tag)
+            add_all(banks, page_b, True, False)
+            add_all(banks, roughs[t], False, False)
             return banks
 
-        z_t = [
-            [sbuf.tile([P, 2, TILES, P], BF16, name=f"z_t{pair}_{c}", align_bytes=64) for c in range(CHUNKS)]
-            for pair in range(2)
-        ]
-        z_bf16 = [sbuf.tile([P, BANK * PACK], BF16, name=f"z_bf16_{c}", align_bytes=64) for c in range(CHUNKS)]
-        span = P // 2
+        words = [at(80 * KB + 8 * first, [P, 2, width], F32, f"words{first}") for first, width in UNITS]
 
-        def close_sum(t, c, bank, page_a):
-            add_transposed(t, bank, c, page_a, False, True)
-            nc.scalar.activation(
-                z_t[t // 2][c][:, :, :, span * (t % 2) : span * (t % 2 + 1)].rearrange("m u x (p e) -> m u x p e", e=2),
-                bank[:].rearrange("m (x p u e) -> m u x p e", x=TILES, u=2, e=2),
-                ACT.Sqrt,
-            )
+        def units_of(c):
+            return [(u, first - c * BANK, width) for u, (first, width) in enumerate(UNITS) if first // BANK == c]
 
-        def turn_back(pair, c, ks, tag, copy):
-            words = z_t[pair][c][:].rearrange("m u x v -> m u (x v)").bitcast(F32)
-            back = psum.tile([P, 2, len(ks) * P], F32, name=tag, tag=tag)
-            for u in range(2):
-                for j, k in enumerate(ks):
-                    nc.tensor.transpose(back[:, u, j * P : (j + 1) * P], words[:, u, k * P : (k + 1) * P], ident[:])
-            cells = z_bf16[c][:].bitcast(F32).rearrange("p (m u) -> p m u", u=2)
-            for half in range(2):
-                rows = slice(half * P // 2, (half + 1) * P // 2)
-                first = (ks[0] + 2 * ((half + pair) % 2)) * P
-                copy(cells[rows, first : first + len(ks) * P, :], back[rows].rearrange("p u m -> p m u"))
+        def roots_of(u, half, e):
+            return words[u][:, half, :].bitcast(BF16).rearrange("p (m e) -> p m e", e=2)[:, :, e]
 
-        def quantise_chunk(c):
-            turn_back(1, c, (0,), "total", nc.vector.tensor_copy)
-            turn_back(1, c, (1,), "total", nc.scalar.copy)
-            z_word = sbuf.tile([P, BANK], U32, name=f"z_word{c}", align_bytes=64)
-            z_scale = sbuf.tile([P, BANK], U8, name=f"z_scale{c}", align_bytes=64)
-            nc.vector.quantize_mx(out=z_word[:].bitcast(FP8X4), scales=z_scale[:], in_=z_bf16[c][:])
-            return z_word, z_scale
+        pair_t = [at((48 + 2 * c) * KB, [P, BANK], F32, f"pair_t{c}") for c in range(CHUNKS)]
 
-        def multiply_chunk(c, z_word, z_scale):
-            for g in range(GROUPS):
-                rows = slice(g * P, (g + 1) * P)
-                result = psum.tile([P, BANK], F32, name="acc", tag="acc")
-                for side in range(2):
-                    cols = slice(side * BANK // 2, (side + 1) * BANK // 2)
-                    nc.tensor.matmul_mx(
-                        out=result[:, cols],
-                        lhsT=wo_word[:, side, rows].bitcast(FP8X4),
-                        lhsT_scale=wo_scale[:, side, rows],
-                        rhs=z_word[:, cols].bitcast(FP8X4),
-                        rhs_scale=z_scale[:, cols],
-                        start=True,
-                        stop=True,
-                    )
-                staged = sbuf.tile([P, BANK], F32, name=f"staged{c}_{g}")
-                if g != 1:
-                    nc.scalar.copy(staged[:], result[:])
-                else:
-                    nc.vector.tensor_copy(staged[:], result[:])
-                nc.sync.dma_start(out[rows, c * BANK : (c + 1) * BANK], staged[:])
-
-        def close_slice(t, banks):
+        def close_pair_slice(t, banks):
             for c in range(CHUNKS):
-                close_sum(t, c, banks[c], pages_a[t % 2])
+                add_transposed(banks[c], c, pages_a[t], False, True)
+                nc.scalar.activation(
+                    pair_t[c][:].bitcast(BF16).rearrange("m (x e) -> m x e", e=2)[:, :, t], banks[c][:], ACT.Sqrt
+                )
 
-        h2_01 = [sbuf.tile([P, S], F32, name=f"h2_{t}", tag=f"h2_{t}", align_bytes=64) for t in range(2)]
+        def turn_pair_back():
+            for c in range(CHUNKS):
+                back = psum.tile([P, BANK], F32, name="acc", tag="acc")
+                for j in range(TILES):
+                    nc.tensor.transpose(back[:, j * P : (j + 1) * P], pair_t[c][:, j * P : (j + 1) * P], ident[:])
+                for u, first, width in units_of(c):
+                    nc.scalar.copy(words[u][:, 0, :], back[:, first : first + width])
+
+        def finish_slice_2(banks):
+            for c in range(CHUNKS):
+                add_transposed(banks[c], c, pages_a[0], False, True)
+                tiles_t = at((44 + c) * KB, [P, BANK // 2], F32, f"tiles_t{c}")
+                nc.scalar.activation(
+                    tiles_t[:].bitcast(BF16).rearrange("m (x p e) -> m x p e", x=2, e=2),
+                    banks[c][:].rearrange("m (x e p) -> m x p e", x=2, e=2),
+                    ACT.Sqrt,
+                )
+                back = psum.tile([P, BANK // 2], F32, name="acc", tag="acc")
+                for x in range(2):
+                    nc.tensor.transpose(back[:, x * P : (x + 1) * P], tiles_t[:, x * P : (x + 1) * P], ident[:])
+                cells = back[:].bitcast(BF16).rearrange("p (x m e) -> p x e m", x=2, e=2)
+                for u, first, width in units_of(c):
+                    xs = slice(first // (2 * P), (first + width) // (2 * P))
+                    nc.scalar.copy(roots_of(u, 1, 0).rearrange("p (x e m) -> p x e m", e=2, m=P), cells[:, xs])
+
+        def base_of_slice_3(banks):
+            based = []
+            for c in range(CHUNKS):
+                add_transposed(banks[c], c, pages_b[1], False, True)
+                turned = at((48 + 2 * c) * KB, [P, BANK], F32, f"turned{c}")
+                nc.scalar.copy(turned[:], banks[c][:])
+                back = psum.tile([P, BANK], F32, name="acc", tag="acc")
+                for j in range(TILES):
+                    nc.tensor.transpose(back[:, j * P : (j + 1) * P], turned[:, j * P : (j + 1) * P], ident[:])
+                based.append(back)
+            return based
+
+        h2_01 = [at((136 + 4 * t) * KB, [P, S], F32, f"h2_{t}") for t in range(2)]
         for h in range(HALVES):
             for t in range(2):
                 square(h2_01[t], "w4", t, h)
-        for h in range(HALVES):
-            for t in range(2):
-                scatter(pages_b[t], idx3, h2_01[t][:, h * BANK : (h + 1) * BANK], gain2, h * BANK, (h + 1) * BANK)
-        w1_bf16 = round_w1()
-        h2_23 = sbuf.tile([P, 2, S], F32, name="h2_23", tag="w1_raw", align_bytes=64)
-        for t in range(2, SLICES):
+        for t, gain in enumerate((gain2_0a, gain2_1a)):
+            scatter(pages_b[t], idx3, h2_01[t][:, :BANK], gain[:, 0, :], 0, BANK)
+        for t in range(2):
+            scatter(pages_b[t], idx3, h2_01[t][:, BANK:], gain2_01b[:, t, :], BANK, S)
+        w1_bf16 = at(144 * KB, [P, SLICES, PASSES, P, PACK], BF16, "w1_bf16")
+        for a in range(PASSES):
+            nc.scalar.copy(
+                w1_bf16[:, :, a, :, :].rearrange("p t m i -> p m t i"),
+                w1_raw[a][:].rearrange("p i (m t) -> p m t i", t=SLICES),
+            )
+        h2_23 = [at((56 + 4 * b) * KB, [P, S], F32, f"h2_{2 + b}") for b in range(2)]
+        for b in range(2):
             for h in range(HALVES):
-                square(h2_23[:, t - 2, :], "w4", t, h)
-        late = sbuf.tile([P, 2 * T2 + S], F32, name="late", tag="w4_word1", align_bytes=64)
-        roughs = [late[:, b * T2 : (b + 1) * T2] for b in range(2)]
-        gain1 = late[:, 2 * T2 :]
-        nc.sync.dma_start(roughs[0], rough[0:P, :])
-        nc.sync.dma_start(gain1, wg1)
-        nc.sync.dma_start(roughs[1], rough[P : 2 * P, :])
-        banks0 = open_sum(0, pages_b[0])
-        w1_word = sbuf.tile([P, SLICES, PASSES, P], U32, name="w1_word", tag="h2_1", align_bytes=64)
-        quantise_w1(w1_bf16)
-        wo_raw = sbuf.tile([P, PACK, N], F32, name="wo_raw", tag="w4_word0", align_bytes=64)
+                square(h2_23[b], "w4", 2 + b, h)
+        banks0 = open_sum(0, "total", pages_b[0])
+        w1_word = at(140 * KB, [P, SLICES, PASSES, P], U32, "w1_word")
+        for first, end in ((2, SLICES), (0, 2)):
+            nc.vector.quantize_mx(
+                out=w1_word[:, first:end].rearrange("p t a c -> p (t a c)").bitcast(FP8X4),
+                scales=w1_scale[:, first:end].rearrange("p t a c -> p (t a c)"),
+                in_=w1_bf16[:, first:end].rearrange("p t a c i -> p (t a c i)"),
+            )
+        wo_raw = at(144 * KB, [P, PACK, N], F32, "wo_raw")
         nc.sync.dma_start(wo_raw[:], wo.rearrange("(p i) n -> p i n", i=PACK))
-        scatter(pages_b[0], idx3, h2_23[:, 0, :], gain2, 0, S)
+        scatter(pages_b[0], idx3, h2_23[0][:], gain2_2[:, 0, :], 0, S)
 
-        h1 = sbuf.tile([P, SLICES, S], F32, name="h1", tag="h1", align_bytes=64)
+        h1 = [at((64 + 4 * t) * KB, [P, S], F32, f"h1_{t}") for t in range(SLICES)]
         for t in (2, 3, 0, 1):
             for h in range(HALVES):
-                square(h1[:, t, :], "w1", t, h)
-        rough23 = sbuf.tile([P, 2, T2], F32, name="rough23", tag="v_word0", align_bytes=64)
-        for b in range(2):
-            nc.sync.dma_start(rough23[:, b, :], rough[(2 + b) * P : (3 + b) * P, :])
-            roughs.append(rough23[:, b, :])
-        wo_bf16 = sbuf.tile([P, 2, N, PACK], BF16, name="wo_bf16", tag="v_word1", align_bytes=64)
-        nc.scalar.copy(wo_bf16[:, 0], wo_raw[:].rearrange("p i n -> p n i"))
-        for half in range(2):
-            nc.sync.dma_start(
-                wo_bf16[half * P // 2 : (half + 1) * P // 2, 1], wo_bf16[(1 - half) * P // 2 : (2 - half) * P // 2, 0]
-            )
-        banks1 = open_sum(1, pages_b[1])
-        scatter(pages_a[0], idx2, h1[:, 0, :], gain1, 0, S)
-        close_slice(0, banks0)
-        banks2 = open_sum(2, pages_b[0])
-        scatter(pages_a[1], idx2, h1[:, 1, :], gain1, 0, S)
-        close_slice(1, banks1)
-        for c in range(CHUNKS):
-            turn_back(0, c, (0, 1), "acc", nc.scalar.copy)
-        scatter(pages_b[1], idx3, h2_23[:, 1, :], gain2, 0, S)
-        banks3 = open_sum(3, pages_b[1])
-        scatter(pages_a[0], idx2, h1[:, 2, :], gain1, 0, S)
-        close_slice(2, banks2)
-        scatter(pages_a[1], idx2, h1[:, 3, :], gain1, 0, S)
+                square(h1[t], "w1", t, h)
+        wo_bf16 = at(132 * KB, [P, N, PACK], BF16, "wo_bf16")
+        nc.scalar.copy(wo_bf16[:], wo_raw[:].rearrange("p i n -> p n i"))
+        banks1 = open_sum(1, "acc", pages_b[1])
+        scatter(pages_a[0], idx2, h1[0][:], gain1_01[:, 0, :], 0, S)
+        close_pair_slice(0, banks0)
+        banks2 = open_sum(2, "total", pages_b[0])
+        scatter(pages_a[1], idx2, h1[1][:], gain1_01[:, 1, :], 0, S)
+        gain2_3 = load_gain(wg2, 68 * KB, "gain2_3", 3, 4, 0, 2)
+        close_pair_slice(1, banks1)
+        turn_pair_back()
+        scatter(pages_a[0], idx2, h1[2][:], gain1_2[:, 0, :], 0, S)
+        gain1_3 = load_gain(wg1, 72 * KB, "gain1_3", 3, 4, 0, 2)
+        finish_slice_2(banks2)
+        banks3 = new_banks("total")
+        add_all(banks3, roughs[3], True, False)
+        scatter(pages_b[1], idx3, h2_23[1][:], gain2_3[:, 0, :], 0, S)
+        based = base_of_slice_3(banks3)
+        scatter(pages_a[1], idx2, h1[3][:], gain1_3[:, 0, :], 0, S)
 
-        wo_scale = sbuf.tile([P, 2, N], U8, name="wo_scale", align_bytes=64)
-        wo_word = sbuf.tile([P, 2, N], U32, name="wo_word", tag="h1", align_bytes=64)
-        for first, end in ((0, BANK), (BANK, 2 * N)):
-            nc.vector.quantize_mx(
-                out=wo_word[:].rearrange("p s n -> p (s n)")[:, first:end].bitcast(FP8X4),
-                scales=wo_scale[:].rearrange("p s n -> p (s n)")[:, first:end],
-                in_=wo_bf16[:].rearrange("p s n i -> p (s n i)")[:, PACK * first : PACK * end],
+        wo_scale = own([P, N], U8, "wo_scale")
+        wo_word = at(76 * KB, [P, N], U32, "wo_word")
+
+        def quantise_wo():
+            for first, end in ((0, 2 * P), (2 * P, N)):
+                nc.vector.quantize_mx(
+                    out=wo_word[:, first:end].bitcast(FP8X4),
+                    scales=wo_scale[:, first:end],
+                    in_=wo_bf16[:].rearrange("p n i -> p (n i)")[:, PACK * first : PACK * end],
+                )
+
+        def root(u):
+            first, width = UNITS[u]
+            total = at(112 * KB + 4 * first, [P, width], F32, f"total{u}")
+            inside = first % BANK
+            nc.vector.tensor_tensor(
+                total[:], based[first // BANK][:, inside : inside + width], pages_a[1][:, first : first + width], ADD
             )
-        quantised = []
-        for c in range(CHUNKS):
-            close_sum(SLICES - 1, c, banks3[c], pages_a[1])
-            quantised.append(quantise_chunk(c))
-            if c > 0:
-                multiply_chunk(c - 1, *quantised[c - 1])
-        multiply_chunk(CHUNKS - 1, *quantised[-1])
+            nc.scalar.activation(roots_of(u, 1, 1), total[:], ACT.Sqrt)
+
+        woven = {}
+        quantised = {}
+
+        def weave(u):
+            first, width = UNITS[u]
+            woven[u] = at(156 * KB + 8 * first, [P, width, 2], F32, f"woven{u}")
+            nc.vector.tensor_copy(woven[u][:], words[u][:].rearrange("p x m -> p m x"))
+
+        def quantise(u):
+            first, width = UNITS[u]
+            z_word = at(172 * KB + 4 * first, [P, width], U32, f"z_word{u}")
+            z_scale = own([P, width], U8, f"z_scale{u}")
+            nc.vector.quantize_mx(
+                out=z_word[:].bitcast(FP8X4),
+                scales=z_scale[:],
+                in_=woven[u][:].rearrange("p m x -> p (m x)").bitcast(BF16),
+            )
+            quantised[u] = (z_word, z_scale)
+
+        def multiply_unit(u, on_vector):
+            first, width = UNITS[u]
+            z_word, z_scale = quantised[u]
+            for g in range(GROUPS):
+                rows = slice(g * P, (g + 1) * P)
+                result = psum.tile([P, width], F32, name="total", tag="total")
+                nc.tensor.matmul_mx(
+                    out=result[:],
+                    lhsT=wo_word[:, rows].bitcast(FP8X4),
+                    lhsT_scale=wo_scale[:, rows],
+                    rhs=z_word[:].bitcast(FP8X4),
+                    rhs_scale=z_scale[:],
+                    start=True,
+                    stop=True,
+                )
+                place = (96 * KB, 104 * KB, 32 * KB)[g] + 4 * first
+                staged = at(place, [P, width], F32, f"staged{u}_{g}")
+                if g in on_vector:
+                    nc.vector.tensor_copy(staged[:], result[:])
+                else:
+                    nc.scalar.copy(staged[:], result[:])
+                nc.sync.dma_start(out[rows, first : first + width], staged[:])
+
+        root(0)
+        root(1)
+        quantise_wo()
+        weave(0)
+        root(2)
+        quantise(0)
+        weave(1)
+        root(3)
+        quantise(1)
+        multiply_unit(0, ())
+        weave(2)
+        root(4)
+        quantise(2)
+        multiply_unit(1, ())
+        weave(3)
+        multiply_unit(2, ())
+        quantise(3)
+        weave(4)
+        quantise(4)
+        multiply_unit(3, (1,))
+        multiply_unit(4, (0, 2))

@@ -130,7 +130,7 @@ def tile_list_inlet_speed_map_kernel(
         pages_a = []
         for b in range(2):
             page = at(8 * b * KB, [P, T2], F32, f"page_a{b}")
-            nc.vector.memset(page[:], 0.0)
+            nc.gpsimd.memset(page[:], 0.0)
             pages_a.append(page)
         for h in range(HALVES):
             entries = idx[:, h * BANK // PER_COLUMN : (h + 1) * BANK // PER_COLUMN]
@@ -340,7 +340,8 @@ def tile_list_inlet_speed_map_kernel(
             z_word, z_scale = quantised[u]
             for g in range(GROUPS):
                 rows = slice(g * P, (g + 1) * P)
-                result = psum.tile([P, width], F32, name="total", tag="total")
+                tag = "acc" if u in (2, 4) else "total"
+                result = psum.tile([P, width], F32, name=tag, tag=tag)
                 nc.tensor.matmul_mx(
                     out=result[:],
                     lhsT=wo_word[:, rows].bitcast(FP8X4),

@@ -54,20 +54,18 @@ def tile_list_inlet_speed_map_kernel(
         idx2 = sbuf.tile([P, S // PER_COLUMN], U16, name="idx2")
         idx3 = sbuf.tile([P, S // PER_COLUMN], U16, name="idx3")
         tab_scale = at(120 * KB, [P, T], U8, "tab_scale")
-        w4_scale_raw = own([P, PASSES, H], U8, "w4_scale_raw")
-        v_scale = own([P, PASSES, S], U8, "v_scale")
-        nc.gpsimd.memset(w4_scale_raw[:].rearrange("p a c -> p (a c)").bitcast(I32), 0)
+        w4_scale_raw = own([P, H], U8, "w4_scale_raw")
+        scales = own([P, PASSES, S + H], U8, "scales")
         nc.vector.memset(tab_scale[0 : P - QUADRANT, :].bitcast(I32), 0)
-        nc.vector.memset(v_scale[:].rearrange("p a c -> p (a c)").bitcast(I32), 0)
+        nc.vector.memset(w4_scale_raw[0 : P - QUADRANT, :].bitcast(I32), 0)
+        nc.vector.memset(scales[:].rearrange("p a c -> p (a c)").bitcast(I32), 0)
 
         tab_word = [at(16 * KB * a, [P, T], I32, f"tab_word{a}") for a in range(PASSES)]
         w4_raw = own([P, PASSES, 2 * H], U8, "w4_raw")
-        w4_scale_rows = w4_scales.bitcast(I32).rearrange("a (q j) c -> j q a c", j=SCALE_ROWS)
         nc.sync.dma_start(idx[:], offs)
         nc.sync.dma_start(tab_scale[P - QUADRANT : P, :].bitcast(I32), tab_scales.bitcast(I32).rearrange("a r t -> r a t"))
+        nc.sync.dma_start(w4_scale_raw[P - QUADRANT : P, :].bitcast(I32), w4_scales.bitcast(I32).rearrange("a r c -> r a c"))
         nc.sync.dma_start(w4_raw[:].bitcast(I32), w4_words.bitcast(I32).rearrange("a p c -> p a c"))
-        for j in range(SCALE_ROWS):
-            nc.sync.dma_start(w4_scale_raw[j:P:QUADRANT, :, :].bitcast(I32), w4_scale_rows[j])
         for a in range(PASSES):
             nc.sync.dma_start(tab_word[a][:], tab_words[a].rearrange("p t i -> p (t i)").bitcast(I32))
         nc.sync.dma_start(idx3[:], offs3)
@@ -104,21 +102,23 @@ def tile_list_inlet_speed_map_kernel(
         ident = sbuf.tile([P, P], F32, name="ident")
         make_identity(nc, ident[:])
 
-        w4_word = [at((144 + 8 * b) * KB, [P, 2, PASSES, 2 * P], U8, f"w4_word{b}") for b in range(2)]
-        w4_scale = own([P, SLICES, PASSES, P], U8, "w4_scale")
-        w4_by_slice = w4_raw[:].bitcast(U16).rearrange("p a (m t) -> p t a m", t=SLICES)
-        for b in range(2):
-            nc.vector.tensor_copy(w4_word[b][:].bitcast(U16), w4_by_slice[:, 2 * b : 2 * b + 2])
-        nc.vector.tensor_copy(w4_scale[:], w4_scale_raw[:].rearrange("p a (m t) -> p t a m", t=SLICES))
-
         picked_scale = own([P, S], U8, "picked_scale")
         nc.vector.tensor_copy(picked_scale[:], tab_scale[:].indirect(idx[:]))
+        joined = own([P, S + H], U8, "joined")
+        nc.vector.tensor_copy(
+            joined[:, S:].rearrange("p (t m) -> p t m", t=SLICES), w4_scale_raw[:].rearrange("p (m t) -> p t m", t=SLICES)
+        )
+        nc.vector.tensor_copy(joined[:, :S].bitcast(I32), picked_scale[:].bitcast(I32))
         rows_a_quadrant = PASSES * SCALE_ROWS
         for q in range(P // QUADRANT):
             nc.scalar.dma_start(
-                v_scale[q * QUADRANT : q * QUADRANT + SCALE_ROWS, :, :].bitcast(I32),
-                picked_scale[P - QUADRANT + q * rows_a_quadrant : P - QUADRANT + (q + 1) * rows_a_quadrant, :].bitcast(I32),
+                scales[q * QUADRANT : q * QUADRANT + SCALE_ROWS, :, :].bitcast(I32),
+                joined[P - QUADRANT + q * rows_a_quadrant : P - QUADRANT + (q + 1) * rows_a_quadrant, :].bitcast(I32),
             )
+        w4_word = [at((144 + 8 * b) * KB, [P, 2, PASSES, 2 * P], U8, f"w4_word{b}") for b in range(2)]
+        w4_by_slice = w4_raw[:].bitcast(U16).rearrange("p a (m t) -> p t a m", t=SLICES)
+        for b in range(2):
+            nc.vector.tensor_copy(w4_word[b][:].bitcast(U16), w4_by_slice[:, 2 * b : 2 * b + 2])
         pages_b = []
         for b in range(2):
             page = at((112 + 8 * b) * KB, [P, T2], F32, f"page_b{b}")
@@ -144,15 +144,15 @@ def tile_list_inlet_speed_map_kernel(
             passes = (0, 1) if (weight, t, h) == ("w4", 0, 0) else (1, 0)
             for a in passes:
                 if weight == "w1":
-                    codes, scales = w1_word[:, t, a, :].bitcast(FP8X4), w1_scale[:, t, a, :]
+                    codes, scale = w1_word[:, t, a, :].bitcast(FP8X4), w1_scale[:, t, a, :]
                 else:
-                    codes, scales = w4_word[t // 2][:, t % 2, a, :].bitcast(FP4X4), w4_scale[:, t, a, :]
+                    codes, scale = w4_word[t // 2][:, t % 2, a, :].bitcast(FP4X4), scales[:, a, S + t * P : S + (t + 1) * P]
                 nc.tensor.matmul_mx(
                     out=acc[:],
                     lhsT=codes,
-                    lhsT_scale=scales,
+                    lhsT_scale=scale,
                     rhs=v_word[a][:, cols].bitcast(FP8X4),
-                    rhs_scale=v_scale[:, a, cols],
+                    rhs_scale=scales[:, a, cols],
                     start=(a == passes[0]),
                     stop=(a == passes[-1]),
                 )
@@ -263,7 +263,7 @@ def tile_list_inlet_speed_map_kernel(
                 square(h2_23[b], "w4", 2 + b, h)
         banks0 = open_sum(0, "total", pages_b[0])
         w1_word = at(140 * KB, [P, SLICES, PASSES, P], U32, "w1_word")
-        for first, end in ((2, SLICES), (0, 2)):
+        for first, end in ((0, 2), (2, SLICES)):
             nc.vector.quantize_mx(
                 out=w1_word[:, first:end].rearrange("p t a c -> p (t a c)").bitcast(FP8X4),
                 scales=w1_scale[:, first:end].rearrange("p t a c -> p (t a c)"),
@@ -274,7 +274,7 @@ def tile_list_inlet_speed_map_kernel(
         scatter(pages_b[0], idx3, h2_23[0][:], gain2_2[:, 0, :], 0, S)
 
         h1 = [at((64 + 4 * t) * KB, [P, S], F32, f"h1_{t}") for t in range(SLICES)]
-        for t in (2, 3, 0, 1):
+        for t in range(SLICES):
             for h in range(HALVES):
                 square(h1[t], "w1", t, h)
         wo_bf16 = at(132 * KB, [P, N, PACK], BF16, "wo_bf16")
@@ -322,7 +322,9 @@ def tile_list_inlet_speed_map_kernel(
         def weave(u):
             first, width = UNITS[u]
             woven[u] = at(156 * KB + 8 * first, [P, width, 2], F32, f"woven{u}")
-            nc.vector.tensor_copy(woven[u][:], words[u][:].rearrange("p x m -> p m x"))
+            nc.vector.tensor_copy(
+                woven[u][:].rearrange("p (c i) x -> p c x i", i=4), words[u][:].rearrange("p x (c i) -> p c x i", i=4)
+            )
 
         def quantise(u):
             first, width = UNITS[u]

@@ -93,9 +93,9 @@ def tile_list_inlet_speed_map_kernel(
         rough_rows = rough.rearrange("(p t) m -> t p m", t=SLICES)
         roughs = [at((80 + 8 * t) * KB, [P, T2], F32, f"rough{t}") for t in range(SLICES)]
         nc.sync.dma_start(roughs[0][:], rough_rows[0])
-        gain1_01 = load_gain(wg1, 16 * KB, "gain1_01", 0, 2, 0, 2)
+        gain1_01 = load_gain(wg1, 0, "gain1_01", 0, 2, 0, 2)
         nc.sync.dma_start(roughs[1][:], rough_rows[1])
-        gain1_2 = load_gain(wg1, 24 * KB, "gain1_2", 2, 3, 0, 2)
+        gain1_2 = load_gain(wg1, 8 * KB, "gain1_2", 2, 3, 0, 2)
         nc.sync.dma_start(roughs[2][:], rough_rows[2])
         nc.sync.dma_start(roughs[3][:], rough_rows[3])
 
@@ -127,14 +127,15 @@ def tile_list_inlet_speed_map_kernel(
 
         v_word = [at((128 + 4 * a) * KB, [P, S], U32, f"v_word{a}") for a in range(PASSES)]
         nc.vector.tensor_copy(v_word[0][:], tab_word[0][:].bitcast(U32).indirect(idx[:]))
-        pages_a = []
-        for b in range(2):
-            page = at(8 * b * KB, [P, T2], F32, f"page_a{b}")
-            nc.gpsimd.memset(page[:], 0.0)
-            pages_a.append(page)
         for h in range(HALVES):
             entries = idx[:, h * BANK // PER_COLUMN : (h + 1) * BANK // PER_COLUMN]
             nc.vector.tensor_copy(v_word[1][:, h * BANK : (h + 1) * BANK], tab_word[1][:].bitcast(U32).indirect(entries))
+
+        pages_a = []
+        for b in range(2):
+            page = at((16 + 8 * b) * KB, [P, T2], F32, f"page_a{b}")
+            nc.gpsimd.memset(page[:], 0.0)
+            pages_a.append(page)
 
         w1_scale = own([P, SLICES, PASSES, P], U8, "w1_scale")
 

@@ -32,6 +32,7 @@ PER_COLUMN = 16
 QUADRANT = 32
 SCALE_ROWS = 4
 KB = 1024
+LEAD = 256
 UNITS = ((0, 256), (256, 256), (512, 512), (1024, 512), (1536, 512))
 
 
@@ -70,32 +71,33 @@ def tile_list_inlet_speed_map_kernel(
             nc.sync.dma_start(tab_word[a][:], tab_words[a].rearrange("p t i -> p (t i)").bitcast(I32))
         nc.sync.dma_start(idx3[:], offs3)
 
-        def load_gain(wg, offset, name, first, end, h_first, h_end):
-            cols = slice(h_first * BANK, h_end * BANK)
-            gain = at(offset, [P, end - first, (h_end - h_first) * BANK], F32, name)
+        def load_gain(wg, offset, name, first, end, j_first, j_end):
+            cols = slice(j_first, j_end)
+            gain = at(offset, [P, end - first, j_end - j_first], F32, name)
             rows = wg.rearrange("(p t) j -> p t j", t=SLICES)[:, first:end, cols]
             for q in (0, 2, 1, 3):
                 nc.sync.dma_start(gain[q * QUADRANT : (q + 1) * QUADRANT], rows)
             return gain
 
-        gain2_0a = load_gain(wg2, 32 * KB, "gain2_0a", 0, 1, 0, 1)
-        gain2_1a = load_gain(wg2, 34 * KB, "gain2_1a", 1, 2, 0, 1)
+        gain2_0a = load_gain(wg2, 32 * KB, "gain2_0a", 0, 1, 0, LEAD)
+        gain2_1a = load_gain(wg2, 33 * KB, "gain2_1a", 1, 2, 0, BANK)
+        gain2_0b = load_gain(wg2, 35 * KB, "gain2_0b", 0, 1, LEAD, S)
         w1_raw = [at((48 + 8 * a) * KB, [P, PACK, H], F32, f"w1_raw{a}") for a in range(PASSES)]
 
         def load_w1(a):
             nc.sync.dma_start(w1_raw[a][:], w1[a * K_PASS : (a + 1) * K_PASS, :].rearrange("(p i) c -> p i c", i=PACK))
 
         load_w1(0)
-        gain2_01b = load_gain(wg2, 36 * KB, "gain2_01b", 0, 2, 1, 2)
+        gain2_1b = load_gain(wg2, 38 * KB, "gain2_1b", 1, 2, BANK, S)
         load_w1(1)
         nc.sync.dma_start(idx2[:], offs2)
-        gain2_2 = load_gain(wg2, 40 * KB, "gain2_2", 2, 3, 0, 2)
+        gain2_2 = load_gain(wg2, 40 * KB, "gain2_2", 2, 3, 0, S)
         rough_rows = rough.rearrange("(p t) m -> t p m", t=SLICES)
         roughs = [at((80 + 8 * t) * KB, [P, T2], F32, f"rough{t}") for t in range(SLICES)]
         nc.sync.dma_start(roughs[0][:], rough_rows[0])
-        gain1_01 = load_gain(wg1, 0, "gain1_01", 0, 2, 0, 2)
+        gain1_01 = load_gain(wg1, 0, "gain1_01", 0, 2, 0, S)
         nc.sync.dma_start(roughs[1][:], rough_rows[1])
-        gain1_2 = load_gain(wg1, 8 * KB, "gain1_2", 2, 3, 0, 2)
+        gain1_2 = load_gain(wg1, 8 * KB, "gain1_2", 2, 3, 0, S)
         nc.sync.dma_start(roughs[2][:], rough_rows[2])
         nc.sync.dma_start(roughs[3][:], rough_rows[3])
 
@@ -142,7 +144,7 @@ def tile_list_inlet_speed_map_kernel(
         def multiply(weight, t, h):
             cols = slice(h * BANK, (h + 1) * BANK)
             acc = psum.tile([P, BANK], F32, name="acc", tag="acc")
-            passes = (0, 1) if (weight, t, h) == ("w4", 0, 0) else (1, 0)
+            passes = (1, 0)
             for a in passes:
                 if weight == "w1":
                     codes, scale = w1_word[:, t, a, :].bitcast(FP8X4), w1_scale[:, t, a, :]
@@ -161,6 +163,22 @@ def tile_list_inlet_speed_map_kernel(
 
         def square(values, weight, t, h):
             nc.scalar.activation(values[:, h * BANK : (h + 1) * BANK], multiply(weight, t, h)[:], ACT.Square)
+
+        def square_narrow(values, first, passes):
+            acc = psum.tile([P, LEAD], F32, name="acc", tag="acc")
+            for a in passes:
+                for j in range(0, LEAD, P):
+                    cols = slice(first + j, first + j + P)
+                    nc.tensor.matmul_mx(
+                        out=acc[:, j : j + P],
+                        lhsT=w4_word[0][:, 0, a, :].bitcast(FP4X4),
+                        lhsT_scale=scales[:, a, S : S + P],
+                        rhs=v_word[a][:, cols].bitcast(FP8X4),
+                        rhs_scale=scales[:, a, cols],
+                        start=(a == passes[0] and j == 0),
+                        stop=(a == passes[-1] and j == LEAD - P),
+                    )
+            nc.scalar.activation(values[:, first : first + LEAD], acc[:], ACT.Square)
 
         def scatter(page, offsets, values, gain, first, end):
             entries = offsets[:, first // PER_COLUMN : end // PER_COLUMN]
@@ -245,13 +263,15 @@ def tile_list_inlet_speed_map_kernel(
             return based
 
         h2_01 = [at((136 + 4 * t) * KB, [P, S], F32, f"h2_{t}") for t in range(2)]
-        for h in range(HALVES):
-            for t in range(2):
-                square(h2_01[t], "w4", t, h)
-        for t, gain in enumerate((gain2_0a, gain2_1a)):
-            scatter(pages_b[t], idx3, h2_01[t][:, :BANK], gain[:, 0, :], 0, BANK)
+        square_narrow(h2_01[0], 0, (0, 1))
+        square(h2_01[1], "w4", 1, 0)
+        square_narrow(h2_01[0], LEAD, (1, 0))
         for t in range(2):
-            scatter(pages_b[t], idx3, h2_01[t][:, BANK:], gain2_01b[:, t, :], BANK, S)
+            square(h2_01[t], "w4", t, 1)
+        scatter(pages_b[0], idx3, h2_01[0][:, :LEAD], gain2_0a[:, 0, :], 0, LEAD)
+        scatter(pages_b[1], idx3, h2_01[1][:, :BANK], gain2_1a[:, 0, :], 0, BANK)
+        scatter(pages_b[0], idx3, h2_01[0][:, LEAD:], gain2_0b[:, 0, :], LEAD, S)
+        scatter(pages_b[1], idx3, h2_01[1][:, BANK:], gain2_1b[:, 0, :], BANK, S)
         w1_bf16 = at(144 * KB, [P, SLICES, PASSES, P, PACK], BF16, "w1_bf16")
         for a in range(PASSES):
             nc.scalar.copy(
@@ -285,11 +305,11 @@ def tile_list_inlet_speed_map_kernel(
         close_pair_slice(0, banks0)
         banks2 = open_sum(2, "total", pages_b[0])
         scatter(pages_a[1], idx2, h1[1][:], gain1_01[:, 1, :], 0, S)
-        gain2_3 = load_gain(wg2, 68 * KB, "gain2_3", 3, 4, 0, 2)
+        gain2_3 = load_gain(wg2, 68 * KB, "gain2_3", 3, 4, 0, S)
         close_pair_slice(1, banks1)
         turn_pair_back()
         scatter(pages_a[0], idx2, h1[2][:], gain1_2[:, 0, :], 0, S)
-        gain1_3 = load_gain(wg1, 72 * KB, "gain1_3", 3, 4, 0, 2)
+        gain1_3 = load_gain(wg1, 72 * KB, "gain1_3", 3, 4, 0, S)
         finish_slice_2(banks2)
         banks3 = new_banks("total")
         add_all(banks3, roughs[3], True, False)
@@ -364,22 +384,22 @@ def tile_list_inlet_speed_map_kernel(
 
         root(0)
         root(1)
-        quantise_wo()
-        weave(0)
         root(2)
+        weave(0)
+        quantise_wo()
         quantise(0)
         weave(1)
-        root(3)
+        weave(2)
         quantise(1)
         multiply_unit(0, ())
-        weave(2)
-        root(4)
+        root(3)
         quantise(2)
         multiply_unit(1, ())
+        root(4)
         weave(3)
-        multiply_unit(2, ())
+        multiply_unit(2, (2,))
         quantise(3)
         weave(4)
+        multiply_unit(3, (2,))
         quantise(4)
-        multiply_unit(3, (1,))
-        multiply_unit(4, (0, 2))
+        multiply_unit(4, (1,))

@@ -59,7 +59,7 @@ def tile_list_inlet_speed_map_kernel(
         scales = own([P, PASSES, S + H], U8, "scales")
         nc.vector.memset(tab_scale[0 : P - QUADRANT, :].bitcast(I32), 0)
         nc.vector.memset(w4_scale_raw[0 : P - QUADRANT, :].bitcast(I32), 0)
-        nc.vector.memset(scales[:].rearrange("p a c -> p (a c)").bitcast(I32), 0)
+        nc.gpsimd.memset(scales[:].rearrange("p a c -> p (a c)").bitcast(I32), 0)
 
         tab_word = [at(16 * KB * a, [P, T], I32, f"tab_word{a}") for a in range(PASSES)]
         w4_raw = own([P, PASSES, 2 * H], U8, "w4_raw")
@@ -97,7 +97,7 @@ def tile_list_inlet_speed_map_kernel(
         nc.sync.dma_start(roughs[0][:], rough_rows[0])
         gain1_01 = load_gain(wg1, 0, "gain1_01", 0, 2, 0, S)
         nc.sync.dma_start(roughs[1][:], rough_rows[1])
-        gain1_2 = load_gain(wg1, 8 * KB, "gain1_2", 2, 3, 0, S)
+        gain1_2 = load_gain(wg1, 16 * KB, "gain1_2", 2, 3, 0, S)
         nc.sync.dma_start(roughs[2][:], rough_rows[2])
         nc.sync.dma_start(roughs[3][:], rough_rows[3])
 
@@ -129,15 +129,14 @@ def tile_list_inlet_speed_map_kernel(
 
         v_word = [at((128 + 4 * a) * KB, [P, S], U32, f"v_word{a}") for a in range(PASSES)]
         nc.vector.tensor_copy(v_word[0][:], tab_word[0][:].bitcast(U32).indirect(idx[:]))
+        pages_a = [at(8 * KB, [P, T2], F32, "page_a0")]
+        nc.vector.memset(pages_a[0][:], 0.0)
         for h in range(HALVES):
             entries = idx[:, h * BANK // PER_COLUMN : (h + 1) * BANK // PER_COLUMN]
             nc.vector.tensor_copy(v_word[1][:, h * BANK : (h + 1) * BANK], tab_word[1][:].bitcast(U32).indirect(entries))
 
-        pages_a = []
-        for b in range(2):
-            page = at((16 + 8 * b) * KB, [P, T2], F32, f"page_a{b}")
-            nc.gpsimd.memset(page[:], 0.0)
-            pages_a.append(page)
+        pages_a.append(at(24 * KB, [P, T2], F32, "page_a1"))
+        nc.gpsimd.memset(pages_a[1][:], 0.0)
 
         w1_scale = own([P, SLICES, PASSES, P], U8, "w1_scale")
 
@@ -283,7 +282,7 @@ def tile_list_inlet_speed_map_kernel(
             for h in range(HALVES):
                 square(h2_23[b], "w4", 2 + b, h)
         banks0 = open_sum(0, "total", pages_b[0])
-        w1_word = at(140 * KB, [P, SLICES, PASSES, P], U32, "w1_word")
+        w1_word = at(136 * KB, [P, SLICES, PASSES, P], U32, "w1_word")
         for first, end in ((0, 2), (2, SLICES)):
             nc.vector.quantize_mx(
                 out=w1_word[:, first:end].rearrange("p t a c -> p (t a c)").bitcast(FP8X4),

@@ -33,6 +33,7 @@ QUADRANT = 32
 SCALE_ROWS = 4
 KB = 1024
 LEAD = 256
+DIRECT = 2
 UNITS = ((0, 256), (256, 256), (512, 512), (1024, 512), (1536, 512))
 
 
@@ -207,12 +208,15 @@ def tile_list_inlet_speed_map_kernel(
             add_all(banks, roughs[t], False, False)
             return banks
 
-        words = [at(80 * KB + 8 * first, [P, 2, width], F32, f"words{first}") for first, width in UNITS]
+        words = {u: at(80 * KB + 8 * UNITS[u][0], [P, 2, UNITS[u][1]], F32, f"words{u}") for u in range(DIRECT, len(UNITS))}
+        woven = [at(156 * KB + 8 * first, [P, width, 2], F32, f"woven{first}") for first, width in UNITS]
 
         def units_of(c):
             return [(u, first - c * BANK, width) for u, (first, width) in enumerate(UNITS) if first // BANK == c]
 
         def roots_of(u, half, e):
+            if u < DIRECT:
+                return woven[u][:].rearrange("p m x -> p (m x)").bitcast(BF16).rearrange("p (m i) -> p m i", i=PACK)[:, :, 2 * half + e]
             return words[u][:, half, :].bitcast(BF16).rearrange("p (m e) -> p m e", e=2)[:, :, e]
 
         pair_t = [at((48 + 2 * c) * KB, [P, BANK], F32, f"pair_t{c}") for c in range(CHUNKS)]
@@ -230,7 +234,7 @@ def tile_list_inlet_speed_map_kernel(
                 for j in range(TILES):
                     nc.tensor.transpose(back[:, j * P : (j + 1) * P], pair_t[c][:, j * P : (j + 1) * P], ident[:])
                 for u, first, width in units_of(c):
-                    nc.scalar.copy(words[u][:, 0, :], back[:, first : first + width])
+                    nc.scalar.copy(woven[u][:, :, 0] if u < DIRECT else words[u][:, 0, :], back[:, first : first + width])
 
         def finish_slice_2(banks):
             for c in range(CHUNKS):
@@ -336,12 +340,9 @@ def tile_list_inlet_speed_map_kernel(
             )
             nc.scalar.activation(roots_of(u, 1, 1), total[:], ACT.Sqrt)
 
-        woven = {}
         quantised = {}
 
         def weave(u):
-            first, width = UNITS[u]
-            woven[u] = at(156 * KB + 8 * first, [P, width, 2], F32, f"woven{u}")
             nc.vector.tensor_copy(
                 woven[u][:].rearrange("p (c i) x -> p c x i", i=4), words[u][:].rearrange("p x (c i) -> p c x i", i=4)
             )
@@ -383,22 +384,20 @@ def tile_list_inlet_speed_map_kernel(
 
         root(0)
         root(1)
-        root(2)
-        weave(0)
         quantise_wo()
+        root(2)
         quantise(0)
-        weave(1)
-        weave(2)
-        quantise(1)
-        multiply_unit(0, ())
         root(3)
-        quantise(2)
-        multiply_unit(1, ())
+        quantise(1)
+        multiply_unit(0, (0,))
+        weave(2)
         root(4)
+        quantise(2)
         weave(3)
-        multiply_unit(2, (2,))
+        multiply_unit(1, (2,))
         quantise(3)
         weave(4)
-        multiply_unit(3, (2,))
+        multiply_unit(2, (2,))
         quantise(4)
+        multiply_unit(3, (2,))
         multiply_unit(4, (1,))

@@ -55,7 +55,7 @@ def tile_list_inlet_speed_map_kernel(
         idx = sbuf.tile([P, S // PER_COLUMN], U16, name="idx")
         idx2 = sbuf.tile([P, S // PER_COLUMN], U16, name="idx2")
         idx3 = sbuf.tile([P, S // PER_COLUMN], U16, name="idx3")
-        tab_scale = at(120 * KB, [P, T], U8, "tab_scale")
+        tab_scale = own([P, T], U8, "tab_scale")
         w4_scale_raw = own([P, H], U8, "w4_scale_raw")
         scales = own([P, PASSES, S + H], U8, "scales")
         nc.vector.memset(tab_scale[0 : P - QUADRANT, :].bitcast(I32), 0)
@@ -63,7 +63,7 @@ def tile_list_inlet_speed_map_kernel(
         nc.gpsimd.memset(scales[:].rearrange("p a c -> p (a c)").bitcast(I32), 0)
 
         tab_word = [at(16 * KB * a, [P, T], I32, f"tab_word{a}") for a in range(PASSES)]
-        w4_raw = own([P, PASSES, 2 * H], U8, "w4_raw")
+        w4_raw = at(184 * KB, [P, PASSES, 2 * H], U8, "w4_raw")
         nc.sync.dma_start(idx[:], offs)
         nc.sync.dma_start(tab_scale[P - QUADRANT : P, :].bitcast(I32), tab_scales.bitcast(I32).rearrange("a r t -> r a t"))
         nc.sync.dma_start(w4_scale_raw[P - QUADRANT : P, :].bitcast(I32), w4_scales.bitcast(I32).rearrange("a r c -> r a c"))
@@ -125,7 +125,7 @@ def tile_list_inlet_speed_map_kernel(
         pages_b = []
         for b in range(2):
             page = at((112 + 8 * b) * KB, [P, T2], F32, f"page_b{b}")
-            nc.vector.memset(page[:], 0.0)
+            (nc.vector, nc.gpsimd)[b].memset(page[:], 0.0)
             pages_b.append(page)
 
         v_word = [at((128 + 4 * a) * KB, [P, S], U32, f"v_word{a}") for a in range(PASSES)]
@@ -136,7 +136,7 @@ def tile_list_inlet_speed_map_kernel(
             entries = idx[:, h * BANK // PER_COLUMN : (h + 1) * BANK // PER_COLUMN]
             nc.vector.tensor_copy(v_word[1][:, h * BANK : (h + 1) * BANK], tab_word[1][:].bitcast(U32).indirect(entries))
 
-        pages_a.append(at(24 * KB, [P, T2], F32, "page_a1"))
+        pages_a.append(at(184 * KB, [P, T2], F32, "page_a1"))
         nc.gpsimd.memset(pages_a[1][:], 0.0)
 
         w1_scale = own([P, SLICES, PASSES, P], U8, "w1_scale")

@@ -253,18 +253,6 @@ def tile_list_inlet_speed_map_kernel(
                     xs = slice(first // (2 * P), (first + width) // (2 * P))
                     nc.scalar.copy(roots_of(u, 1, 0).rearrange("p (x e m) -> p x e m", e=2, m=P), cells[:, xs])
 
-        def base_of_slice_3(banks):
-            based = []
-            for c in range(CHUNKS):
-                add_transposed(banks[c], c, pages_b[1], False, True)
-                turned = at((48 + 2 * c) * KB, [P, BANK], F32, f"turned{c}")
-                nc.scalar.copy(turned[:], banks[c][:])
-                back = psum.tile([P, BANK], F32, name="acc", tag="acc")
-                for j in range(TILES):
-                    nc.tensor.transpose(back[:, j * P : (j + 1) * P], turned[:, j * P : (j + 1) * P], ident[:])
-                based.append(back)
-            return based
-
         h2_01 = [at((136 + 4 * t) * KB, [P, S], F32, f"h2_{t}") for t in range(2)]
         square_narrow(h2_01[0], 0, (0, 1))
         square(h2_01[1], "w4", 1, 0)
@@ -314,14 +302,15 @@ def tile_list_inlet_speed_map_kernel(
         scatter(pages_a[0], idx2, h1[2][:], gain1_2[:, 0, :], 0, S)
         gain1_3 = load_gain(wg1, 72 * KB, "gain1_3", 3, 4, 0, S)
         finish_slice_2(banks2)
-        banks3 = new_banks("total")
-        add_all(banks3, roughs[3], True, False)
         scatter(pages_b[1], idx3, h2_23[1][:], gain2_3[:, 0, :], 0, S)
-        based = base_of_slice_3(banks3)
-        scatter(pages_a[1], idx2, h1[3][:], gain1_3[:, 0, :], 0, S)
+        placed = at(68 * KB, [P, S], F32, "placed")
+        nc.vector.tensor_tensor(placed[:], h1[3][:], gain1_3[:, 0, :], MULT)
+        based = at(72 * KB, [P, T2], F32, "based")
+        nc.gpsimd.tensor_tensor(based[:], pages_b[1][:], roughs[3][:], ADD)
+        nc.vector.tensor_copy(pages_a[1][:].indirect(idx2[:]), placed[:])
 
         wo_scale = own([P, N], U8, "wo_scale")
-        wo_word = at(76 * KB, [P, N], U32, "wo_word")
+        wo_word = at(68 * KB, [P, N], U32, "wo_word")
 
         def quantise_wo():
             for first, end in ((0, 2 * P), (2 * P, N)):
@@ -334,10 +323,7 @@ def tile_list_inlet_speed_map_kernel(
         def root(u):
             first, width = UNITS[u]
             total = at(112 * KB + 4 * first, [P, width], F32, f"total{u}")
-            inside = first % BANK
-            nc.vector.tensor_tensor(
-                total[:], based[first // BANK][:, inside : inside + width], pages_a[1][:, first : first + width], ADD
-            )
+            nc.vector.tensor_tensor(total[:], based[:, first : first + width], pages_a[1][:, first : first + width], ADD)
             nc.scalar.activation(roots_of(u, 1, 1), total[:], ACT.Sqrt)
 
         quantised = {}

@@ -33,6 +33,7 @@ QUADRANT = 32
 SCALE_ROWS = 4
 KB = 1024
 LEAD = 256
+SECOND = 384
 DIRECT = 2
 UNITS = ((0, 256), (256, 256), (512, 512), (1024, 512), (1536, 512))
 
@@ -82,25 +83,32 @@ def tile_list_inlet_speed_map_kernel(
 
         gain2_0a = load_gain(wg2, 32 * KB, "gain2_0a", 0, 1, 0, LEAD)
         gain2_1a = load_gain(wg2, 33 * KB, "gain2_1a", 1, 2, 0, BANK)
+        gain2_2a = load_gain(wg2, 40 * KB, "gain2_2a", 2, 3, 0, LEAD)
         gain2_0b = load_gain(wg2, 35 * KB, "gain2_0b", 0, 1, LEAD, S)
+        gain2_1b = load_gain(wg2, 38 * KB, "gain2_1b", 1, 2, BANK, S)
+        gain2_3a = load_gain(wg2, 44 * KB, "gain2_3a", 3, 4, 0, SECOND)
         w1_raw = [at((48 + 8 * a) * KB, [P, PACK, H], F32, f"w1_raw{a}") for a in range(PASSES)]
 
         def load_w1(a):
             nc.sync.dma_start(w1_raw[a][:], w1[a * K_PASS : (a + 1) * K_PASS, :].rearrange("(p i) c -> p i c", i=PACK))
 
         load_w1(0)
-        gain2_1b = load_gain(wg2, 38 * KB, "gain2_1b", 1, 2, BANK, S)
         load_w1(1)
+        gain2_2b = load_gain(wg2, 41 * KB, "gain2_2b", 2, 3, LEAD, S)
         nc.sync.dma_start(idx2[:], offs2)
-        gain2_2 = load_gain(wg2, 40 * KB, "gain2_2", 2, 3, 0, S)
         rough_rows = rough.rearrange("(p t) m -> t p m", t=SLICES)
         roughs = [at((80 + 8 * t) * KB, [P, T2], F32, f"rough{t}") for t in range(SLICES)]
         nc.sync.dma_start(roughs[0][:], rough_rows[0])
-        gain1_01 = load_gain(wg1, 0, "gain1_01", 0, 2, 0, S)
+        gains1 = [load_gain(wg1, 0, "gain1_0", 0, 1, 0, S)]
         nc.sync.dma_start(roughs[1][:], rough_rows[1])
-        gain1_2 = load_gain(wg1, 16 * KB, "gain1_2", 2, 3, 0, S)
+        wo_raw = at(48 * KB, [P, PACK, N], F32, "wo_raw")
+        nc.sync.dma_start(wo_raw[:], wo.rearrange("(p i) n -> p i n", i=PACK))
+        gains1.append(load_gain(wg1, 4 * KB, "gain1_1", 1, 2, 0, S))
         nc.sync.dma_start(roughs[2][:], rough_rows[2])
+        gains1.append(load_gain(wg1, 16 * KB, "gain1_2", 2, 3, 0, S))
+        gain2_3b = load_gain(wg2, 45 * KB + 512, "gain2_3b", 3, 4, SECOND, S)
         nc.sync.dma_start(roughs[3][:], rough_rows[3])
+        gains1.append(load_gain(wg1, 20 * KB, "gain1_3", 3, 4, 0, S))
 
         ident = sbuf.tile([P, P], F32, name="ident")
         make_identity(nc, ident[:])
@@ -138,6 +146,8 @@ def tile_list_inlet_speed_map_kernel(
 
         pages_a.append(at(184 * KB, [P, T2], F32, "page_a1"))
         nc.gpsimd.memset(pages_a[1][:], 0.0)
+        pages_b.append(at(24 * KB, [P, T2], F32, "page_b2"))
+        nc.gpsimd.memset(pages_b[2][:], 0.0)
 
         w1_scale = own([P, SLICES, PASSES, P], U8, "w1_scale")
 
@@ -183,6 +193,17 @@ def tile_list_inlet_speed_map_kernel(
         def scatter(page, offsets, values, gain, first, end):
             entries = offsets[:, first // PER_COLUMN : end // PER_COLUMN]
             nc.vector.tensor_tensor(page[:].indirect(entries), values, gain, MULT)
+
+        def weigh(engine, offset, name, values, gain, piece=S):
+            width = values.shape[1]
+            weighted = at(offset, [P, width], F32, name)
+            for first in range(0, width, piece):
+                cols = slice(first, min(first + piece, width))
+                engine.tensor_tensor(weighted[:, cols], values[:, cols], gain[:, cols], MULT)
+            return weighted
+
+        def place(page, offsets, weighted, first, end):
+            nc.vector.tensor_copy(page[:].indirect(offsets[:, first // PER_COLUMN : end // PER_COLUMN]), weighted[:])
 
         def add_transposed(bank, c, rows, opens, closes):
             for j in range(TILES):
@@ -259,58 +280,63 @@ def tile_list_inlet_speed_map_kernel(
         square_narrow(h2_01[0], LEAD, (1, 0))
         for t in range(2):
             square(h2_01[t], "w4", t, 1)
+        h2_23 = [at((216, 220)[b] * KB, [P, S], F32, f"h2_{2 + b}") for b in range(2)]
+        for h in range(HALVES):
+            for b in range(2):
+                square(h2_23[b], "w4", 2 + b, h)
         scatter(pages_b[0], idx3, h2_01[0][:, :LEAD], gain2_0a[:, 0, :], 0, LEAD)
         scatter(pages_b[1], idx3, h2_01[1][:, :BANK], gain2_1a[:, 0, :], 0, BANK)
+        b2a = weigh(nc.vector, 192 * KB, "b2a", h2_23[0][:, :LEAD], gain2_2a[:, 0, :])
         scatter(pages_b[0], idx3, h2_01[0][:, LEAD:], gain2_0b[:, 0, :], LEAD, S)
         scatter(pages_b[1], idx3, h2_01[1][:, BANK:], gain2_1b[:, 0, :], BANK, S)
-        w1_bf16 = at(144 * KB, [P, SLICES, PASSES, P, PACK], BF16, "w1_bf16")
+        banks0 = new_banks("total")
+        add_all(banks0, pages_b[0], True, False)
+        w1_bf16 = at(208 * KB, [P, SLICES, PASSES, P, PACK], BF16, "w1_bf16")
         for a in range(PASSES):
             nc.scalar.copy(
                 w1_bf16[:, :, a, :, :].rearrange("p t m i -> p m t i"),
                 w1_raw[a][:].rearrange("p i (m t) -> p m t i", t=SLICES),
             )
-        h2_23 = [at((56 + 4 * b) * KB, [P, S], F32, f"h2_{2 + b}") for b in range(2)]
-        for b in range(2):
-            for h in range(HALVES):
-                square(h2_23[b], "w4", 2 + b, h)
-        banks0 = open_sum(0, "total", pages_b[0])
-        w1_word = at(136 * KB, [P, SLICES, PASSES, P], U32, "w1_word")
+        b3a = weigh(nc.gpsimd, 140 * KB, "b3a", h2_23[1][:, :SECOND], gain2_3a[:, 0, :])
+        b2b = weigh(nc.gpsimd, 141 * KB + 512, "b2b", h2_23[0][:, LEAD:], gain2_2b[:, 0, :])
+        place(pages_b[0], idx3, b2a, 0, LEAD)
+        place(pages_b[2], idx3, b3a, 0, SECOND)
+        w1_word = at(192 * KB, [P, SLICES, PASSES, P], U32, "w1_word")
         for first, end in ((0, 2), (2, SLICES)):
             nc.vector.quantize_mx(
                 out=w1_word[:, first:end].rearrange("p t a c -> p (t a c)").bitcast(FP8X4),
                 scales=w1_scale[:, first:end].rearrange("p t a c -> p (t a c)"),
                 in_=w1_bf16[:, first:end].rearrange("p t a c i -> p (t a c i)"),
             )
-        wo_raw = at(144 * KB, [P, PACK, N], F32, "wo_raw")
-        nc.sync.dma_start(wo_raw[:], wo.rearrange("(p i) n -> p i n", i=PACK))
-        scatter(pages_b[0], idx3, h2_23[0][:], gain2_2[:, 0, :], 0, S)
+        place(pages_b[0], idx3, b2b, LEAD, S)
+        add_all(banks0, roughs[0], False, False)
 
         h1 = [at((64 + 4 * t) * KB, [P, S], F32, f"h1_{t}") for t in range(SLICES)]
         for t in range(SLICES):
             for h in range(HALVES):
                 square(h1[t], "w1", t, h)
+        weighted1 = [weigh(nc.gpsimd, (196 + 4 * t) * KB, f"a{t}", h1[t][:], gains1[t][:, 0, :], BANK if t == 0 else S) for t in range(SLICES - 1)]
         wo_bf16 = at(132 * KB, [P, N, PACK], BF16, "wo_bf16")
         nc.scalar.copy(wo_bf16[:], wo_raw[:].rearrange("p i n -> p n i"))
         banks1 = open_sum(1, "acc", pages_b[1])
-        scatter(pages_a[0], idx2, h1[0][:], gain1_01[:, 0, :], 0, S)
+        place(pages_a[0], idx2, weighted1[0], 0, S)
         close_pair_slice(0, banks0)
         banks2 = open_sum(2, "total", pages_b[0])
-        scatter(pages_a[1], idx2, h1[1][:], gain1_01[:, 1, :], 0, S)
-        gain2_3 = load_gain(wg2, 68 * KB, "gain2_3", 3, 4, 0, S)
+        place(pages_a[1], idx2, weighted1[1], 0, S)
         close_pair_slice(1, banks1)
         turn_pair_back()
-        scatter(pages_a[0], idx2, h1[2][:], gain1_2[:, 0, :], 0, S)
-        gain1_3 = load_gain(wg1, 72 * KB, "gain1_3", 3, 4, 0, S)
+        place(pages_a[0], idx2, weighted1[2], 0, S)
+        b3b = weigh(nc.gpsimd, 112 * KB, "b3b", h2_23[1][:, SECOND:], gain2_3b[:, 0, :])
+        weighted1.append(weigh(nc.gpsimd, 220 * KB, "a3", h1[3][:], gains1[3][:, 0, :]))
         finish_slice_2(banks2)
-        scatter(pages_b[1], idx3, h2_23[1][:], gain2_3[:, 0, :], 0, S)
-        placed = at(68 * KB, [P, S], F32, "placed")
-        nc.vector.tensor_tensor(placed[:], h1[3][:], gain1_3[:, 0, :], MULT)
+        place(pages_b[2], idx3, b3b, SECOND, S)
         based = at(72 * KB, [P, T2], F32, "based")
-        nc.gpsimd.tensor_tensor(based[:], pages_b[1][:], roughs[3][:], ADD)
-        nc.vector.tensor_copy(pages_a[1][:].indirect(idx2[:]), placed[:])
+        nc.gpsimd.tensor_tensor(based[:], pages_b[2][:], roughs[3][:], ADD)
+        place(pages_a[1], idx2, weighted1[3], 0, S)
+        total = at(44 * KB, [P, T2], F32, "total")
 
         wo_scale = own([P, N], U8, "wo_scale")
-        wo_word = at(68 * KB, [P, N], U32, "wo_word")
+        wo_word = at(24 * KB, [P, N], U32, "wo_word")
 
         def quantise_wo():
             for first, end in ((0, 2 * P), (2 * P, N)):
@@ -322,9 +348,9 @@ def tile_list_inlet_speed_map_kernel(
 
         def root(u):
             first, width = UNITS[u]
-            total = at(112 * KB + 4 * first, [P, width], F32, f"total{u}")
-            nc.vector.tensor_tensor(total[:], based[:, first : first + width], pages_a[1][:, first : first + width], ADD)
-            nc.scalar.activation(roots_of(u, 1, 1), total[:], ACT.Sqrt)
+            cells = slice(first, first + width)
+            nc.vector.tensor_tensor(total[:, cells], based[:, cells], pages_a[1][:, cells], ADD)
+            nc.scalar.activation(roots_of(u, 1, 1), total[:, cells], ACT.Sqrt)
 
         quantised = {}
 
@@ -360,17 +386,17 @@ def tile_list_inlet_speed_map_kernel(
                     start=True,
                     stop=True,
                 )
-                place = (96 * KB, 104 * KB, 32 * KB)[g] + 4 * first
-                staged = at(place, [P, width], F32, f"staged{u}_{g}")
+                spot = (96 * KB, 104 * KB, 32 * KB)[g] + 4 * first
+                staged = at(spot, [P, width], F32, f"staged{u}_{g}")
                 if g in on_vector:
                     nc.vector.tensor_copy(staged[:], result[:])
                 else:
                     nc.scalar.copy(staged[:], result[:])
                 nc.sync.dma_start(out[rows, first : first + width], staged[:])
 
+        quantise_wo()
         root(0)
         root(1)
-        quantise_wo()
         root(2)
         quantise(0)
         root(3)

@@ -140,9 +140,9 @@ def tile_list_inlet_speed_map_kernel(
         nc.vector.tensor_copy(v_word[0][:], tab_word[0][:].bitcast(U32).indirect(idx[:]))
         pages_a = [at(8 * KB, [P, T2], F32, "page_a0")]
         nc.vector.memset(pages_a[0][:], 0.0)
-        for h in range(HALVES):
-            entries = idx[:, h * BANK // PER_COLUMN : (h + 1) * BANK // PER_COLUMN]
-            nc.vector.tensor_copy(v_word[1][:, h * BANK : (h + 1) * BANK], tab_word[1][:].bitcast(U32).indirect(entries))
+        for first, end in ((0, LEAD), (LEAD, BANK), (BANK, S)):
+            entries = idx[:, first // PER_COLUMN : end // PER_COLUMN]
+            nc.vector.tensor_copy(v_word[1][:, first:end], tab_word[1][:].bitcast(U32).indirect(entries))
 
         pages_a.append(at(184 * KB, [P, T2], F32, "page_a1"))
         nc.gpsimd.memset(pages_a[1][:], 0.0)
@@ -271,8 +271,11 @@ def tile_list_inlet_speed_map_kernel(
                     nc.tensor.transpose(back[:, x * P : (x + 1) * P], tiles_t[:, x * P : (x + 1) * P], ident[:])
                 cells = back[:].bitcast(BF16).rearrange("p (x m e) -> p x e m", x=2, e=2)
                 for u, first, width in units_of(c):
-                    xs = slice(first // (2 * P), (first + width) // (2 * P))
-                    nc.scalar.copy(roots_of(u, 1, 0).rearrange("p (x e m) -> p x e m", e=2, m=P), cells[:, xs])
+                    if width == P:
+                        nc.scalar.copy(roots_of(u, 1, 0), cells[:, first // (2 * P), first // P % 2, :])
+                    else:
+                        xs = slice(first // (2 * P), (first + width) // (2 * P))
+                        nc.scalar.copy(roots_of(u, 1, 0).rearrange("p (x e m) -> p x e m", e=2, m=P), cells[:, xs])
 
         h2_01 = [at((136 + 4 * t) * KB, [P, S], F32, f"h2_{t}") for t in range(2)]
         square_narrow(h2_01[0], 0, (0, 1))
@@ -333,28 +336,37 @@ def tile_list_inlet_speed_map_kernel(
         based = at(72 * KB, [P, T2], F32, "based")
         nc.gpsimd.tensor_tensor(based[:], pages_b[2][:], roughs[3][:], ADD)
         place(pages_a[1], idx2, weighted1[3], 0, S)
-        total = at(44 * KB, [P, T2], F32, "total")
+        early = at(44 * KB, [P, 2 * BANK], F32, "early")
+        late = [at(offset, [P, BANK], F32, f"late{offset}") for offset in (132 * KB, 156 * KB)]
+
+        def total_of(u):
+            first, width = UNITS[u]
+            return early[:, first : first + width] if first < 2 * BANK else late[first // BANK - 2][:]
 
         wo_scale = own([P, N], U8, "wo_scale")
         wo_word = at(24 * KB, [P, N], U32, "wo_word")
 
         def quantise_wo():
-            for first, end in ((0, 2 * P), (2 * P, N)):
+            for first, end in ((0, P), (P, N)):
                 nc.vector.quantize_mx(
                     out=wo_word[:, first:end].bitcast(FP8X4),
                     scales=wo_scale[:, first:end],
                     in_=wo_bf16[:].rearrange("p n i -> p (n i)")[:, PACK * first : PACK * end],
                 )
 
-        def root(u):
+        def add(u):
             first, width = UNITS[u]
             cells = slice(first, first + width)
-            nc.vector.tensor_tensor(total[:, cells], based[:, cells], pages_a[1][:, cells], ADD)
-            nc.scalar.activation(roots_of(u, 1, 1), total[:, cells], ACT.Sqrt)
+            nc.vector.tensor_tensor(total_of(u), based[:, cells], pages_a[1][:, cells], ADD)
+
+        def root(u):
+            nc.scalar.activation(roots_of(u, 1, 1), total_of(u), ACT.Sqrt)
 
         quantised = {}
 
         def weave(u):
+            if u < DIRECT:
+                return
             nc.vector.tensor_copy(
                 woven[u][:].rearrange("p (c i) x -> p c x i", i=4), words[u][:].rearrange("p x (c i) -> p c x i", i=4)
             )
@@ -370,12 +382,12 @@ def tile_list_inlet_speed_map_kernel(
             )
             quantised[u] = (z_word, z_scale)
 
-        def multiply_unit(u, on_vector):
+        def multiply_unit(u):
             first, width = UNITS[u]
             z_word, z_scale = quantised[u]
             for g in range(GROUPS):
                 rows = slice(g * P, (g + 1) * P)
-                tag = "acc" if u in (2, 4) else "total"
+                tag = ("acc", "total")[u % 2]
                 result = psum.tile([P, width], F32, name=tag, tag=tag)
                 nc.tensor.matmul_mx(
                     out=result[:],
@@ -388,28 +400,16 @@ def tile_list_inlet_speed_map_kernel(
                 )
                 spot = (96 * KB, 104 * KB, 32 * KB)[g] + 4 * first
                 staged = at(spot, [P, width], F32, f"staged{u}_{g}")
-                if g in on_vector:
+                if g == (1 if u == len(UNITS) - 1 else 2):
                     nc.vector.tensor_copy(staged[:], result[:])
                 else:
                     nc.scalar.copy(staged[:], result[:])
                 nc.sync.dma_start(out[rows, first : first + width], staged[:])
 
-        quantise_wo()
-        root(0)
-        root(1)
-        root(2)
-        quantise(0)
-        root(3)
-        quantise(1)
-        multiply_unit(0, (0,))
-        weave(2)
-        root(4)
-        quantise(2)
-        weave(3)
-        multiply_unit(1, (2,))
-        quantise(3)
-        weave(4)
-        multiply_unit(2, (2,))
-        quantise(4)
-        multiply_unit(3, (2,))
-        multiply_unit(4, (1,))
+        steps = ((quantise, 3), (add, 0), (weave, 2), (multiply_unit, 4), (root, 1))
+        for k in range(len(UNITS) + 4):
+            if k == 3:
+                quantise_wo()
+            for step, lag in steps:
+                if 0 <= k - lag < len(UNITS):
+                    step(k - lag)

@@ -68,9 +68,9 @@ def tile_list_inlet_speed_map_kernel(
         nc.sync.dma_start(idx[:], offs)
         nc.sync.dma_start(tab_scale[P - QUADRANT : P, :].bitcast(I32), tab_scales.bitcast(I32).rearrange("a r t -> r a t"))
         nc.sync.dma_start(w4_scale_raw[P - QUADRANT : P, :].bitcast(I32), w4_scales.bitcast(I32).rearrange("a r c -> r a c"))
-        nc.sync.dma_start(w4_raw[:].bitcast(I32), w4_words.bitcast(I32).rearrange("a p c -> p a c"))
         for a in range(PASSES):
             nc.sync.dma_start(tab_word[a][:], tab_words[a].rearrange("p t i -> p (t i)").bitcast(I32))
+        nc.sync.dma_start(w4_raw[:].bitcast(I32), w4_words.bitcast(I32).rearrange("a p c -> p a c"))
         nc.sync.dma_start(idx3[:], offs3)
 
         def load_gain(wg, offset, name, first, end, j_first, j_end):
@@ -128,8 +128,9 @@ def tile_list_inlet_speed_map_kernel(
             )
         w4_word = [at((144 + 8 * b) * KB, [P, 2, PASSES, 2 * P], U8, f"w4_word{b}") for b in range(2)]
         w4_by_slice = w4_raw[:].bitcast(U16).rearrange("p a (m t) -> p t a m", t=SLICES)
-        for b in range(2):
-            nc.vector.tensor_copy(w4_word[b][:].bitcast(U16), w4_by_slice[:, 2 * b : 2 * b + 2])
+        for t in range(2):
+            nc.scalar.copy(w4_word[0][:, t].bitcast(U16), w4_by_slice[:, t])
+        nc.scalar.copy(w4_word[1][:].bitcast(U16), w4_by_slice[:, 2:4])
         pages_b = []
         for b in range(2):
             page = at((112 + 8 * b) * KB, [P, T2], F32, f"page_b{b}")

@@ -56,7 +56,7 @@ def tile_list_inlet_speed_map_kernel(
         idx = sbuf.tile([P, S // PER_COLUMN], U16, name="idx")
         idx2 = sbuf.tile([P, S // PER_COLUMN], U16, name="idx2")
         idx3 = sbuf.tile([P, S // PER_COLUMN], U16, name="idx3")
-        tab_scale = own([P, T], U8, "tab_scale")
+        tab_scale = at(112 * KB, [P, T], U8, "tab_scale")
         w4_scale_raw = own([P, H], U8, "w4_scale_raw")
         scales = own([P, PASSES, S + H], U8, "scales")
         nc.vector.memset(tab_scale[0 : P - QUADRANT, :].bitcast(I32), 0)

@@ -33,7 +33,6 @@ QUADRANT = 32
 SCALE_ROWS = 4
 KB = 1024
 LEAD = 256
-SECOND = 384
 DIRECT = 2
 UNITS = ((0, 256), (256, 256), (512, 512), (1024, 512), (1536, 512))
 
@@ -73,42 +72,46 @@ def tile_list_inlet_speed_map_kernel(
         nc.sync.dma_start(w4_raw[:].bitcast(I32), w4_words.bitcast(I32).rearrange("a p c -> p a c"))
         nc.sync.dma_start(idx3[:], offs3)
 
-        def load_gain(wg, offset, name, first, end, j_first, j_end):
-            cols = slice(j_first, j_end)
-            gain = at(offset, [P, end - first, j_end - j_first], F32, name)
-            rows = wg.rearrange("(p t) j -> p t j", t=SLICES)[:, first:end, cols]
-            for q in (0, 2, 1, 3):
+        def load_quadrants(gain, wg, t, j_first, quadrants):
+            rows = wg.rearrange("(p t) j -> p t j", t=SLICES)[:, t : t + 1, j_first : j_first + gain.shape[2]]
+            for q in quadrants:
                 nc.sync.dma_start(gain[q * QUADRANT : (q + 1) * QUADRANT], rows)
+
+        def load_gain(wg, offset, name, first, end, j_first, j_end, quadrants=(0, 2, 1, 3)):
+            gain = at(offset, [P, end - first, j_end - j_first], F32, name)
+            load_quadrants(gain, wg, first, j_first, quadrants)
             return gain
 
-        gain2_0a = load_gain(wg2, 32 * KB, "gain2_0a", 0, 1, 0, LEAD)
-        gain2_1a = load_gain(wg2, 33 * KB, "gain2_1a", 1, 2, 0, BANK)
-        gain2_2a = load_gain(wg2, 40 * KB, "gain2_2a", 2, 3, 0, LEAD)
-        gain2_0b = load_gain(wg2, 35 * KB, "gain2_0b", 0, 1, LEAD, S)
-        gain2_1b = load_gain(wg2, 38 * KB, "gain2_1b", 1, 2, BANK, S)
-        gain2_3a = load_gain(wg2, 44 * KB, "gain2_3a", 3, 4, 0, SECOND)
         w1_raw = [at((48 + 8 * a) * KB, [P, PACK, H], F32, f"w1_raw{a}") for a in range(PASSES)]
+        rough_rows = rough.rearrange("(p t) m -> t p m", t=SLICES)
+        roughs = [at((80 + 8 * t) * KB, [P, T2], F32, f"rough{t}") for t in range(SLICES)]
 
         def load_w1(a):
             nc.sync.dma_start(w1_raw[a][:], w1[a * K_PASS : (a + 1) * K_PASS, :].rearrange("(p i) c -> p i c", i=PACK))
 
+        gain2_0a = load_gain(wg2, 32 * KB, "gain2_0a", 0, 1, 0, LEAD)
+        gain2_1a = load_gain(wg2, 33 * KB, "gain2_1a", 1, 2, 0, BANK)
+        gain2_0b = load_gain(wg2, 35 * KB, "gain2_0b", 0, 1, LEAD, S)
         load_w1(0)
+        gain2_1b = load_gain(wg2, 38 * KB, "gain2_1b", 1, 2, BANK, S)
         load_w1(1)
-        gain2_2b = load_gain(wg2, 41 * KB, "gain2_2b", 2, 3, LEAD, S)
+        gain2_2a = load_gain(wg2, 40 * KB, "gain2_2a", 2, 3, 0, BANK)
         nc.sync.dma_start(idx2[:], offs2)
-        rough_rows = rough.rearrange("(p t) m -> t p m", t=SLICES)
-        roughs = [at((80 + 8 * t) * KB, [P, T2], F32, f"rough{t}") for t in range(SLICES)]
         nc.sync.dma_start(roughs[0][:], rough_rows[0])
-        gains1 = [load_gain(wg1, 0, "gain1_0", 0, 1, 0, S)]
+        gain2_2b = load_gain(wg2, 56 * KB, "gain2_2b", 2, 3, BANK, S)
+        gain1_0 = load_gain(wg1, 0, "gain1_0", 0, 1, 0, S)
         nc.sync.dma_start(roughs[1][:], rough_rows[1])
         wo_raw = at(48 * KB, [P, PACK, N], F32, "wo_raw")
         nc.sync.dma_start(wo_raw[:], wo.rearrange("(p i) n -> p i n", i=PACK))
-        gains1.append(load_gain(wg1, 4 * KB, "gain1_1", 1, 2, 0, S))
+        gain1_1 = load_gain(wg1, 4 * KB, "gain1_1", 1, 2, 0, S)
         nc.sync.dma_start(roughs[2][:], rough_rows[2])
-        gains1.append(load_gain(wg1, 16 * KB, "gain1_2", 2, 3, 0, S))
-        gain2_3b = load_gain(wg2, 45 * KB + 512, "gain2_3b", 3, 4, SECOND, S)
+        gain1_2b = load_gain(wg1, 16 * KB, "gain1_2b", 2, 3, S - LEAD, S)
+        gain2_3a = load_gain(wg2, 20 * KB, "gain2_3a", 3, 4, 0, BANK, (0, 2, 1))
+        gain1_2a = load_gain(wg1, 17 * KB, "gain1_2a", 2, 3, 0, S - LEAD)
+        load_quadrants(gain2_3a, wg2, 3, 0, (3,))
+        gain2_3b = load_gain(wg2, 22 * KB, "gain2_3b", 3, 4, BANK, S)
         nc.sync.dma_start(roughs[3][:], rough_rows[3])
-        gains1.append(load_gain(wg1, 20 * KB, "gain1_3", 3, 4, 0, S))
+        gain1_3 = load_gain(wg1, 32 * KB, "gain1_3", 3, 4, 0, S)
 
         ident = sbuf.tile([P, P], F32, name="ident")
         make_identity(nc, ident[:])
@@ -260,7 +263,7 @@ def tile_list_inlet_speed_map_kernel(
 
         def finish_slice_2(banks):
             for c in range(CHUNKS):
-                add_transposed(banks[c], c, pages_a[0], False, True)
+                add_transposed(banks[c], c, pages_a[2], False, True)
                 tiles_t = at((44 + c) * KB, [P, BANK // 2], F32, f"tiles_t{c}")
                 nc.scalar.activation(
                     tiles_t[:].bitcast(BF16).rearrange("m (x p e) -> m x p e", x=2, e=2),
@@ -288,9 +291,10 @@ def tile_list_inlet_speed_map_kernel(
         for h in range(HALVES):
             for b in range(2):
                 square(h2_23[b], "w4", 2 + b, h)
+        pages_a.append(at(144 * KB, [P, T2], F32, "page_a2"))
+        nc.gpsimd.memset(pages_a[2][:], 0.0)
         scatter(pages_b[0], idx3, h2_01[0][:, :LEAD], gain2_0a[:, 0, :], 0, LEAD)
         scatter(pages_b[1], idx3, h2_01[1][:, :BANK], gain2_1a[:, 0, :], 0, BANK)
-        b2a = weigh(nc.vector, 192 * KB, "b2a", h2_23[0][:, :LEAD], gain2_2a[:, 0, :])
         scatter(pages_b[0], idx3, h2_01[0][:, LEAD:], gain2_0b[:, 0, :], LEAD, S)
         scatter(pages_b[1], idx3, h2_01[1][:, BANK:], gain2_1b[:, 0, :], BANK, S)
         banks0 = new_banks("total")
@@ -301,42 +305,41 @@ def tile_list_inlet_speed_map_kernel(
                 w1_bf16[:, :, a, :, :].rearrange("p t m i -> p m t i"),
                 w1_raw[a][:].rearrange("p i (m t) -> p m t i", t=SLICES),
             )
-        b3a = weigh(nc.gpsimd, 140 * KB, "b3a", h2_23[1][:, :SECOND], gain2_3a[:, 0, :])
-        b2b = weigh(nc.gpsimd, 141 * KB + 512, "b2b", h2_23[0][:, LEAD:], gain2_2b[:, 0, :])
-        place(pages_b[0], idx3, b2a, 0, LEAD)
-        place(pages_b[2], idx3, b3a, 0, SECOND)
-        w1_word = at(192 * KB, [P, SLICES, PASSES, P], U32, "w1_word")
+        scatter(pages_b[0], idx3, h2_23[0][:, :BANK], gain2_2a[:, 0, :], 0, BANK)
+        w1_word = at(40 * KB, [P, SLICES, PASSES, P], U32, "w1_word")
         for first, end in ((0, 2), (2, SLICES)):
             nc.vector.quantize_mx(
                 out=w1_word[:, first:end].rearrange("p t a c -> p (t a c)").bitcast(FP8X4),
                 scales=w1_scale[:, first:end].rearrange("p t a c -> p (t a c)"),
                 in_=w1_bf16[:, first:end].rearrange("p t a c i -> p (t a c i)"),
             )
-        place(pages_b[0], idx3, b2b, LEAD, S)
+        scatter(pages_b[0], idx3, h2_23[0][:, BANK:], gain2_2b[:, 0, :], BANK, S)
         add_all(banks0, roughs[0], False, False)
 
         h1 = [at((64 + 4 * t) * KB, [P, S], F32, f"h1_{t}") for t in range(SLICES)]
         for t in range(SLICES):
             for h in range(HALVES):
                 square(h1[t], "w1", t, h)
-        weighted1 = [weigh(nc.gpsimd, (196 + 4 * t) * KB, f"a{t}", h1[t][:], gains1[t][:, 0, :], BANK if t == 0 else S) for t in range(SLICES - 1)]
         wo_bf16 = at(132 * KB, [P, N, PACK], BF16, "wo_bf16")
         nc.scalar.copy(wo_bf16[:], wo_raw[:].rearrange("p i n -> p n i"))
         banks1 = open_sum(1, "acc", pages_b[1])
-        place(pages_a[0], idx2, weighted1[0], 0, S)
+        scatter(pages_a[0], idx2, h1[0][:], gain1_0[:, 0, :], 0, S)
         close_pair_slice(0, banks0)
         banks2 = open_sum(2, "total", pages_b[0])
-        place(pages_a[1], idx2, weighted1[1], 0, S)
+        a2b = weigh(nc.vector, 196 * KB, "a2b", h1[2][:, S - LEAD :], gain1_2b[:, 0, :])
+        scatter(pages_a[1], idx2, h1[1][:], gain1_1[:, 0, :], 0, S)
         close_pair_slice(1, banks1)
         turn_pair_back()
-        place(pages_a[0], idx2, weighted1[2], 0, S)
-        b3b = weigh(nc.gpsimd, 112 * KB, "b3b", h2_23[1][:, SECOND:], gain2_3b[:, 0, :])
-        weighted1.append(weigh(nc.gpsimd, 220 * KB, "a3", h1[3][:], gains1[3][:, 0, :]))
+        scatter(pages_a[2], idx2, h1[2][:, : S - LEAD], gain1_2a[:, 0, :], 0, S - LEAD)
+        scatter(pages_b[2], idx3, h2_23[1][:, :BANK], gain2_3a[:, 0, :], 0, BANK)
+        b3b = weigh(nc.gpsimd, 19 * KB, "b3b", h2_23[1][:, BANK:], gain2_3b[:, 0, :])
+        a3 = weigh(nc.gpsimd, 220 * KB, "a3", h1[3][:], gain1_3[:, 0, :])
+        place(pages_a[2], idx2, a2b, S - LEAD, S)
         finish_slice_2(banks2)
-        place(pages_b[2], idx3, b3b, SECOND, S)
+        place(pages_b[2], idx3, b3b, BANK, S)
         based = at(72 * KB, [P, T2], F32, "based")
         nc.gpsimd.tensor_tensor(based[:], pages_b[2][:], roughs[3][:], ADD)
-        place(pages_a[1], idx2, weighted1[3], 0, S)
+        place(pages_a[1], idx2, a3, 0, S)
         early = at(44 * KB, [P, 2 * BANK], F32, "early")
         late = [at(offset, [P, BANK], F32, f"late{offset}") for offset in (132 * KB, 156 * KB)]
 

@@ -95,10 +95,9 @@ def tile_list_inlet_speed_map_kernel(
         load_w1(0)
         gain2_1b = load_gain(wg2, 38 * KB, "gain2_1b", 1, 2, BANK, S)
         load_w1(1)
-        gain2_2a = load_gain(wg2, 40 * KB, "gain2_2a", 2, 3, 0, BANK)
+        gain2_2 = load_gain(wg2, 40 * KB, "gain2_2", 2, 3, 0, S)
         nc.sync.dma_start(idx2[:], offs2)
         nc.sync.dma_start(roughs[0][:], rough_rows[0])
-        gain2_2b = load_gain(wg2, 56 * KB, "gain2_2b", 2, 3, BANK, S)
         gain1_0 = load_gain(wg1, 0, "gain1_0", 0, 1, 0, S)
         nc.sync.dma_start(roughs[1][:], rough_rows[1])
         wo_raw = at(48 * KB, [P, PACK, N], F32, "wo_raw")
@@ -289,8 +288,7 @@ def tile_list_inlet_speed_map_kernel(
             square(h2_01[t], "w4", t, 1)
         h2_23 = [at((216, 220)[b] * KB, [P, S], F32, f"h2_{2 + b}") for b in range(2)]
         for h in range(HALVES):
-            for b in range(2):
-                square(h2_23[b], "w4", 2 + b, h)
+            square(h2_23[0], "w4", 2, h)
         pages_a.append(at(144 * KB, [P, T2], F32, "page_a2"))
         nc.gpsimd.memset(pages_a[2][:], 0.0)
         scatter(pages_b[0], idx3, h2_01[0][:, :LEAD], gain2_0a[:, 0, :], 0, LEAD)
@@ -305,15 +303,15 @@ def tile_list_inlet_speed_map_kernel(
                 w1_bf16[:, :, a, :, :].rearrange("p t m i -> p m t i"),
                 w1_raw[a][:].rearrange("p i (m t) -> p m t i", t=SLICES),
             )
-        scatter(pages_b[0], idx3, h2_23[0][:, :BANK], gain2_2a[:, 0, :], 0, BANK)
-        w1_word = at(40 * KB, [P, SLICES, PASSES, P], U32, "w1_word")
-        for first, end in ((0, 2), (2, SLICES)):
-            nc.vector.quantize_mx(
-                out=w1_word[:, first:end].rearrange("p t a c -> p (t a c)").bitcast(FP8X4),
-                scales=w1_scale[:, first:end].rearrange("p t a c -> p (t a c)"),
-                in_=w1_bf16[:, first:end].rearrange("p t a c i -> p (t a c i)"),
-            )
-        scatter(pages_b[0], idx3, h2_23[0][:, BANK:], gain2_2b[:, 0, :], BANK, S)
+        for h in range(HALVES):
+            square(h2_23[1], "w4", 3, h)
+        w1_word = at(192 * KB, [P, SLICES, PASSES, P], U32, "w1_word")
+        nc.vector.quantize_mx(
+            out=w1_word[:].rearrange("p t a c -> p (t a c)").bitcast(FP8X4),
+            scales=w1_scale[:].rearrange("p t a c -> p (t a c)"),
+            in_=w1_bf16[:].rearrange("p t a c i -> p (t a c i)"),
+        )
+        scatter(pages_b[0], idx3, h2_23[0][:], gain2_2[:, 0, :], 0, S)
         add_all(banks0, roughs[0], False, False)
 
         h1 = [at((64 + 4 * t) * KB, [P, S], F32, f"h1_{t}") for t in range(SLICES)]

@@ -94,15 +94,16 @@ def tile_list_inlet_speed_map_kernel(
         gain2_0b = load_gain(wg2, 35 * KB, "gain2_0b", 0, 1, LEAD, S)
         load_w1(0)
         gain2_1b = load_gain(wg2, 38 * KB, "gain2_1b", 1, 2, BANK, S)
+        gain2_2a = load_gain(wg2, 40 * KB, "gain2_2a", 2, 3, 0, BANK)
         load_w1(1)
-        gain2_2 = load_gain(wg2, 40 * KB, "gain2_2", 2, 3, 0, S)
         nc.sync.dma_start(idx2[:], offs2)
         nc.sync.dma_start(roughs[0][:], rough_rows[0])
+        gain2_2b = load_gain(wg2, 42 * KB, "gain2_2b", 2, 3, BANK, S)
         gain1_0 = load_gain(wg1, 0, "gain1_0", 0, 1, 0, S)
         nc.sync.dma_start(roughs[1][:], rough_rows[1])
+        gain1_1 = load_gain(wg1, 4 * KB, "gain1_1", 1, 2, 0, S)
         wo_raw = at(48 * KB, [P, PACK, N], F32, "wo_raw")
         nc.sync.dma_start(wo_raw[:], wo.rearrange("(p i) n -> p i n", i=PACK))
-        gain1_1 = load_gain(wg1, 4 * KB, "gain1_1", 1, 2, 0, S)
         nc.sync.dma_start(roughs[2][:], rough_rows[2])
         gain1_2b = load_gain(wg1, 16 * KB, "gain1_2b", 2, 3, S - LEAD, S)
         gain2_3a = load_gain(wg2, 20 * KB, "gain2_3a", 3, 4, 0, BANK, (0, 2, 1))
@@ -288,13 +289,16 @@ def tile_list_inlet_speed_map_kernel(
             square(h2_01[t], "w4", t, 1)
         h2_23 = [at((216, 220)[b] * KB, [P, S], F32, f"h2_{2 + b}") for b in range(2)]
         for h in range(HALVES):
-            square(h2_23[0], "w4", 2, h)
-        pages_a.append(at(144 * KB, [P, T2], F32, "page_a2"))
-        nc.gpsimd.memset(pages_a[2][:], 0.0)
+            for b in range(2):
+                square(h2_23[b], "w4", 2 + b, h)
+        page_b_late = at(144 * KB, [P, T2], F32, "page_b_late")
+        nc.gpsimd.memset(page_b_late[:], 0.0)
         scatter(pages_b[0], idx3, h2_01[0][:, :LEAD], gain2_0a[:, 0, :], 0, LEAD)
         scatter(pages_b[1], idx3, h2_01[1][:, :BANK], gain2_1a[:, 0, :], 0, BANK)
         scatter(pages_b[0], idx3, h2_01[0][:, LEAD:], gain2_0b[:, 0, :], LEAD, S)
         scatter(pages_b[1], idx3, h2_01[1][:, BANK:], gain2_1b[:, 0, :], BANK, S)
+        pages_a.append(at(136 * KB, [P, T2], F32, "page_a2"))
+        nc.gpsimd.memset(pages_a[2][:], 0.0)
         banks0 = new_banks("total")
         add_all(banks0, pages_b[0], True, False)
         w1_bf16 = at(208 * KB, [P, SLICES, PASSES, P, PACK], BF16, "w1_bf16")
@@ -303,27 +307,27 @@ def tile_list_inlet_speed_map_kernel(
                 w1_bf16[:, :, a, :, :].rearrange("p t m i -> p m t i"),
                 w1_raw[a][:].rearrange("p i (m t) -> p m t i", t=SLICES),
             )
-        for h in range(HALVES):
-            square(h2_23[1], "w4", 3, h)
+        scatter(page_b_late, idx3, h2_23[0][:, :BANK], gain2_2a[:, 0, :], 0, BANK)
         w1_word = at(192 * KB, [P, SLICES, PASSES, P], U32, "w1_word")
-        nc.vector.quantize_mx(
-            out=w1_word[:].rearrange("p t a c -> p (t a c)").bitcast(FP8X4),
-            scales=w1_scale[:].rearrange("p t a c -> p (t a c)"),
-            in_=w1_bf16[:].rearrange("p t a c i -> p (t a c i)"),
-        )
-        scatter(pages_b[0], idx3, h2_23[0][:], gain2_2[:, 0, :], 0, S)
-        add_all(banks0, roughs[0], False, False)
+        for first, end in ((0, 2), (2, SLICES)):
+            nc.vector.quantize_mx(
+                out=w1_word[:, first:end].rearrange("p t a c -> p (t a c)").bitcast(FP8X4),
+                scales=w1_scale[:, first:end].rearrange("p t a c -> p (t a c)"),
+                in_=w1_bf16[:, first:end].rearrange("p t a c i -> p (t a c i)"),
+            )
+        scatter(page_b_late, idx3, h2_23[0][:, BANK:], gain2_2b[:, 0, :], BANK, S)
 
         h1 = [at((64 + 4 * t) * KB, [P, S], F32, f"h1_{t}") for t in range(SLICES)]
         for t in range(SLICES):
             for h in range(HALVES):
                 square(h1[t], "w1", t, h)
+        add_all(banks0, roughs[0], False, False)
         wo_bf16 = at(132 * KB, [P, N, PACK], BF16, "wo_bf16")
         nc.scalar.copy(wo_bf16[:], wo_raw[:].rearrange("p i n -> p n i"))
         banks1 = open_sum(1, "acc", pages_b[1])
         scatter(pages_a[0], idx2, h1[0][:], gain1_0[:, 0, :], 0, S)
         close_pair_slice(0, banks0)
-        banks2 = open_sum(2, "total", pages_b[0])
+        banks2 = open_sum(2, "total", page_b_late)
         a2b = weigh(nc.vector, 196 * KB, "a2b", h1[2][:, S - LEAD :], gain1_2b[:, 0, :])
         scatter(pages_a[1], idx2, h1[1][:], gain1_1[:, 0, :], 0, S)
         close_pair_slice(1, banks1)

@@ -33,6 +33,7 @@ QUADRANT = 32
 SCALE_ROWS = 4
 KB = 1024
 LEAD = 256
+LAST = 320
 DIRECT = 2
 UNITS = ((0, 256), (256, 256), (512, 512), (1024, 512), (1536, 512))
 
@@ -105,9 +106,9 @@ def tile_list_inlet_speed_map_kernel(
         wo_raw = at(48 * KB, [P, PACK, N], F32, "wo_raw")
         nc.sync.dma_start(wo_raw[:], wo.rearrange("(p i) n -> p i n", i=PACK))
         nc.sync.dma_start(roughs[2][:], rough_rows[2])
-        gain1_2b = load_gain(wg1, 16 * KB, "gain1_2b", 2, 3, S - LEAD, S)
+        gain1_2b = load_gain(wg1, 16 * KB, "gain1_2b", 2, 3, S - LAST, S)
         gain2_3a = load_gain(wg2, 20 * KB, "gain2_3a", 3, 4, 0, BANK, (0, 2, 1))
-        gain1_2a = load_gain(wg1, 17 * KB, "gain1_2a", 2, 3, 0, S - LEAD)
+        gain1_2a = load_gain(wg1, 16 * KB + 4 * LAST, "gain1_2a", 2, 3, 0, S - LAST)
         load_quadrants(gain2_3a, wg2, 3, 0, (3,))
         gain2_3b = load_gain(wg2, 22 * KB, "gain2_3b", 3, 4, BANK, S)
         nc.sync.dma_start(roughs[3][:], rough_rows[3])
@@ -328,15 +329,15 @@ def tile_list_inlet_speed_map_kernel(
         scatter(pages_a[0], idx2, h1[0][:], gain1_0[:, 0, :], 0, S)
         close_pair_slice(0, banks0)
         banks2 = open_sum(2, "total", page_b_late)
-        a2b = weigh(nc.vector, 196 * KB, "a2b", h1[2][:, S - LEAD :], gain1_2b[:, 0, :])
+        a2b = weigh(nc.vector, 196 * KB, "a2b", h1[2][:, S - LAST :], gain1_2b[:, 0, :])
         scatter(pages_a[1], idx2, h1[1][:], gain1_1[:, 0, :], 0, S)
         close_pair_slice(1, banks1)
         turn_pair_back()
-        scatter(pages_a[2], idx2, h1[2][:, : S - LEAD], gain1_2a[:, 0, :], 0, S - LEAD)
+        scatter(pages_a[2], idx2, h1[2][:, : S - LAST], gain1_2a[:, 0, :], 0, S - LAST)
         scatter(pages_b[2], idx3, h2_23[1][:, :BANK], gain2_3a[:, 0, :], 0, BANK)
         b3b = weigh(nc.gpsimd, 19 * KB, "b3b", h2_23[1][:, BANK:], gain2_3b[:, 0, :])
         a3 = weigh(nc.gpsimd, 220 * KB, "a3", h1[3][:], gain1_3[:, 0, :])
-        place(pages_a[2], idx2, a2b, S - LEAD, S)
+        place(pages_a[2], idx2, a2b, S - LAST, S)
         finish_slice_2(banks2)
         place(pages_b[2], idx3, b3b, BANK, S)
         based = at(72 * KB, [P, T2], F32, "based")

from contextlib import ExitStack

import concourse.mybir as mybir
from concourse.masks import make_identity

K, T, S, H, T2, N = 1024, 4096, 1024, 512, 2048, 384
FLOPS = 2 * (2 * K * H * S + H * N * T2)

F32 = mybir.dt.float32
BF16 = mybir.dt.bfloat16
I32 = mybir.dt.int32
U32 = mybir.dt.uint32
U16 = mybir.dt.uint16
U8 = mybir.dt.uint8
FP8X4 = mybir.dt.float8_e4m3fn_x4
FP4X4 = mybir.dt.float4_e2m1fn_x4
ACT = mybir.ActivationFunctionType
MULT = mybir.AluOpType.mult
ADD = mybir.AluOpType.add

P = 128
PACK = 4
K_PASS = P * PACK
PASSES = K // K_PASS
SLICES = PACK
BANK = 512
HALVES = S // BANK
CHUNKS = T2 // BANK
TILES = BANK // P
GROUPS = N // P
PER_COLUMN = 16
QUADRANT = 32
SCALE_ROWS = 4
KB = 1024
LEAD = 256
LAST = 320
DIRECT = 2
UNITS = ((0, 256), (256, 256), (512, 512), (1024, 512), (1536, 512))


def tile_list_inlet_speed_map_kernel(
    tc, tab_words, tab_scales, w1, w4_words, w4_scales, wo, rough, wg1, wg2, offs, offs2, offs3, out
):
    nc = tc.nc
    with ExitStack() as ctx:
        sbuf = ctx.enter_context(tc.tile_pool(name="sbuf", bufs=1))
        arena = ctx.enter_context(tc.tile_pool(name="arena", bufs=1))
        psum = ctx.enter_context(tc.psum_pool(name="psum", bufs=4))

        def own(shape, dtype, name):
            return sbuf.tile(shape, dtype, name=name, align_bytes=64)

        def at(offset, shape, dtype, name):
            return arena.tile(shape, dtype, name=name, offset=offset, align_bytes=64)

        idx = sbuf.tile([P, S // PER_COLUMN], U16, name="idx")
        idx2 = sbuf.tile([P, S // PER_COLUMN], U16, name="idx2")
        idx3 = sbuf.tile([P, S // PER_COLUMN], U16, name="idx3")
        tab_scale = at(112 * KB, [P, T], U8, "tab_scale")
        w4_scale_raw = own([P, H], U8, "w4_scale_raw")
        scales = own([P, PASSES, S + H], U8, "scales")
        nc.vector.memset(tab_scale[0 : P - QUADRANT, :].bitcast(I32), 0)
        nc.vector.memset(w4_scale_raw[0 : P - QUADRANT, :].bitcast(I32), 0)
        nc.gpsimd.memset(scales[:].rearrange("p a c -> p (a c)").bitcast(I32), 0)

        tab_word = [at(16 * KB * a, [P, T], I32, f"tab_word{a}") for a in range(PASSES)]
        w4_raw = at(184 * KB, [P, PASSES, 2 * H], U8, "w4_raw")
        nc.sync.dma_start(idx[:], offs)
        nc.sync.dma_start(tab_scale[P - QUADRANT : P, :].bitcast(I32), tab_scales.bitcast(I32).rearrange("a r t -> r a t"))
        nc.sync.dma_start(w4_scale_raw[P - QUADRANT : P, :].bitcast(I32), w4_scales.bitcast(I32).rearrange("a r c -> r a c"))
        for a in range(PASSES):
            nc.sync.dma_start(tab_word[a][:], tab_words[a].rearrange("p t i -> p (t i)").bitcast(I32))
        nc.sync.dma_start(w4_raw[:].bitcast(I32), w4_words.bitcast(I32).rearrange("a p c -> p a c"))
        nc.sync.dma_start(idx3[:], offs3)

        def load_quadrants(gain, wg, t, j_first, quadrants):
            rows = wg.rearrange("(p t) j -> p t j", t=SLICES)[:, t : t + 1, j_first : j_first + gain.shape[2]]
            for q in quadrants:
                nc.sync.dma_start(gain[q * QUADRANT : (q + 1) * QUADRANT], rows)

        def load_gain(wg, offset, name, first, end, j_first, j_end, quadrants=(0, 2, 1, 3)):
            gain = at(offset, [P, end - first, j_end - j_first], F32, name)
            load_quadrants(gain, wg, first, j_first, quadrants)
            return gain

        w1_raw = [at((48 + 8 * a) * KB, [P, PACK, H], F32, f"w1_raw{a}") for a in range(PASSES)]
        rough_rows = rough.rearrange("(p t) m -> t p m", t=SLICES)
        roughs = [at((80 + 8 * t) * KB, [P, T2], F32, f"rough{t}") for t in range(SLICES)]

        def load_w1(a):
            nc.sync.dma_start(w1_raw[a][:], w1[a * K_PASS : (a + 1) * K_PASS, :].rearrange("(p i) c -> p i c", i=PACK))

        gain2_0a = load_gain(wg2, 32 * KB, "gain2_0a", 0, 1, 0, LEAD)
        gain2_1a = load_gain(wg2, 33 * KB, "gain2_1a", 1, 2, 0, BANK)
        gain2_0b = load_gain(wg2, 35 * KB, "gain2_0b", 0, 1, LEAD, S)
        load_w1(0)
        gain2_1b = load_gain(wg2, 38 * KB, "gain2_1b", 1, 2, BANK, S)
        gain2_2a = load_gain(wg2, 40 * KB, "gain2_2a", 2, 3, 0, BANK)
        load_w1(1)
        nc.sync.dma_start(idx2[:], offs2)
        nc.sync.dma_start(roughs[0][:], rough_rows[0])
        gain2_2b = load_gain(wg2, 42 * KB, "gain2_2b", 2, 3, BANK, S)
        gain1_0 = load_gain(wg1, 0, "gain1_0", 0, 1, 0, S)
        nc.sync.dma_start(roughs[1][:], rough_rows[1])
        gain1_1 = load_gain(wg1, 4 * KB, "gain1_1", 1, 2, 0, S)
        wo_raw = at(48 * KB, [P, PACK, N], F32, "wo_raw")
        nc.sync.dma_start(wo_raw[:], wo.rearrange("(p i) n -> p i n", i=PACK))
        nc.sync.dma_start(roughs[2][:], rough_rows[2])
        gain1_2b = load_gain(wg1, 16 * KB, "gain1_2b", 2, 3, S - LAST, S)
        gain2_3a = load_gain(wg2, 20 * KB, "gain2_3a", 3, 4, 0, BANK, (0, 2, 1))
        gain1_2a = load_gain(wg1, 16 * KB + 4 * LAST, "gain1_2a", 2, 3, 0, S - LAST)
        load_quadrants(gain2_3a, wg2, 3, 0, (3,))
        gain2_3b = load_gain(wg2, 22 * KB, "gain2_3b", 3, 4, BANK, S)
        nc.sync.dma_start(roughs[3][:], rough_rows[3])
        gain1_3 = load_gain(wg1, 32 * KB, "gain1_3", 3, 4, 0, S)

        ident = sbuf.tile([P, P], F32, name="ident")
        make_identity(nc, ident[:])

        picked_scale = own([P, S], U8, "picked_scale")
        nc.vector.tensor_copy(picked_scale[:], tab_scale[:].indirect(idx[:]))
        joined = own([P, S + H], U8, "joined")
        nc.vector.tensor_copy(
            joined[:, S:].rearrange("p (t m) -> p t m", t=SLICES), w4_scale_raw[:].rearrange("p (m t) -> p t m", t=SLICES)
        )
        nc.vector.tensor_copy(joined[:, :S].bitcast(I32), picked_scale[:].bitcast(I32))
        rows_a_quadrant = PASSES * SCALE_ROWS
        for q in range(P // QUADRANT):
            nc.scalar.dma_start(
                scales[q * QUADRANT : q * QUADRANT + SCALE_ROWS, :, :].bitcast(I32),
                joined[P - QUADRANT + q * rows_a_quadrant : P - QUADRANT + (q + 1) * rows_a_quadrant, :].bitcast(I32),
            )
        w4_word = [at((144 + 8 * b) * KB, [P, 2, PASSES, 2 * P], U8, f"w4_word{b}") for b in range(2)]
        w4_by_slice = w4_raw[:].bitcast(U16).rearrange("p a (m t) -> p t a m", t=SLICES)
        for t in range(2):
            nc.scalar.copy(w4_word[0][:, t].bitcast(U16), w4_by_slice[:, t])
        nc.scalar.copy(w4_word[1][:].bitcast(U16), w4_by_slice[:, 2:4])
        pages_b = []
        for b in range(2):
            page = at((112 + 8 * b) * KB, [P, T2], F32, f"page_b{b}")
            (nc.vector, nc.gpsimd)[b].memset(page[:], 0.0)
            pages_b.append(page)

        v_word = [at((128 + 4 * a) * KB, [P, S], U32, f"v_word{a}") for a in range(PASSES)]
        nc.vector.tensor_copy(v_word[0][:], tab_word[0][:].bitcast(U32).indirect(idx[:]))
        pages_a = [at(8 * KB, [P, T2], F32, "page_a0")]
        nc.vector.memset(pages_a[0][:], 0.0)
        for first, end in ((0, LEAD), (LEAD, BANK), (BANK, S)):
            entries = idx[:, first // PER_COLUMN : end // PER_COLUMN]
            nc.vector.tensor_copy(v_word[1][:, first:end], tab_word[1][:].bitcast(U32).indirect(entries))

        pages_a.append(at(184 * KB, [P, T2], F32, "page_a1"))
        nc.gpsimd.memset(pages_a[1][:], 0.0)
        pages_b.append(at(24 * KB, [P, T2], F32, "page_b2"))
        nc.gpsimd.memset(pages_b[2][:], 0.0)

        w1_scale = own([P, SLICES, PASSES, P], U8, "w1_scale")

        def multiply(weight, t, h):
            cols = slice(h * BANK, (h + 1) * BANK)
            acc = psum.tile([P, BANK], F32, name="acc", tag="acc")
            passes = (1, 0)
            for a in passes:
                if weight == "w1":
                    codes, scale = w1_word[:, t, a, :].bitcast(FP8X4), w1_scale[:, t, a, :]
                else:
                    codes, scale = w4_word[t // 2][:, t % 2, a, :].bitcast(FP4X4), scales[:, a, S + t * P : S + (t + 1) * P]
                nc.tensor.matmul_mx(
                    out=acc[:],
                    lhsT=codes,
                    lhsT_scale=scale,
                    rhs=v_word[a][:, cols].bitcast(FP8X4),
                    rhs_scale=scales[:, a, cols],
                    start=(a == passes[0]),
                    stop=(a == passes[-1]),
                )
            return acc

        def square(values, weight, t, h):
            nc.scalar.activation(values[:, h * BANK : (h + 1) * BANK], multiply(weight, t, h)[:], ACT.Square)

        def square_narrow(values, first, passes):
            acc = psum.tile([P, LEAD], F32, name="acc", tag="acc")
            for a in passes:
                for j in range(0, LEAD, P):
                    cols = slice(first + j, first + j + P)
                    nc.tensor.matmul_mx(
                        out=acc[:, j : j + P],
                        lhsT=w4_word[0][:, 0, a, :].bitcast(FP4X4),
                        lhsT_scale=scales[:, a, S : S + P],
                        rhs=v_word[a][:, cols].bitcast(FP8X4),
                        rhs_scale=scales[:, a, cols],
                        start=(a == passes[0] and j == 0),
                        stop=(a == passes[-1] and j == LEAD - P),
                    )
            nc.scalar.activation(values[:, first : first + LEAD], acc[:], ACT.Square)

        def scatter(page, offsets, values, gain, first, end):
            entries = offsets[:, first // PER_COLUMN : end // PER_COLUMN]
            nc.vector.tensor_tensor(page[:].indirect(entries), values, gain, MULT)

        def weigh(engine, offset, name, values, gain, piece=S):
            width = values.shape[1]
            weighted = at(offset, [P, width], F32, name)
            for first in range(0, width, piece):
                cols = slice(first, min(first + piece, width))
                engine.tensor_tensor(weighted[:, cols], values[:, cols], gain[:, cols], MULT)
            return weighted

        def place(page, offsets, weighted, first, end):
            nc.vector.tensor_copy(page[:].indirect(offsets[:, first // PER_COLUMN : end // PER_COLUMN]), weighted[:])

        def add_transposed(bank, c, rows, opens, closes):
            for j in range(TILES):
                nc.tensor.matmul(
                    bank[:, j * P : (j + 1) * P],
                    rows[:, c * BANK + j * P : c * BANK + (j + 1) * P],
                    ident[:],
                    is_transpose=True,
                    start=(opens and j == 0),
                    stop=(closes and j == TILES - 1),
                )

        def new_banks(tag):
            return [psum.tile([P, BANK], F32, name=tag, tag=tag) for c in range(CHUNKS)]

        def add_all(banks, rows, opens, closes):
            for c in range(CHUNKS):
                add_transposed(banks[c], c, rows, opens, closes)

        def open_sum(t, tag, page_b):
            banks = new_banks(tag)
            add_all(banks, page_b, True, False)
            add_all(banks, roughs[t], False, False)
            return banks

        words = {u: at(80 * KB + 8 * UNITS[u][0], [P, 2, UNITS[u][1]], F32, f"words{u}") for u in range(DIRECT, len(UNITS))}
        woven = [at(156 * KB + 8 * first, [P, width, 2], F32, f"woven{first}") for first, width in UNITS]

        def units_of(c):
            return [(u, first - c * BANK, width) for u, (first, width) in enumerate(UNITS) if first // BANK == c]

        def roots_of(u, half, e):
            if u < DIRECT:
                return woven[u][:].rearrange("p m x -> p (m x)").bitcast(BF16).rearrange("p (m i) -> p m i", i=PACK)[:, :, 2 * half + e]
            return words[u][:, half, :].bitcast(BF16).rearrange("p (m e) -> p m e", e=2)[:, :, e]

        pair_t = [at((48 + 2 * c) * KB, [P, BANK], F32, f"pair_t{c}") for c in range(CHUNKS)]

        def close_pair_slice(t, banks):
            for c in range(CHUNKS):
                add_transposed(banks[c], c, pages_a[t], False, True)
                nc.scalar.activation(
                    pair_t[c][:].bitcast(BF16).rearrange("m (x e) -> m x e", e=2)[:, :, t], banks[c][:], ACT.Sqrt
                )

        def turn_pair_back():
            for c in range(CHUNKS):
                back = psum.tile([P, BANK], F32, name="acc", tag="acc")
                for j in range(TILES):
                    nc.tensor.transpose(back[:, j * P : (j + 1) * P], pair_t[c][:, j * P : (j + 1) * P], ident[:])
                for u, first, width in units_of(c):
                    nc.scalar.copy(woven[u][:, :, 0] if u < DIRECT else words[u][:, 0, :], back[:, first : first + width])

        def finish_slice_2(banks):
            for c in range(CHUNKS):
                add_transposed(banks[c], c, pages_a[2], False, True)
                tiles_t = at((44 + c) * KB, [P, BANK // 2], F32, f"tiles_t{c}")
                nc.scalar.activation(
                    tiles_t[:].bitcast(BF16).rearrange("m (x p e) -> m x p e", x=2, e=2),
                    banks[c][:].rearrange("m (x e p) -> m x p e", x=2, e=2),
                    ACT.Sqrt,
                )
                back = psum.tile([P, BANK // 2], F32, name="acc", tag="acc")
                for x in range(2):
                    nc.tensor.transpose(back[:, x * P : (x + 1) * P], tiles_t[:, x * P : (x + 1) * P], ident[:])
                cells = back[:].bitcast(BF16).rearrange("p (x m e) -> p x e m", x=2, e=2)
                for u, first, width in units_of(c):
                    if width == P:
                        nc.scalar.copy(roots_of(u, 1, 0), cells[:, first // (2 * P), first // P % 2, :])
                    else:
                        xs = slice(first // (2 * P), (first + width) // (2 * P))
                        nc.scalar.copy(roots_of(u, 1, 0).rearrange("p (x e m) -> p x e m", e=2, m=P), cells[:, xs])

        h2_01 = [at((136 + 4 * t) * KB, [P, S], F32, f"h2_{t}") for t in range(2)]
        square_narrow(h2_01[0], 0, (0, 1))
        square(h2_01[1], "w4", 1, 0)
        square_narrow(h2_01[0], LEAD, (1, 0))
        for t in range(2):
            square(h2_01[t], "w4", t, 1)
        h2_23 = [at((216, 220)[b] * KB, [P, S], F32, f"h2_{2 + b}") for b in range(2)]
        for h in range(HALVES):
            for b in range(2):
                square(h2_23[b], "w4", 2 + b, h)
        page_b_late = at(144 * KB, [P, T2], F32, "page_b_late")
        nc.gpsimd.memset(page_b_late[:], 0.0)
        scatter(pages_b[0], idx3, h2_01[0][:, :LEAD], gain2_0a[:, 0, :], 0, LEAD)
        scatter(pages_b[1], idx3, h2_01[1][:, :BANK], gain2_1a[:, 0, :], 0, BANK)
        scatter(pages_b[0], idx3, h2_01[0][:, LEAD:], gain2_0b[:, 0, :], LEAD, S)
        scatter(pages_b[1], idx3, h2_01[1][:, BANK:], gain2_1b[:, 0, :], BANK, S)
        pages_a.append(at(136 * KB, [P, T2], F32, "page_a2"))
        nc.gpsimd.memset(pages_a[2][:], 0.0)
        banks0 = new_banks("total")
        add_all(banks0, pages_b[0], True, False)
        w1_bf16 = at(208 * KB, [P, SLICES, PASSES, P, PACK], BF16, "w1_bf16")
        for a in range(PASSES):
            nc.scalar.copy(
                w1_bf16[:, :, a, :, :].rearrange("p t m i -> p m t i"),
                w1_raw[a][:].rearrange("p i (m t) -> p m t i", t=SLICES),
            )
        scatter(page_b_late, idx3, h2_23[0][:, :BANK], gain2_2a[:, 0, :], 0, BANK)
        w1_word = at(192 * KB, [P, SLICES, PASSES, P], U32, "w1_word")
        for first, end in ((0, 2), (2, SLICES)):
            nc.vector.quantize_mx(
                out=w1_word[:, first:end].rearrange("p t a c -> p (t a c)").bitcast(FP8X4),
                scales=w1_scale[:, first:end].rearrange("p t a c -> p (t a c)"),
                in_=w1_bf16[:, first:end].rearrange("p t a c i -> p (t a c i)"),
            )
        scatter(page_b_late, idx3, h2_23[0][:, BANK:], gain2_2b[:, 0, :], BANK, S)

        h1 = [at((64 + 4 * t) * KB, [P, S], F32, f"h1_{t}") for t in range(SLICES)]
        for t in range(SLICES):
            for h in range(HALVES):
                square(h1[t], "w1", t, h)
        add_all(banks0, roughs[0], False, False)
        wo_bf16 = at(132 * KB, [P, N, PACK], BF16, "wo_bf16")
        nc.scalar.copy(wo_bf16[:], wo_raw[:].rearrange("p i n -> p n i"))
        banks1 = open_sum(1, "acc", pages_b[1])
        scatter(pages_a[0], idx2, h1[0][:], gain1_0[:, 0, :], 0, S)
        close_pair_slice(0, banks0)
        banks2 = open_sum(2, "total", page_b_late)
        a2b = weigh(nc.vector, 196 * KB, "a2b", h1[2][:, S - LAST :], gain1_2b[:, 0, :])
        scatter(pages_a[1], idx2, h1[1][:], gain1_1[:, 0, :], 0, S)
        close_pair_slice(1, banks1)
        turn_pair_back()
        scatter(pages_a[2], idx2, h1[2][:, : S - LAST], gain1_2a[:, 0, :], 0, S - LAST)
        scatter(pages_b[2], idx3, h2_23[1][:, :BANK], gain2_3a[:, 0, :], 0, BANK)
        b3b = weigh(nc.gpsimd, 19 * KB, "b3b", h2_23[1][:, BANK:], gain2_3b[:, 0, :])
        a3 = weigh(nc.gpsimd, 220 * KB, "a3", h1[3][:], gain1_3[:, 0, :])
        place(pages_a[2], idx2, a2b, S - LAST, S)
        finish_slice_2(banks2)
        place(pages_b[2], idx3, b3b, BANK, S)
        based = at(72 * KB, [P, T2], F32, "based")
        nc.gpsimd.tensor_tensor(based[:], pages_b[2][:], roughs[3][:], ADD)
        place(pages_a[1], idx2, a3, 0, S)
        early = at(44 * KB, [P, 2 * BANK], F32, "early")
        late = [at(offset, [P, BANK], F32, f"late{offset}") for offset in (132 * KB, 156 * KB)]

        def total_of(u):
            first, width = UNITS[u]
            return early[:, first : first + width] if first < 2 * BANK else late[first // BANK - 2][:]

        wo_scale = own([P, N], U8, "wo_scale")
        wo_word = at(24 * KB, [P, N], U32, "wo_word")

        def quantise_wo():
            for first, end in ((0, P), (P, N)):
                nc.vector.quantize_mx(
                    out=wo_word[:, first:end].bitcast(FP8X4),
                    scales=wo_scale[:, first:end],
                    in_=wo_bf16[:].rearrange("p n i -> p (n i)")[:, PACK * first : PACK * end],
                )

        def add(u):
            first, width = UNITS[u]
            cells = slice(first, first + width)
            nc.vector.tensor_tensor(total_of(u), based[:, cells], pages_a[1][:, cells], ADD)

        def root(u):
            nc.scalar.activation(roots_of(u, 1, 1), total_of(u), ACT.Sqrt)

        quantised = {}

        def weave(u):
            if u < DIRECT:
                return
            nc.vector.tensor_copy(
                woven[u][:].rearrange("p (c i) x -> p c x i", i=4), words[u][:].rearrange("p x (c i) -> p c x i", i=4)
            )

        def quantise(u):
            first, width = UNITS[u]
            z_word = at(172 * KB + 4 * first, [P, width], U32, f"z_word{u}")
            z_scale = own([P, width], U8, f"z_scale{u}")
            nc.vector.quantize_mx(
                out=z_word[:].bitcast(FP8X4),
                scales=z_scale[:],
                in_=woven[u][:].rearrange("p m x -> p (m x)").bitcast(BF16),
            )
            quantised[u] = (z_word, z_scale)

        def multiply_unit(u):
            first, width = UNITS[u]
            z_word, z_scale = quantised[u]
            for g in range(GROUPS):
                rows = slice(g * P, (g + 1) * P)
                tag = ("acc", "total")[u % 2]
                result = psum.tile([P, width], F32, name=tag, tag=tag)
                nc.tensor.matmul_mx(
                    out=result[:],
                    lhsT=wo_word[:, rows].bitcast(FP8X4),
                    lhsT_scale=wo_scale[:, rows],
                    rhs=z_word[:].bitcast(FP8X4),
                    rhs_scale=z_scale[:],
                    start=True,
                    stop=True,
                )
                spot = (96 * KB, 104 * KB, 32 * KB)[g] + 4 * first
                staged = at(spot, [P, width], F32, f"staged{u}_{g}")
                if g == (1 if u == len(UNITS) - 1 else 2):
                    nc.vector.tensor_copy(staged[:], result[:])
                else:
                    nc.scalar.copy(staged[:], result[:])
                nc.sync.dma_start(out[rows, first : first + width], staged[:])

        steps = ((quantise, 3), (add, 0), (weave, 2), (multiply_unit, 4), (root, 1))
        for k in range(len(UNITS) + 4):
            if k == 3:
                quantise_wo()
            for step, lag in steps:
                if 0 <= k - lag < len(UNITS):
                    step(k - lag)
